import numpy as np, ml_dtypes
CORES = [16,18,20,22]
N = 4
BF = ml_dtypes.bfloat16
V, M, CAP, RO = 1024, 2, 64, 4
def phone(rng):
    loc = rng.choice(np.array([0.0, 0.2, 0.5, 0.8]), (N, 8, 1, 1))
    far = rng.integers(0, N * V, (N, 8, 16, V)); near = rng.integers(0, V, (N, 8, 16, V)) + V * np.arange(N)[:, None, None, None]
    return np.where(rng.random((N, 8, 16, V)) < loc, near, far)
def lore(rng):
    share = rng.choice(np.array([0.0, 0.0, 0.0625, 0.125, 0.3]), (N, 8, 1, V))
    return np.where(rng.random((N, 8, 16, V)) < share, rng.integers(1, 256, (N, 8, 16, V)), 0)
def dense(rng, sec, tel, g, d, lean):
    x = np.arange(N * V).reshape(N, 1, V); goal = x[:, 0] ^ 1; h = V // 2; i = 0
    run = 2 * ((64 * int(rng.integers(0, V // 128)) + rng.permutation((N - 1) * CAP)) % h)
    for r in range(N):
        if r == d: continue
        goal[r, 2 * rng.permutation(h)[:CAP]] = d * V + run[i:i + CAP]; i += CAP
    s = rng.integers(0, 256, (N, 16, V)); a, b = (int(k) for k in rng.permutation(16)[:2])
    s[:, a, 0::2] = rng.integers(0, 51, (N, h)); s[d, a, 0::2] = rng.integers(51, 101, h); s[:, a, 1::2] = rng.integers(101, 256, (N, h))
    s[:, b, 0::2] = rng.integers(128, 256, (N, h)); s[:, b, 1::2] = rng.integers(0, 128, (N, h))
    sec[:, g] = s
    if lean:
        row = rng.integers(0, 16, (N, 1, V)); t = np.where(np.arange(16)[None, :, None] == row, goal[:, None, :], x)
        if M == 2: t[:, :, 1::2] = tel[:, g, :, 1::2]
        tel[:, g] = t
    else: tel[:, g] = goal[:, None, :]
def pack(sec, tel):
    return {"sec": np.ascontiguousarray(sec.reshape(N, 128, V)).astype(np.float32).astype(BF), "tel": np.ascontiguousarray(tel.reshape(N, 128, V)).astype(np.int32)}
def setup_inputs(rng):
    tel, sec = phone(rng), lore(rng); me = np.arange(N * V).reshape(N, 1, 1, V)
    tel = np.where(rng.random((N, 8, 1, V)) < 0.03, me, tel); sec = np.where(rng.random((N, 8, 1, V)) < 0.004, 255, sec)
    return pack(sec, tel)
def setup_inputs_room(rng):
    b = rng.integers(0, 100, (8, 16)); sec = np.broadcast_to(b[None, :, :, None], (N, 8, 16, V)).copy()
    o = np.argsort(rng.random((N, 8, V)), axis=-1); kn, non = o[:, :, :16], o[:, :, 16:]
    s = rng.integers(0, N, (N, 8, 16, V)); tel = s * V + non[s, np.arange(8)[None, :, None, None], rng.integers(0, V - 16, (N, 8, 16, V))]
    for q in range(N):
        for g in range(8):
            sec[q, g][:, kn[q, g]] = b[g][:, None] + rng.integers(1, 100, (16, 16))
            cal = non[q, g][non[q, g] % M == 0]; pos = 0
            for d in range(1, N + 1):
                z = (q + d) % N; n = int(rng.choice(np.array([0, 1, CAP - 1, CAP, CAP + 1, CAP + 8])))
                if q == 0 and d == 1: n = (CAP, CAP + 1, CAP - 1, CAP + 8, 1, 0, CAP, CAP + 1)[g]
                if d == N: n = 20
                tel[q, g, rng.integers(0, 16, n), cal[pos:pos + n]] = z * V + kn[z, g, rng.integers(0, 16, n)]
                pos += n
    return pack(sec, tel)
def setup_inputs_ties(rng):
    tel = phone(rng); tel[:, :, 8:] = tel[:, :, 7::-1]
    sec = (rng.random((N, 8, 16, V)) < rng.choice(np.array([0.05, 0.2, 0.5]), (N, 8, 1, V))).astype(np.int64)
    sec[:, ::2] *= 255
    m = rng.random((N, 4, 16, V)) < 0.1
    tel[:, 1::2] = np.where(m, rng.choice(np.array([0, V - 1, V, N * V - 1]), m.shape), tel[:, 1::2])
    return pack(sec, tel)
def setup_inputs_crowd(rng):
    tel, sec = phone(rng), lore(rng); x = np.arange(N * V).reshape(N, 1, V); o = rng.permutation(8)
    for g in o[:3]: sec[:, g] = rng.integers(0, 256, (N, 16, V))
    tel[:, o[0]] = (x + M) % (N * V); tel[:, o[1]] = x ^ M; tel[:, o[2]] = (x + V) % (N * V)
    sec[:, o[3:5]] = np.minimum(sec[:, o[3:5]], 200)
    star = int(rng.choice(np.array([0, V - 1, N * V - V, N * V - 1]))); tel[:, o[3], int(rng.integers(0, 16))] = star; sec[star // V, o[3], :, star % V] = 255
    place = rng.choice(np.array([0, V - 1]), N)
    tel[:, o[4], int(rng.integers(0, 16))] = (np.arange(N) * V + place)[rng.integers(0, N, (N, V))]
    for q in range(N): sec[q, o[4], :, place[q]] = 255
    dense(rng, sec, tel, int(o[5]), N - 1, False)
    dense(rng, sec, tel, int(o[6]), int(rng.integers(0, N - 1)), True)
    return pack(sec, tel)
def setup_inputs_alike(rng):
    tel, sec = phone(rng), lore(rng); x = np.arange(N * V).reshape(N, 1, V); o = rng.permutation(8)
    sec[:, o[0]] = rng.integers(0, 256, (1, 16, 1))
    sec[:, o[1]] = 0; sec[int(rng.integers(0, N)), o[1]] = 255
    one = int(rng.choice(np.array([0, N * V - 1]))); sec[:, o[2]] = 0; sec[one // V, o[2], int(rng.integers(0, 16)), one % V] = int(rng.integers(1, 256)); tel[:, o[2], 15] = one
    tel[:, o[3], 1:] = x
    sec[:, o[4]] = rng.integers(254, 256, (N, 16, V))
    sec[:, o[5]] = np.where(rng.random((N, 1, V)) < 0.5, 0, rng.integers(230, 256, (N, 16, V)))
    z = rng.integers(-40, 41, (N, 8, V)); s = 128 + np.concatenate([z, -z], axis=1); s[:, int(rng.integers(0, 16))] += rng.integers(-1, 2, (N, V))
    sec[:, o[6]] = np.where(rng.random((N, 1, V)) < 0.5, 0, s)
    return pack(sec, tel)
def setup_inputs_spread(rng):
    sec = np.floor(np.exp2(8 * rng.random((N, 8, 1, V))) * np.exp2(-4 * rng.random((1, 8, 16, 1))) * rng.random((N, 8, 16, V))).astype(np.int64)
    sec = np.where(rng.random((N, 8, 16, V)) < rng.random((N, 8, 1, V)), np.minimum(sec, 255), 0)
    o = np.argsort(rng.random((8, N * V)), axis=-1); k = np.minimum((N * V * rng.random((N, 8, 16, V)) ** 3).astype(np.int64), N * V - 1)
    return pack(sec, o[np.arange(8)[None, :, None, None], k])
def check_inputs(d):
    bad = []; s = np.asarray(d["sec"]).astype(np.float32); a = np.asarray(d["tel"])
    if not np.all((s >= 0) & (s <= 255) & (s == np.floor(s))): bad.append("sec: whole numbers from 0 to 255")
    if np.min(a) < 0 or np.max(a) > N * V - 1: bad.append("range of tel")
    return bad
def world(a):
    return np.ascontiguousarray(a.astype(np.int64).reshape(N, 8, 16, V).transpose(1, 2, 0, 3)).reshape(8, 16, N * V)
def ranks(a):
    return np.ascontiguousarray(a.reshape(8, 16, N, V).transpose(2, 0, 1, 3)).reshape(N, 128, V).astype(np.float32)
def reference(sec, tel):
    S, T = world(sec.astype(np.float32)), world(tel)
    for t in range(RO):
        x = (np.arange(N)[:, None] * V + np.arange(t % M, V, M)[None, :]).reshape(-1)
        Sn, Tn = S.copy(), T.copy()
        for g in range(8):
            tl = T[g][:, x]; gain = np.zeros(tl.shape, np.int64)
            for f in range(16): gain += np.maximum(S[g, f][tl] - S[g, f][x][None, :], 0)
            row = np.argmax(gain, axis=0)
            c = np.take_along_axis(tl, row[None, :], 0)[0]; call = np.max(gain, axis=0) > 0
            through = call.reshape(N, -1)
            for s in range(N):
                flag = (call & (c // V == s)).reshape(N, -1); count = np.add.accumulate(flag.astype(np.int64), axis=1)
                through = through & (~flag | (count <= CAP) | (np.arange(N)[:, None] == s))
            w = np.flatnonzero(through.reshape(-1)); u, first = np.unique(c[w], return_index=True); w = w[first]; v = x[w]
            Sn[g][:, v] = np.maximum(S[g][:, v], S[g][:, u])
            Sn[g][:, u] = np.maximum(Sn[g][:, u], S[g][:, v])
            Tn[g][:, v] = np.where(gain[:, w] == 0, T[g][:, u], T[g][:, v])
            Tn[g, t, u] = v
        S, T = Sn, Tn
        if t < RO - 1: T = np.roll(Tn, 1, axis=0)
    return {"ysec": ranks(S).astype(BF), "ytel": ranks(T)}

@@ -1,0 +1,662 @@
+import math
+from concourse.bass import DstId, RemoteDMATransfer
+from concourse.mybir import AluOpType, ActivationFunctionType
+
+ALU = AluOpType
+ACT = ActivationFunctionType
+NV = 10
+NB = 11
+RO = 4
+LG = math.log(1.40)
+LW0 = 124 * math.log(2.0)
+
+F, B, I, U = "float32", "bfloat16", "int32", "uint16"
+SCRATCH = {}
+
+
+def _decl(where, dtype, **kw):
+    for k in kw:
+        SCRATCH[k] = (where, kw[k] if isinstance(kw[k], list) else [128, kw[k]], dtype)
+
+
+_decl("psum", F, K0=512, K1=512, D0=512, D1=512, ZN=512, PA=512, PB=512, TS=512)
+_decl("dram", I, dT=[8, 128, 128], lT=[8, 128, 128])
+_decl("dram", B, dS=[8, 128, 128], lS=[8, 128, 128], oS=[8, 128, 128], loS=[8, 128, 128])
+_decl("dram", F, oT=[8, 128, 128], loT=[8, 128, 128])
+_decl("sbuf", I, CI=16, TRAW=1024, II=64, DG=256, NC=64, ID=64)
+_decl("sbuf", U, OFF0=512, OFF1=512, OFF2=512, OFF3=512, OFS=512, CL=128, FU=64, SBU=32, CU=64)
+_decl("sbuf", B, SRAW=1024, SW0=4112, SW1=4112, SA=512, SB0=512, SB1=512, SD0=1024, M=8192, G0=512, G1=512, HI=512, IOT=192,
+      IDB=128, NEG=128, HIR=256, SEL=512, SUMR=16, OWNR=256, CR=512, ONE1=128, RM16=512, RM4=512, ONES=256, LS=128, LI=128,
+      L0=128, FB=320, EM=512, RHS=416, BZ=144, AA=4096, BB=2048, BX=256, EE=512, ZP=512, EQ=512, OS=1024, TMPB=256)
+_decl("sbuf", F, CF=32, TD0=1024, TD1=1024, TD2=1024, TD3=1024, TW0=4096, TW1=4096, LT=3072, LR=192, LN=96, IOF=160, IDF=128,
+      SELF=512, IZ0=160, IZ1=160, IF0=160, IF1=160, WT=64, THR=128, STAB=128, SELFC=128, IDN=1024, KS=1024, CS=64, AB=192, OK=128,
+      TH=160, HS=1024, ZQ=256, H2=256, Q2=256, XY=128, LL=128, QS=128, T1=192, FF=64, WW=256, DC=64, C1=128, TSS=512, TG=512,
+      TX=512, OLDX=64, X1=96, FY=128, HY=64, RY=64, Y1=128, RN=64, TD_=512, TB=512, OT=1024, LRI=256, TMPF=256)
+
+_DMA_GROUPS = ["ldT", "ldS", "own", "rawT", "rawS", "oS", "oT", "out", "ryl"] + ["%s%d" % (n, t) for t in range(3) for n in
+              ("rya", "ryb", "cpa", "cpb", "fxa", "fxb", "cpn")] + ["tw%s%d" % (h, t) for t in range(4) for h in "ab"]
+_ARRIVE = ["aT", "aS", "aoS", "aoT", "aRI"] + ["%s%d" % (n, t) for t in range(3) for n in ("aa", "ab", "ara", "arb", "ao", "an")]
+SEMAPHORES = ["ev", "es", "ep", "eg"] + _DMA_GROUPS + _ARRIVE + ["s" + n for n in _ARRIVE]
+ENGSEM = {"v": "ev", "s": "es", "p": "ep", "g": "eg"}
+
+
+def R(name, c0=None, c1=None, st=1, p0=0, p1=128, ps=1):
+    if c0 is None:
+        c0, c1 = 0, SCRATCH[name][1][1]
+    return (name, p0, p1, ps, c0, c1, st)
+
+
+def DR(name, k0=0, k1=8, r0=0, r1=128):
+    return (name, k0, k1, 1, r0, r1, 1)
+
+
+def _touch(a, b):
+    if SCRATCH[a[0]][0] == "psum":
+        return True
+    return a[1] < b[2] and b[1] < a[2] and a[4] < b[5] and b[4] < a[5]
+
+
+def rank_program(g, core, T, topo):
+    rank = T.rank_of(core)
+    if rank is None:
+        return
+    cores = T.cores
+    n = len(cores)
+    ops = []
+    Q = {"v": g.vector, "s": g.scalar, "p": g.tensor, "g": g, "y": g.sync}
+
+    def ap(x):
+        if not isinstance(x, tuple):
+            return x
+        if x[0] == "ind":
+            return ap(x[1]).indirect(ap(x[2]))
+        if x[0] == "raw":
+            return x[1]
+        nm, p0, p1, ps, c0, c1, st = x
+        if SCRATCH[nm][0] == "dram":
+            return T[nm][p0, c0:c1, :] if p1 == p0 + 1 else T[nm][p0:p1, c0:c1, :]
+        a = slice(p0, p1) if ps == 1 else slice(p0, p1, ps)
+        b = slice(c0, c1) if st == 1 else slice(c0, c1, st)
+        return T[nm][a, b]
+
+    def regs(xs):
+        out = []
+        for x in xs:
+            if isinstance(x, tuple):
+                if x[0] == "ind":
+                    out += [x[1], x[2]]
+                elif x[0] != "raw":
+                    out.append(x)
+        return out
+
+    def add(eng, fn, w, r, group=None, count=0):
+        ops.append({"e": eng, "f": fn, "w": regs(w), "r": regs(r), "grp": group, "n": count})
+
+    def ind(win, off):
+        return ("ind", win, off)
+
+    def tt(o, a, b, op):
+        add("v", lambda: g.vector.tensor_tensor(ap(o), ap(a), ap(b), op), [o], [a, b])
+
+    def ts(o, a, s1, op0, s2=None, op1=None):
+        if op1 is None:
+            add("v", lambda: g.vector.tensor_scalar(ap(o), ap(a), ap(s1), None, op0), [o], [a, s1])
+        else:
+            add("v", lambda: g.vector.tensor_scalar(ap(o), ap(a), ap(s1), ap(s2), op0, op1), [o], [a, s1, s2])
+
+    def cp(o, a):
+        add("v", lambda: g.vector.tensor_copy(ap(o), ap(a)), [o], [a])
+
+    def ms(o, val):
+        add("v", lambda: g.vector.memset(ap(o), val), [o], [])
+
+    def scan(o, d0, d1, op0, op1):
+        add("v", lambda: g.vector.tensor_tensor_scan(ap(o), ap(d0), ap(d1), 0.0, op0, op1), [o], [d0, d1])
+
+    def tr(o, a):
+        add("v", lambda: g.vector.transpose(ap(o), ap(a)), [o], [a])
+
+    def act(o, a, fn, bias=None, scale=None):
+        def call():
+            kw = {}
+            if bias is not None:
+                kw["bias"] = ap(bias)
+            if scale is not None:
+                kw["scale"] = ap(scale)
+            return g.scalar.activation(ap(o), ap(a), fn, **kw)
+        add("s", call, [o], [a, bias, scale])
+
+    def mm(o, l, r, start, stop):
+        add("p", lambda: g.tensor.matmul(ap(o), ap(l), ap(r), start, stop), [o], [l, r])
+
+    def iota(o, pat, base=0, cm=0):
+        if SCRATCH[o[0]][2] == I:
+            add("g", lambda: g.iota(ap(o), pat, base, cm), [o], [])
+        else:
+            add("g", lambda: g.iota(ap(o), pat, base, cm, allow_small_or_imprecise_dtypes=True), [o], [])
+
+    def dma(o, a, group, q="y"):
+        add(q, lambda: Q[q].dma_start(ap(o), ap(a)), [o], [a], group, 16)
+
+    def send(name, items, width):
+        def fn():
+            trs = []
+            for k, (d, src, dst) in enumerate(items):
+                eng = topo.engines(core, cores[d])[k * width:(k + 1) * width]
+                rid, pid, _ = topo.addr(cores[d])
+                trs.append(RemoteDMATransfer(dst_ids=[DstId(rid=rid, pnc=pid)], dma_engine_mask=sum(1 << e for e in eng),
+                                             remote_sem=T.sem[name], src=ap(src), dst=ap(dst)))
+            g.remote_dma_fused(trs, local_sem=T.sem["s" + name])
+            return None
+        add("g", fn, [], [x[1] for x in items], "s" + name, width * len(items))
+
+    def arrive(name, lands, count):
+        add("x", None, lands, [], name, count)
+
+    nxt = (rank + 1) % n
+    flip = rank == 0
+    wide = len(topo.engines(core, cores[nxt]))
+    w6 = wide // 8
+    others = [(rank + d) % n for d in range(1, n)]
+    pieces = [(d, w) for d in others for w in range(2)]
+
+    def exchange(name, src, land):
+        send(name, [(d, DR(src, d + n * w, d + n * w + 1), DR(land, rank + n * w, rank + n * w + 1)) for d, w in pieces], w6)
+        arrive(name, [DR(land, d + n * w, d + n * w + 1) for d, w in pieces], 6 * w6)
+
+    def hand(o, a, group):
+        for w in range(2):
+            dma(R(o[0], o[4], o[5], 1, 64 * w, 64 * w + 64), R(a[0], a[4], a[5], 1, 64 - 64 * w, 128 - 64 * w), group)
+
+    def pass_on(name, src, land, final, group):
+        send(name, [(nxt, src, land if nxt == 0 else final)], wide)
+        arrive(name, [land if flip else final], wide)
+        if flip:
+            hand(final, land, group)
+
+    def col(k):
+        return R("CF", k, k + 1)
+
+    dma(DR("dT"), ("raw", T.tel[:]), "ldT")
+    dma(DR("dS"), ("raw", T.sec[:]), "ldS", "s")
+    for w in range(2):
+        gg = rank + n * w
+        dma(DR("lT", gg, gg + 1), ("raw", T.tel[16 * gg:16 * gg + 16, :]), "own")
+        dma(DR("lS", gg, gg + 1), ("raw", T.sec[16 * gg:16 * gg + 16, :]), "own", "s")
+    P15, PG, PW, PQ, B4, P3, PH, PP, SK, MQ, NB4, P2, Z15, P16, C32, Q1K, CS0, CS1, P316, CS2, CS3 = (
+        0, 1, 2, 3, 4, 5, 6, 7, 8, 9, 13, 14, 15, 16, 17, 18, 19, 20, 21, 24, 25)
+    iota(R("CI", 8, 9), [[0, 1]], 0, 1)
+    iota(R("IOF"), [[1, 160]])
+    iota(R("IOT"), [[1, 192]], -64)
+    iota(R("TMPF", 0, 128), [[16, 2], [0, 4], [1, 16]])
+    iota(R("TMPF", 128, 160), [[16, 16], [256, 2]])
+    iota(R("TMPF", 160, 192), [[1, 16], [16, 2]])
+    iota(R("TMPB"), [[0, 2], [1, 8], [0, 16]])
+    exchange("aT", "dT", "lT")
+    exchange("aS", "dS", "lS")
+    dma(R("TRAW"), DR("lT"), "rawT")
+    dma(R("SRAW"), DR("lS"), "rawS")
+
+    pc = R("CI", 8, 9)
+    sh, an = ALU.arith_shift_right, ALU.bitwise_and
+    I128 = R("IOT", 64, 192)
+    ms(R("CR", p1=33), 0.0)
+    for k, a, b in ((P15, 0, 15), (PG, 4, 7), (PW, 6, 1), (PQ, 4, 3), (B4, 4, 1), (P3, 0, 3), (PH, 2, 31), (PP, 0, 127), (9, 2, 3)):
+        ts(R("CI", k, k + 1), pc, a, sh, b, an)
+    ms(R("ONE1", p1=33), 1.0)
+    cp(R("CF", 0, 8), R("CI", 0, 8))
+    cp(col(P2), R("CI", 9, 10))
+    for rl in range(2):
+        ms(R("CR", 256 * rl, 256 * rl + 128, 1, 32, 33), -1.0)
+        ms(R("CR", 256 * rl + 128, 256 * rl + 256, 1, 32, 33), 32.0)
+    ts(col(SK), col(PW), 16.0, ALU.mult, col(P15), ALU.add)
+    for s in range(4):
+        ts(col(MQ + s), col(PQ), float(s), ALU.is_equal)
+    ts(col(NB4), col(B4), 0.0, ALU.is_equal)
+    ts(col(P16), col(PP), 16.0, ALU.add)
+    ts(col(C32), col(P15), 32.0, ALU.mult)
+    ts(col(22), col(PW), -128.0, ALU.mult, 64.0, ALU.add)
+    ts(col(P316), col(P3), 16.0, ALU.mult)
+    ts(col(Z15), col(PG), 16.0, ALU.mult, 15.0, ALU.add)
+    ts(col(Q1K), col(PQ), 1024.0, ALU.mult)
+    ts(R("IDB"), I128, col(PP), ALU.is_equal)
+    ts(col(23), col(22), col(P16), ALU.add)
+    ts(col(CS1), col(Q1K), col(P15), ALU.add)
+    ts(R("IZ0"), R("IOF"), col(P16), ALU.is_equal, col(NB4), ALU.mult)
+    ts(R("IZ1"), R("IOF"), col(P16), ALU.is_equal, col(B4), ALU.mult)
+    ts(col(CS0), col(CS1), col(P15), ALU.add)
+    ts(col(CS3), col(CS1), 512.0, ALU.add)
+    for s in range(4):
+        ts(R("SEL", 128 * s, 128 * s + 128), R("TMPF", 0, 128), col(SK), ALU.is_equal, col(MQ + s), ALU.mult)
+    ts(col(CS2), col(CS0), 1.0, ALU.add)
+    L1, L2, EL, FL = R("CL", 0, 32), R("CL", 32, 64), R("CL", 64, 96), R("CL", 96, 104)
+    ts(L1, R("TMPF", 128, 160), col(P15), ALU.add)
+    ts(L2, R("TMPF", 160, 192), col(C32), ALU.add)
+    ts(R("RHS", 384, 416), R("IOT", 64, 96), col(PH), ALU.is_equal)
+    ms(R("SW0", 4096, 4112), 0.0)
+    ms(R("SW1", 4096, 4112), 0.0)
+    ts(R("SUMR"), R("TMPB", 0, 256, 16), col(PG), ALU.is_equal, 4096.0, ALU.mult)
+    ts(R("OWNR"), R("TMPB"), col(PG), ALU.is_equal, -4096.0, ALU.mult)
+    ms(R("RM16"), 1.0)
+    ms(R("RM4"), 1.0)
+    for i in range(NV, 16):
+        ms(R("OWNR", i, 256, 16), 0.0)
+    ms(R("RM16", 0, 512, 16), 0.0)
+    ms(R("RM4", 0, 512, 4), 0.0)
+    ms(R("ONES"), 1.0)
+    ms(R("ZQ", 0, 256, 4), 0.0)
+    ms(R("FB", 0, 96), 0.0)
+    ms(R("FB", 224, 320), 0.0)
+    ts(R("LS"), I128, col(PP), ALU.is_gt)
+    ts(R("LI"), I128, col(PP), ALU.is_ge)
+    ts(R("BZ"), R("IOF", 0, 144), col(Z15), ALU.is_equal)
+    if nxt == 0:
+        ts(R("IF0"), R("IOF"), col(23), ALU.is_equal, col(NB4), ALU.mult)
+        ts(R("IF1"), R("IOF"), col(23), ALU.is_equal, col(B4), ALU.mult)
+    act(R("NEG"), R("IDB"), ACT.Copy, None, -1.0)
+    act(R("IDF"), R("IDB"), ACT.Copy)
+    act(R("HIR", 0, 128), R("IDB"), ACT.Copy)
+    act(R("HIR", 128, 256), R("IDB"), ACT.Copy, None, -32.0)
+    act(R("L0"), R("IDB"), ACT.Copy, None, -1024.0)
+    act(R("SELF"), R("SEL"), ACT.Copy)
+    for dg, sc in enumerate(((64, 64, 4), (32, 16, 1), (2, 1, 0), (1, 512, 32))):
+        for k in range(3):
+            act(R("RHS", 96 * dg + 32 * k, 96 * dg + 32 * k + 32), R("RHS", 384, 416), ACT.Copy, None, float(sc[k]))
+    for par in range(2):
+        act(R("SELFC", 64 * par, 64 * par + 32), R("IOF", 0, 32), ACT.Identity, col(CS2 if par else CS0), 32.0)
+        act(R("SELFC", 64 * par + 32, 64 * par + 64), R("IOF", 0, 32), ACT.Identity, col(CS3 if par else CS1), 16.0)
+    tt(R("L0"), R("L0"), R("LS"), ALU.add)
+    for rl in range(2):
+        iota(R("CR", 256 * rl, 256 * rl + 128, p1=1), [[0, 8], [-256, 16]], 256 * 15 - 128)
+        iota(R("CR", 256 * rl + 128, 256 * rl + 256, p1=1), [[0, 8], [-256, 16]], 256 * 31)
+    iota(R("TMPF", 192, 200), [[16, 4], [4, 2]])
+    iota(R("TMPF", 208, 240), [[136, 2], [64, 2], [1, 8]])
+    iota(R("THR"), [[0, 8], [-1, 4], [1, 4]])
+    iota(R("WT", 32, 64), [[1, 4], [0, 8]], 0, 4)
+    iota(R("EM"), [[0, 32], [1, 4], [0, 4]])
+    iota(R("STAB"), [[0, 32], [16, 4]])
+    iota(R("IDN"), [[1, 2], [2, 512]])
+    ts(FL, R("TMPF", 192, 200), col(P2), ALU.add)
+    ts(EL, R("TMPF", 208, 240), col(P316), ALU.add)
+    ts(R("THR"), R("THR"), 0.0, ALU.is_equal, 960.0, ALU.mult)
+    act(R("WT", 0, 32), R("WT", 32, 64), ACT.Exp, LW0, -LG)
+    act(R("THR"), R("THR"), ACT.Identity, -961.0)
+
+    BANKS = ["K0", "K1", "D0", "D1"]
+
+    def PM(a, b, nm="IZ"):
+        o = 16 + 16 * (a - b)
+        return R("%s%d" % (nm, a), o, o + 128)
+
+    def spread(src, par, sw, engines):
+        for s in range(4):
+            mm(R(BANKS[s]), R("SEL", 128 * s, 128 * s + 128), src, True, True)
+        for s in range(4):
+            o = R(sw, 1024 * s + par, 1024 * s + 1024, 2)
+            if engines[s] == "v":
+                cp(o, R(BANKS[s]))
+            else:
+                act(o, R(BANKS[s]), ACT.Copy)
+
+    def lists_pe(td, par, nm="IZ"):
+        for q0 in range(2):
+            for be in range(2):
+                c = 512 * par + 256 * be
+                mm(R("TS", 256 * q0, 256 * q0 + 256), PM(q0, be, nm), R(td, c, c + 256), be == 0, be == 1)
+
+    def lists_s():
+        act(R("TSS"), R("TS"), ACT.Copy)
+        act(R("TG"), ind(R("TSS"), L1), ACT.Copy)
+
+    def window(td, tw, par, group):
+        for w in range(2):
+            for s in range(4):
+                src = R(td, 512 * par, 512 * par + 512, 1, 64 * w + 16 * s, 64 * w + 16 * s + 16)
+                for q in range(4):
+                    c = 1024 * s + 512 * par
+                    dma(R(tw, c, c + 512, 1, 64 * w + 16 * q, 64 * w + 16 * q + 16), src, group)
+
+    def row_select(a, b, fy, hy):
+        tt(R("Y1", a, b), fy, R("RY", a, b), ALU.subtract)
+        tt(R("Y1", 64 + a, 64 + b), R("Y1", a, b), hy, ALU.mult)
+        tt(R("RN", a, b), R("Y1", 64 + a, 64 + b), R("RY", a, b), ALU.add)
+
+    def row_fix(td, h, t, land, group):
+        for w in range(2):
+            lw = 1 - w if flip else w
+            dma(R(td, 512 * h, 512 * h + 512, 1, 64 * w + t, 64 * w + 64, 16), R(land[0], land[4], land[5], 1, 64 * lw, 64 * lw + 64), group)
+
+    cp(R("TD0", 0, 512), R("TRAW", 0, 1024, 2))
+    lists_pe("TD0", 0)
+    lists_s()
+    cp(R("TD0", 512, 1024), R("TRAW", 1, 1024, 2))
+    cp(R("SD0", 0, 512), R("SRAW", 0, 1024, 2))
+    cp(R("SD0", 512, 1024), R("SRAW", 1, 1024, 2))
+    spread(R("SD0", 0, 512), 0, "SW0", "vvvs")
+    tr(R("TX"), R("TG"))
+    spread(R("SD0", 512, 1024), 1, "SW0", "ssvs")
+    cp(R("OFF0"), ind(R("TX"), L2))
+    window("TD0", "TW0", 0, "twa0")
+    window("TD0", "TW0", 1, "twb0")
+    sd = [R("SD0", 0, 512), R("SD0", 512, 1024)]
+    later, later2 = [], []
+
+    for t in range(RO):
+        par, npar, last = t % 2, 1 - t % 2, t == RO - 1
+        td, tdn = "TD%d" % t, "TD%d" % (t + 1)
+        tw, twn = "TW%d" % par, "TW%d" % npar
+        sw, swn = "SW%d" % par, "SW%d" % npar
+        off, offn = "OFF%d" % t, "OFF%d" % (t + 1)
+        own = sd[par]
+        win = R(sw)
+        tpar = R(td, 512 * par, 512 * par + 512)
+        tnp = R(td, 512 * npar, 512 * npar + 512)
+
+        def kcol(r, c0, c1, st=1):
+            return R("K%d" % (r // 2), 256 * (r % 2) + c0, 256 * (r % 2) + c1, st)
+
+        def sums(i, stop):
+            for r in range(4):
+                mm(kcol(r, i, 256, 16), R("M", 512 * i + r, 512 * i + 512, 4), R("SUMR"), False, stop and r % 2 == 1)
+
+        for k in range(2):
+            mm(R("K%d" % k), R("ONE1", p1=33), R("CR", p1=33), True, False)
+        for r in range(4):
+            mm(kcol(r, 0, 256), R(own[0], own[4] + r, own[5], 4), R("OWNR"), False, False)
+        vrows = [i for i in range(NV) if i != t - 1] + ([t - 1] if t else [])
+        srows = list(range(NV, 16))
+        ev = [(860 * (k + 1), "v", i) for k, i in enumerate(vrows)]
+        clock = 0
+        for m, i in enumerate(srows):
+            clock += 860
+            ev.append((clock, "g", i))
+            if m > 0:
+                clock += 580
+                ev.append((clock, "r", srows[m - 1]))
+            if m == len(srows) - 2:
+                clock += 580
+                ev.append((clock, "h", 0))
+        ev.append((clock + 600, "r", srows[-1]))
+        ev.append((860 * 6 + 1, "l", 0))
+        ev.append((860 * (NV - 2) + 1, "m", 0))
+        ev.sort()
+        lastsum = [e for e in ev if e[1] in "vr"][-1]
+        for e in ev:
+            i = e[2]
+            mi = R("M", 512 * i, 512 * i + 512)
+            oi = R(off, 32 * i, 32 * i + 32)
+            if e[1] == "v":
+                tt(mi, ind(win, oi), own, ALU.max)
+                sums(i, e == lastsum)
+            elif e[1] == "g":
+                act(R("G%d" % (i % 2)), ind(win, oi), ACT.Copy)
+                mm(R("D%d" % (i % 2)), R("IDB"), R("G%d" % (i % 2)), True, False)
+                mm(R("D%d" % (i % 2)), R("NEG"), own, False, True)
+            elif e[1] == "r":
+                act(mi, R("D%d" % (i % 2)), ACT.Relu)
+                sums(i, e == lastsum)
+            elif e[1] == "h":
+                act(R("HI"), tpar, ACT.Identity, 129 - 0.484375, 1.0 / 32)
+                for r in range(4):
+                    mm(kcol(r, 128, 256), R(td, 512 * par + r, 512 * par + 512, 4), R("IDF"), False, False)
+                    mm(kcol(r, 0, 256), R("HI", r, 512, 4), R("HIR"), False, False)
+            elif e[1] == "m":
+                for fn in later2:
+                    fn()
+            else:
+                for fn in later:
+                    fn()
+        if t == 0:
+            ts(R("EM"), R("EM"), col(P3), ALU.is_equal)
+
+        for k in range(2):
+            scan(R("KS", 512 * k, 512 * k + 512), R("RM16"), R("K%d" % k), ALU.mult, ALU.max)
+        cp(R("II"), R("KS", 15, 1024, 16))
+        ts(R("NC"), R("KS", 15, 1024, 16), 4096.0, ALU.is_lt, 64.0, ALU.mult)
+        ts(R("DG", 0, 64), R("II"), 1, sh, 48, an)
+        ts(R("DG", 64, 128), R("II"), 31, an)
+        tt(R("CS"), R("DG", 0, 64), R("NC"), ALU.add)
+        ts(R("DG", 192, 256), R("II"), 1, an)
+        tt(R("FB", 96, 224), ind(R("CS"), FL), R("STAB"), ALU.is_equal)
+        cnt = R("PA", 0, 128)
+        mm(cnt, R("L0"), R("FB", 96, 224), True, False)
+        for k in range(1, 4):
+            mm(cnt, R("LI"), R("FB", 96 - 32 * k, 224 - 32 * k), False, False)
+            mm(cnt, R("LS"), R("FB", 96 + 32 * k, 224 + 32 * k), False, k == 3)
+        for r in range(4):
+            act(R("ZP", 128 * r, 128 * r + 128), kcol(r, 0, 128), ACT.Sign, 4095.5, -1.0)
+        act(R("ZP"), R("ZP"), ACT.Relu)
+        ts(R("AB", 128, 192), R("DG", 192, 256), 32.0, ALU.mult)
+        ts(R("DG", 128, 192), R("II"), 1, sh, 15, an)
+        tt(R("AB", 64, 120), R("DG", 64, 120), R("AB", 136, 192), ALU.add)
+        tt(R("AB", 0, 56), R("DG", 0, 56), R("DG", 136, 192), ALU.add)
+        tt(R("OK"), cnt, R("THR"), ALU.is_le)
+        scan(R("TH", 0, 128), R("RM4", 0, 128), R("OK"), ALU.mult, ALU.max)
+        tt(R("TH", 128, 160), R("TH", 3, 128, 4), R("WT", 0, 32), ALU.mult)
+        for r in range(4):
+            mm(R("ZN", r, 512, 4), R("ZP", 128 * r, 128 * r + 128), R("IDB"), True, True)
+
+        if not last:
+            pass_on("aa%d" % t, tnp, R("LT", 1024 * t, 1024 * t + 512), R(tdn, 512 * npar, 512 * npar + 512), "cpa%d" % t)
+            dma(R("RY", 32 * npar, 32 * npar + 32), R(td, 512 * npar, 512 * npar + 512, 1, t, 128, 16), "rya%d" % t)
+
+        for blk in range(16):
+            q, r = blk // 4, blk % 4
+            byS = (blk + 1) * NB // 16 != blk * NB // 16
+            for w in range(2):
+                G, k = 4 * w + q, 2 * blk + w
+                c = 16 * r + G
+                th = 128 + 8 * r + G
+                bcol = R("AB", 64 + c, 65 + c)
+                ts(R("AA", 128 * k, 128 * k + 128), R("IOT", 64 - 64 * w, 192 - 64 * w), R("AB", c, c + 1), ALU.is_equal,
+                   R("TH", th, th + 1), ALU.mult)
+                if byS:
+                    x = 128 * (blk % 2) + 64 * w
+                    act(R("BX", x, x + 64), R("IOT", 64, 128), ACT.Abs, bcol, -1.0)
+                else:
+                    ts(R("BB", 64 * k, 64 * k + 64), R("IOT", 64, 128), bcol, ALU.is_equal)
+            if byS:
+                act(R("BB", 128 * blk, 128 * blk + 128), R("BX", 128 * (blk % 2), 128 * (blk % 2) + 128), ACT.Relu, 1.0, -1.0)
+            for h in range(2):
+                o = R("D%d" % h, (3 - q) * 4 + r, 512, 16)
+                for w in range(2):
+                    k = 2 * blk + w
+                    mm(o, R("AA", 128 * k, 128 * k + 128), R("BB", 64 * k + 32 * h, 64 * k + 32 * h + 32), w == 0, w == 1)
+        tt(R("EE"), ind(R("DG"), EL), R("EM"), ALU.mult)
+        for dg in range(4):
+            mm(R("PB", 0, 96), R("EE", 128 * dg, 128 * dg + 128), R("RHS", 96 * dg, 96 * dg + 96), dg == 0, dg == 3)
+        if not last:
+            lists_pe(td, npar, "IF" if nxt == 0 else "IZ")
+        if t == 0:
+            act(R("IDN"), R("IDN"), ACT.Identity, col(Q1K))
+        for h in range(2):
+            scan(R("HS", 512 * h, 512 * h + 512), R("RM4"), R("D%d" % h), ALU.mult, ALU.max)
+        for qq in range(1, 4):
+            ts(R("ZQ", qq, 256, 4), R("HS", 4 * qq + 3, 1024, 16), 0.0, ALU.is_equal)
+        scan(R("H2"), R("ZQ"), R("HS", 3, 1024, 4), ALU.mult, ALU.add)
+        hs = R("H2", 3, 256, 4)
+        ts(R("XY", 0, 64), hs, 1.0, ALU.min, 2.0 ** 62, ALU.mult)
+        ts(R("XY", 64, 128), hs, 1.0, ALU.max, 2.0 ** -62, ALU.mult)
+        act(R("LL"), R("XY"), ACT.Ln, 1e-23)
+        if not last:
+            lists_s()
+        scan(R("Q2"), R("ONES"), R("ZQ"), ALU.add, ALU.mult)
+        ts(R("QS", 64, 128), hs, 0.0, ALU.is_equal, -8192.0 * LG, ALU.mult)
+        ts(R("QS", 0, 64), R("Q2", 3, 256, 4), -512.0 * LG, ALU.mult, -LW0 - 0.448 * LG, ALU.add)
+        tt(R("T1", 0, 64), R("LL", 0, 64), R("LL", 64, 128), ALU.add)
+        tt(R("QS", 0, 64), R("QS", 0, 64), R("QS", 64, 128), ALU.add)
+        cp(R("SBU"), R("PB", 64, 96))
+        tt(R("T1", 64, 128), R("T1", 0, 64), R("QS", 0, 64), ALU.add)
+        tt(R("DC"), R("PB", 0, 64), R("SELFC", 64 * par, 64 * par + 64), ALU.subtract)
+        ts(R("T1", 128, 192), R("T1", 64, 128), -1.0 / LG, ALU.mult, 2048.0, ALU.min)
+        cp(R("ID"), R("T1", 128, 192))
+        ts(R("FF"), R("ID"), 2.0, ALU.mult, float(par), ALU.add)
+        ts(R("FU"), R("ID"), 2.0, ALU.mult, float(par), ALU.add)
+        for s in range(4):
+            mm(R("PA", 64 * s, 64 * s + 64), R("SELF", 128 * s, 128 * s + 128), R("FF"), True, True)
+        act(R("WW"), R("PA", 0, 256), ACT.Copy)
+        if not last:
+            ln = R("LN", 32 * t, 32 * t + 32)
+            send("an%d" % t, [(nxt, R("FF", 32 * npar, 32 * npar + 32), ln)], wide)
+            arrive("an%d" % t, [ln], wide)
+        for pp in range(2):
+            for s0 in range(2):
+                for h0 in range(2):
+                    c = 128 + 32 * pp + 16 * s0
+                    mm(R("PB", c, c + 16), PM(s0, h0), R("FF", 32 * pp + h0, 32 * pp + 32, 2), h0 == 0, h0 == 1)
+
+        keep = R("SD0", 512 * npar, 512 * npar + 512) if sd[npar][0] != "SD0" else R("SB%d" % npar)
+        done = R("SD0", 512 * par, 512 * par + 512) if own[0] != "SD0" else R("SB%d" % par)
+        tt(keep, ind(win, R("FU", 32 * npar, 32 * npar + 32)), sd[npar], ALU.max)
+        if not last:
+            spread(keep, npar, swn, "ssss")
+            tr(R("TX"), R("TG"))
+        else:
+            act(R("OT", npar, 1024, 2), tnp, ACT.Copy)
+            act(R("OS", npar, 1024, 2), keep, ACT.Copy)
+        tt(R("EQ"), ind(R("WW"), R("SBU")), R("IDN", 512 * par, 512 * par + 512), ALU.is_equal)
+        if not last:
+            cp(R("OFS"), ind(R("TX"), L2))
+            send("ao%d" % t, [(nxt, R("OFS"), R(offn))], wide)
+            arrive("ao%d" % t, [R(offn)], wide)
+        conn = R("PA", 256, 288)
+        for l in range(16):
+            mm(conn, R("BZ", 15 - l, 143 - l), R("EQ", l, 512, 16), l == 0, l == 15)
+        tt(R("SA"), ind(win, R("FU", 32 * par, 32 * par + 32)), own, ALU.max)
+        tt(R("C1", 0, 32), conn, R("DC", 0, 32), ALU.mult)
+        tt(R("C1", 32, 64), conn, R("DC", 32, 64), ALU.mult)
+        tr(R("FY", 0, 64), R("PB", 128, 192))
+        tt(R("C1", 64, 128), R("C1", 0, 64), R("SELFC", 64 * par, 64 * par + 64), ALU.add)
+        if last:
+            for pp in range(2):
+                cp(R("FY", 64 + pp, 128, 2), R("FY", 32 * pp, 32 * pp + 32))
+        else:
+            ts(R("HY"), R("FY", 0, 64), 4096.0, ALU.is_lt)
+        cp(R("CU"), R("C1", 64, 128))
+        sd = [None, None]
+        sd[par], sd[npar] = done, keep
+        if not last:
+            tt(done, ind(win, R("CU", 0, 32)), R("SA"), ALU.max)
+            spread(done, par, swn, "ssss")
+            if flip:
+                hand(R("OLDX", 32, 64), ln, "cpn%d" % t)
+
+            def row_list(t=t, offn=offn, fx=R("OLDX", 32, 64) if flip else ln):
+                cp(R("OLDX", 0, 32), R(offn, 32 * t, 32 * t + 32))
+                ts(R("X1", 0, 32), fx, 4096.0, ALU.is_lt)
+                tt(R("X1", 32, 64), fx, R("OLDX", 0, 32), ALU.subtract)
+                tt(R("X1", 64, 96), R("X1", 32, 64), R("X1", 0, 32), ALU.mult)
+                tt(R("X1", 0, 32), R("X1", 64, 96), R("OLDX", 0, 32), ALU.add)
+                cp(R(offn, 32 * t, 32 * t + 32), R("X1", 0, 32))
+            later2 = [row_list]
+            a = 32 * npar
+            row_select(a, a + 32, R("FY", a, a + 32), R("HY", a, a + 32))
+            lra = R("LR", 64 * t, 64 * t + 32)
+            send("ara%d" % t, [(nxt, R("RN", a, a + 32), lra)], wide)
+            arrive("ara%d" % t, [lra], wide)
+            row_fix(tdn, npar, t, lra, "fxa%d" % t)
+
+        tt(R("TD_"), ind(R(tw), R("CU", 32, 64)), tpar, ALU.subtract)
+        tt(R("TS"), R("ZN"), R("TD_"), ALU.mult)
+        if not last:
+            tt(R("TB"), R("TS"), tpar, ALU.add)
+            dma(R("RY", 32 * par, 32 * par + 32), R("TB", 0, 512, 1, t, 128, 16), "ryb%d" % t)
+            pass_on("ab%d" % t, R("TB"), R("LT", 1024 * t + 512, 1024 * t + 1024), R(tdn, 512 * par, 512 * par + 512), "cpb%d" % t)
+
+            def rest(t=t, par=par, npar=npar, tdn=tdn, twn=twn):
+                a = 32 * par
+                row_select(a, a + 32, R("FY", a, a + 32), R("HY", a, a + 32))
+                lrb = R("LR", 64 * t + 32, 64 * t + 64)
+                send("arb%d" % t, [(nxt, R("RN", a, a + 32), lrb)], wide)
+                arrive("arb%d" % t, [lrb], wide)
+                window(tdn, twn, npar, "twa%d" % (t + 1))
+                row_fix(tdn, par, t, lrb, "fxb%d" % t)
+                window(tdn, twn, par, "twb%d" % (t + 1))
+            later = [rest]
+            continue
+
+        tt(R("OT", par, 1024, 2), R("TS"), tpar, ALU.add)
+        dma(R("RY"), R("OT", 0, 1024, 1, t, 128, 16), "ryl", "s")
+        dma(DR("oT"), R("OT"), "oT")
+        tt(done, ind(win, R("CU", 0, 32)), R("SA"), ALU.max)
+        cp(R("OS", par, 1024, 2), done)
+        dma(DR("oS"), R("OS"), "oS", "s")
+        ts(R("HY"), R("FY", 64, 128), 4096.0, ALU.is_lt)
+        row_select(0, 64, R("FY", 64, 128), R("HY"))
+        exchange("aoT", "oT", "loT")
+        send("aRI", [(d, R("RN"), R("LRI", 64 * rank, 64 * rank + 64)) for d in others], 2 * w6)
+        arrive("aRI", [R("LRI", 64 * d, 64 * d + 64) for d in others], 6 * w6)
+        exchange("aoS", "oS", "loS")
+        for mine in (True, False):
+            worlds = [gg for gg in range(8) if (gg % n == rank) == mine]
+            for gg in worlds:
+                p0 = 64 * (gg // n) + 16 * rank
+                a = R("OT", 0, 1024, 1, p0 + t + 1, p0 + 16) if mine else DR("loT", gg, gg + 1, 8 * t + 8, 128)
+                b = R("OT", 0, 1024, 1, p0, p0 + t) if mine else DR("loT", gg, gg + 1, 0, 8 * t)
+                dma(("raw", T.ytel[16 * gg + t + 1:16 * gg + 16, :]), a, "out", "y")
+                dma(("raw", T.ytel[16 * gg:16 * gg + t, :]), b, "out", "s")
+            for gg in worlds:
+                p0 = 64 * (gg // n) + 16 * rank
+                c = R("RN", 0, 64, 1, p0, p0 + 16) if mine else R("LRI", 64 * (gg % n), 64 * (gg % n) + 64, 1, p0, p0 + 16)
+                dma(("raw", T.ytel[16 * gg + t:16 * gg + t + 1, :]), c, "out", "s")
+                a = R("OS", 0, 1024, 1, p0, p0 + 16) if mine else DR("loS", gg, gg + 1)
+                dma(("raw", T.ysec[16 * gg:16 * gg + 16, :]), a, "out", "y")
+
+    emit(ops, Q, T, g)
+
+
+def emit(ops, Q, T, g):
+    hist = {}
+    for k, o in enumerate(ops):
+        deps = set()
+        for kind in ("r", "w"):
+            for a in o[kind]:
+                psum = SCRATCH[a[0]][0] == "psum"
+                for j, kj, b in hist.get(a[0], []):
+                    pe = ops[j]["e"]
+                    if psum and pe == "p" and o["e"] == "p":
+                        continue
+                    if (kind == "w" or kj == "w" or (psum and pe != o["e"])) and _touch(a, b):
+                        deps.add(j)
+        for kind in ("r", "w"):
+            for a in o[kind]:
+                hist.setdefault(a[0], []).append((k, kind, a))
+        o["d"] = deps if o["e"] != "x" else set()
+        best = {}
+        for j in o["d"]:
+            if ops[j]["grp"] is None:
+                best[ops[j]["e"]] = max(best.get(ops[j]["e"], -1), j)
+        o["cd"] = best
+        for j in best.values():
+            ops[j]["sig"] = True
+    count, total = {}, {}
+    for o in ops:
+        if o["grp"] is not None:
+            total[o["grp"]] = total.get(o["grp"], 0) + o["n"]
+        elif o.get("sig"):
+            count[o["e"]] = count.get(o["e"], 0) + 1
+            o["tok"] = count[o["e"]]
+    seen = {}
+    for o in ops:
+        if o["e"] == "x":
+            continue
+        need = {}
+        for j in o["d"]:
+            if ops[j]["grp"] is not None:
+                need[ops[j]["grp"]] = total[ops[j]["grp"]]
+        for e in o["cd"]:
+            need[ENGSEM[e]] = ops[o["cd"][e]]["tok"]
+        for s in sorted(need):
+            if seen.get((o["e"], s), 0) < need[s]:
+                Q[o["e"]].wait_ge(T.sem[s], need[s])
+                seen[(o["e"], s)] = need[s]
+        ins = o["f"]()
+        if ins is not None:
+            if o["grp"] is not None:
+                ins.then_inc(T.sem[o["grp"]], 16)
+            elif o.get("sig"):
+                ins.then_inc(T.sem[ENGSEM[o["e"]]], 1)
+    for e in count:
+        g.wait_ge(T.sem[ENGSEM[e]], count[e])
+    for s in total:
+        g.wait_ge(T.sem[s], total[s])

@@ -5,7 +5,7 @@ from concourse.mybir import AluOpType, ActivationFunctionType
 ALU = AluOpType
 ACT = ActivationFunctionType
 NV = 10
-NB = 11
+NB = 13
 RO = 4
 LG = math.log(1.40)
 LW0 = 124 * math.log(2.0)
@@ -23,17 +23,17 @@ _decl("psum", F, K0=512, K1=512, D0=512, D1=512, ZN=512, PA=512, PB=512, TS=512)
 _decl("dram", I, dT=[8, 128, 128], lT=[8, 128, 128])
 _decl("dram", B, dS=[8, 128, 128], lS=[8, 128, 128], oS=[8, 128, 128], loS=[8, 128, 128])
 _decl("dram", F, oT=[8, 128, 128], loT=[8, 128, 128])
-_decl("sbuf", I, CI=16, TRAW=1024, II=64, DG=256, NC=64, ID=64)
-_decl("sbuf", U, OFF0=512, OFF1=512, OFF2=512, OFF3=512, OFS=512, CL=128, FU=64, SBU=32, CU=64)
+_decl("sbuf", I, CI=16, TRAW=1024, TRA2=1024, II=64, DG=256, NC=64, ID=64)
+_decl("sbuf", U, OFF0=512, OFF1=512, OFF2=512, OFF3=512, OFS=512, CL=160, FU=64, SBU=32, CU=64)
 _decl("sbuf", B, SRAW=1024, SW0=4112, SW1=4112, SA=512, SB0=512, SB1=512, SD0=1024, M=8192, G0=512, G1=512, HI=512, IOT=192,
       IDB=128, NEG=128, HIR=256, SEL=512, SUMR=16, OWNR=256, CR=512, ONE1=128, RM16=512, RM4=512, ONES=256, LS=128, LI=128,
-      L0=128, FB=320, EM=512, RHS=416, BZ=144, AA=4096, BB=2048, BX=256, EE=512, ZP=512, EQ=512, OS=1024, TMPB=256)
+      L0=128, FB=320, EM=512, RHS=416, BZ=144, AA=4096, BB=2048, BX=2048, EE=512, ZP=512, EQ=512, OS=1024, TMPB=256)
 _decl("sbuf", F, CF=32, TD0=1024, TD1=1024, TD2=1024, TD3=1024, TW0=4096, TW1=4096, LT=3072, LR=192, LN=96, IOF=160, IDF=128,
       SELF=512, IZ0=160, IZ1=160, IF0=160, IF1=160, WT=64, THR=128, STAB=128, SELFC=128, IDN=1024, KS=1024, CS=64, AB=192, OK=128,
       TH=160, HS=1024, ZQ=256, H2=256, Q2=256, XY=128, LL=128, QS=128, T1=192, FF=64, WW=256, DC=64, C1=128, TSS=512, TG=512,
       TX=512, OLDX=64, X1=96, FY=128, HY=64, RY=64, Y1=128, RN=64, TD_=512, TB=512, OT=1024, LRI=256, TMPF=256)
 
-_DMA_GROUPS = ["ldT", "ldS", "own", "rawT", "rawS", "oS", "oT", "out", "ryl"] + ["%s%d" % (n, t) for t in range(3) for n in
+_DMA_GROUPS = ["ldT", "ldS", "own", "rawT", "rawU", "rawS", "oS", "oT", "out", "ryl"] + ["%s%d" % (n, t) for t in range(3) for n in
               ("rya", "ryb", "cpa", "cpb", "fxa", "fxb", "cpn")] + ["tw%s%d" % (h, t) for t in range(4) for h in "ab"]
 _ARRIVE = ["aT", "aS", "aoS", "aoT", "aRI"] + ["%s%d" % (n, t) for t in range(3) for n in ("aa", "ab", "ara", "arb", "ao", "an")]
 SEMAPHORES = ["ev", "es", "ep", "eg"] + _DMA_GROUPS + _ARRIVE + ["s" + n for n in _ARRIVE]
@@ -53,6 +53,8 @@ def DR(name, k0=0, k1=8, r0=0, r1=128):
 def _touch(a, b):
     if SCRATCH[a[0]][0] == "psum":
         return True
+    if a[6] == b[6] > 1 and (a[4] - b[4]) % a[6]:
+        return False
     return a[1] < b[2] and b[1] < a[2] and a[4] < b[5] and b[4] < a[5]
 
 
@@ -177,11 +179,13 @@ def rank_program(g, core, T, topo):
     def col(k):
         return R("CF", k, k + 1)
 
-    dma(DR("dT"), ("raw", T.tel[:]), "ldT")
+    for be in range(2):
+        dma(DR("dT", 0, 8, 64 * be, 64 * be + 64), ("raw", T.tel[:, 512 * be:512 * be + 512]), "ldT")
     dma(DR("dS"), ("raw", T.sec[:]), "ldS", "s")
     for w in range(2):
         gg = rank + n * w
-        dma(DR("lT", gg, gg + 1), ("raw", T.tel[16 * gg:16 * gg + 16, :]), "own")
+        for be in range(2):
+            dma(DR("lT", gg, gg + 1, 64 * be, 64 * be + 64), ("raw", T.tel[16 * gg:16 * gg + 16, 512 * be:512 * be + 512]), "own")
         dma(DR("lS", gg, gg + 1), ("raw", T.sec[16 * gg:16 * gg + 16, :]), "own", "s")
     P15, PG, PW, PQ, B4, P3, PH, PP, SK, MQ, NB4, P2, Z15, P16, C32, Q1K, CS0, CS1, P316, CS2, CS3 = (
         0, 1, 2, 3, 4, 5, 6, 7, 8, 9, 13, 14, 15, 16, 17, 18, 19, 20, 21, 24, 25)
@@ -194,8 +198,13 @@ def rank_program(g, core, T, topo):
     iota(R("TMPB"), [[0, 2], [1, 8], [0, 16]])
     exchange("aT", "dT", "lT")
     exchange("aS", "dS", "lS")
-    dma(R("TRAW"), DR("lT"), "rawT")
+    for gg in range(8):
+        for be in range(2):
+            p0, c0 = 32 * (gg // 2) + 16 * be, 512 * (gg % 2)
+            dma(R("TRA2", c0, c0 + 512, 1, p0, p0 + 16), DR("lT", gg, gg + 1, 64 * be, 64 * be + 64), "rawU")
     dma(R("SRAW"), DR("lS"), "rawS")
+    for be in range(2):
+        dma(R("TRAW", 512 * be, 512 * be + 512), DR("lT", 0, 8, 64 * be, 64 * be + 64), "rawT")
 
     pc = R("CI", 8, 9)
     sh, an = ALU.arith_shift_right, ALU.bitwise_and
@@ -231,6 +240,7 @@ def rank_program(g, core, T, topo):
     ts(col(CS2), col(CS0), 1.0, ALU.add)
     L1, L2, EL, FL = R("CL", 0, 32), R("CL", 32, 64), R("CL", 64, 96), R("CL", 96, 104)
     ts(L1, R("TMPF", 128, 160), col(P15), ALU.add)
+    ts(R("CL", 128, 160), R("TMPF", 128, 160), col(P15), ALU.add, 2.0, ALU.mult)
     ts(L2, R("TMPF", 160, 192), col(C32), ALU.add)
     ts(R("RHS", 384, 416), R("IOT", 64, 96), col(PH), ALU.is_equal)
     ms(R("SW0", 4096, 4112), 0.0)
@@ -279,6 +289,7 @@ def rank_program(g, core, T, topo):
     ts(FL, R("TMPF", 192, 200), col(P2), ALU.add)
     ts(EL, R("TMPF", 208, 240), col(P316), ALU.add)
     ts(R("THR"), R("THR"), 0.0, ALU.is_equal, 960.0, ALU.mult)
+    ts(R("EM"), R("EM"), col(P3), ALU.is_equal)
     act(R("WT", 0, 32), R("WT", 32, 64), ACT.Exp, LW0, -LG)
     act(R("THR"), R("THR"), ACT.Identity, -961.0)
 
@@ -298,16 +309,6 @@ def rank_program(g, core, T, topo):
             else:
                 act(o, R(BANKS[s]), ACT.Copy)
 
-    def lists_pe(td, par, nm="IZ"):
-        for q0 in range(2):
-            for be in range(2):
-                c = 512 * par + 256 * be
-                mm(R("TS", 256 * q0, 256 * q0 + 256), PM(q0, be, nm), R(td, c, c + 256), be == 0, be == 1)
-
-    def lists_s():
-        act(R("TSS"), R("TS"), ACT.Copy)
-        act(R("TG"), ind(R("TSS"), L1), ACT.Copy)
-
     def window(td, tw, par, group):
         for w in range(2):
             for s in range(4):
@@ -317,29 +318,28 @@ def rank_program(g, core, T, topo):
                     dma(R(tw, c, c + 512, 1, 64 * w + 16 * q, 64 * w + 16 * q + 16), src, group)
 
     def row_select(a, b, fy, hy):
-        tt(R("Y1", a, b), fy, R("RY", a, b), ALU.subtract)
-        tt(R("Y1", 64 + a, 64 + b), R("Y1", a, b), hy, ALU.mult)
-        tt(R("RN", a, b), R("Y1", 64 + a, 64 + b), R("RY", a, b), ALU.add)
+        return [lambda: tt(R("Y1", a, b), fy, R("RY", a, b), ALU.subtract),
+                lambda: tt(R("Y1", 64 + a, 64 + b), R("Y1", a, b), hy, ALU.mult),
+                lambda: tt(R("RN", a, b), R("Y1", 64 + a, 64 + b), R("RY", a, b), ALU.add)]
 
     def row_fix(td, h, t, land, group):
         for w in range(2):
             lw = 1 - w if flip else w
             dma(R(td, 512 * h, 512 * h + 512, 1, 64 * w + t, 64 * w + 64, 16), R(land[0], land[4], land[5], 1, 64 * lw, 64 * lw + 64), group)
 
-    cp(R("TD0", 0, 512), R("TRAW", 0, 1024, 2))
-    lists_pe("TD0", 0)
-    lists_s()
-    cp(R("TD0", 512, 1024), R("TRAW", 1, 1024, 2))
+    cp(R("TG"), ind(R("TRA2"), R("CL", 128, 160)))
     cp(R("SD0", 0, 512), R("SRAW", 0, 1024, 2))
     cp(R("SD0", 512, 1024), R("SRAW", 1, 1024, 2))
-    spread(R("SD0", 0, 512), 0, "SW0", "vvvs")
     tr(R("TX"), R("TG"))
-    spread(R("SD0", 512, 1024), 1, "SW0", "ssvs")
+    spread(R("SD0", 0, 512), 0, "SW0", "ssss")
     cp(R("OFF0"), ind(R("TX"), L2))
+    spread(R("SD0", 512, 1024), 1, "SW0", "vvsv")
+    cp(R("TD0", 0, 512), R("TRAW", 0, 1024, 2))
+    cp(R("TD0", 512, 1024), R("TRAW", 1, 1024, 2))
     window("TD0", "TW0", 0, "twa0")
     window("TD0", "TW0", 1, "twb0")
     sd = [R("SD0", 0, 512), R("SD0", 512, 1024)]
-    later, later2 = [], []
+    later = {}
 
     for t in range(RO):
         par, npar, last = t % 2, 1 - t % 2, t == RO - 1
@@ -365,20 +365,23 @@ def rank_program(g, core, T, topo):
             mm(kcol(r, 0, 256), R(own[0], own[4] + r, own[5], 4), R("OWNR"), False, False)
         vrows = [i for i in range(NV) if i != t - 1] + ([t - 1] if t else [])
         srows = list(range(NV, 16))
-        ev = [(860 * (k + 1), "v", i) for k, i in enumerate(vrows)]
+        ev, clock = [], 0
+        for k, i in enumerate(vrows):
+            clock += 860
+            ev.append((clock, "v", i))
+            ev.append((clock + 1, "l", k))
+            clock += 110 * len(later.get(k, []))
         clock = 0
         for m, i in enumerate(srows):
             clock += 860
             ev.append((clock, "g", i))
             if m > 0:
-                clock += 580
+                clock += 540
                 ev.append((clock, "r", srows[m - 1]))
-            if m == len(srows) - 2:
-                clock += 580
+            if m == 3:
+                clock += 540
                 ev.append((clock, "h", 0))
         ev.append((clock + 600, "r", srows[-1]))
-        ev.append((860 * 6 + 1, "l", 0))
-        ev.append((860 * (NV - 2) + 1, "m", 0))
         ev.sort()
         lastsum = [e for e in ev if e[1] in "vr"][-1]
         for e in ev:
@@ -400,14 +403,9 @@ def rank_program(g, core, T, topo):
                 for r in range(4):
                     mm(kcol(r, 128, 256), R(td, 512 * par + r, 512 * par + 512, 4), R("IDF"), False, False)
                     mm(kcol(r, 0, 256), R("HI", r, 512, 4), R("HIR"), False, False)
-            elif e[1] == "m":
-                for fn in later2:
-                    fn()
             else:
-                for fn in later:
+                for fn in later.get(i, []):
                     fn()
-        if t == 0:
-            ts(R("EM"), R("EM"), col(P3), ALU.is_equal)
 
         for k in range(2):
             scan(R("KS", 512 * k, 512 * k + 512), R("RM16"), R("K%d" % k), ALU.mult, ALU.max)
@@ -423,6 +421,11 @@ def rank_program(g, core, T, topo):
         for k in range(1, 4):
             mm(cnt, R("LI"), R("FB", 96 - 32 * k, 224 - 32 * k), False, False)
             mm(cnt, R("LS"), R("FB", 96 + 32 * k, 224 + 32 * k), False, k == 3)
+        if not last:
+            for q0 in range(2):
+                for be in range(2):
+                    c = 512 * npar + 256 * be
+                    mm(R("TS", 256 * q0, 256 * q0 + 256), PM(q0, be, "IF" if nxt == 0 else "IZ"), R(td, c, c + 256), be == 0, be == 1)
         for r in range(4):
             act(R("ZP", 128 * r, 128 * r + 128), kcol(r, 0, 128), ACT.Sign, 4095.5, -1.0)
         act(R("ZP"), R("ZP"), ACT.Relu)
@@ -430,68 +433,77 @@ def rank_program(g, core, T, topo):
         ts(R("DG", 128, 192), R("II"), 1, sh, 15, an)
         tt(R("AB", 64, 120), R("DG", 64, 120), R("AB", 136, 192), ALU.add)
         tt(R("AB", 0, 56), R("DG", 0, 56), R("DG", 136, 192), ALU.add)
+        byS = [(blk + 1) * NB // 16 != blk * NB // 16 for blk in range(16)]
         tt(R("OK"), cnt, R("THR"), ALU.is_le)
+        tt(R("EE", 0, 256), ind(R("DG"), R("CL", 64, 80)), R("EM", 0, 256), ALU.mult)
         scan(R("TH", 0, 128), R("RM4", 0, 128), R("OK"), ALU.mult, ALU.max)
+        tt(R("EE", 256, 512), ind(R("DG"), R("CL", 80, 96)), R("EM", 256, 512), ALU.mult)
         tt(R("TH", 128, 160), R("TH", 3, 128, 4), R("WT", 0, 32), ALU.mult)
+
+        def bcol(k):
+            c = 64 + 16 * (k // 2 % 4) + 4 * (k % 2) + k // 8
+            return R("AB", c, c + 1)
+
+        for k in range(32):
+            if not byS[k // 2]:
+                ts(R("BB", 64 * k, 64 * k + 64), R("IOT", 64, 128), bcol(k), ALU.is_equal)
+        prev = None
+        for blk in [b for b in range(16) if byS[b]] + [None]:
+            if blk is not None:
+                for k in (2 * blk, 2 * blk + 1):
+                    act(R("BX", 64 * k, 64 * k + 64), R("IOT", 64, 128), ACT.Abs, bcol(k), -1.0)
+            if prev is not None:
+                act(R("BB", 128 * prev, 128 * prev + 128), R("BX", 128 * prev, 128 * prev + 128), ACT.Relu, 1.0, -1.0)
+            prev = blk
+        for dg in range(4):
+            mm(R("PB", 0, 96), R("EE", 128 * dg, 128 * dg + 128), R("RHS", 96 * dg, 96 * dg + 96), dg == 0, dg == 3)
         for r in range(4):
             mm(R("ZN", r, 512, 4), R("ZP", 128 * r, 128 * r + 128), R("IDB"), True, True)
-
         if not last:
             pass_on("aa%d" % t, tnp, R("LT", 1024 * t, 1024 * t + 512), R(tdn, 512 * npar, 512 * npar + 512), "cpa%d" % t)
             dma(R("RY", 32 * npar, 32 * npar + 32), R(td, 512 * npar, 512 * npar + 512, 1, t, 128, 16), "rya%d" % t)
-
         for blk in range(16):
             q, r = blk // 4, blk % 4
-            byS = (blk + 1) * NB // 16 != blk * NB // 16
             for w in range(2):
                 G, k = 4 * w + q, 2 * blk + w
                 c = 16 * r + G
                 th = 128 + 8 * r + G
-                bcol = R("AB", 64 + c, 65 + c)
                 ts(R("AA", 128 * k, 128 * k + 128), R("IOT", 64 - 64 * w, 192 - 64 * w), R("AB", c, c + 1), ALU.is_equal,
                    R("TH", th, th + 1), ALU.mult)
-                if byS:
-                    x = 128 * (blk % 2) + 64 * w
-                    act(R("BX", x, x + 64), R("IOT", 64, 128), ACT.Abs, bcol, -1.0)
-                else:
-                    ts(R("BB", 64 * k, 64 * k + 64), R("IOT", 64, 128), bcol, ALU.is_equal)
-            if byS:
-                act(R("BB", 128 * blk, 128 * blk + 128), R("BX", 128 * (blk % 2), 128 * (blk % 2) + 128), ACT.Relu, 1.0, -1.0)
             for h in range(2):
                 o = R("D%d" % h, (3 - q) * 4 + r, 512, 16)
                 for w in range(2):
                     k = 2 * blk + w
                     mm(o, R("AA", 128 * k, 128 * k + 128), R("BB", 64 * k + 32 * h, 64 * k + 32 * h + 32), w == 0, w == 1)
-        tt(R("EE"), ind(R("DG"), EL), R("EM"), ALU.mult)
-        for dg in range(4):
-            mm(R("PB", 0, 96), R("EE", 128 * dg, 128 * dg + 128), R("RHS", 96 * dg, 96 * dg + 96), dg == 0, dg == 3)
         if not last:
-            lists_pe(td, npar, "IF" if nxt == 0 else "IZ")
+            act(R("TSS"), R("TS"), ACT.Copy)
+            act(R("TG"), ind(R("TSS"), L1), ACT.Copy)
         if t == 0:
             act(R("IDN"), R("IDN"), ACT.Identity, col(Q1K))
+        cp(R("SBU"), R("PB", 64, 96))
         for h in range(2):
             scan(R("HS", 512 * h, 512 * h + 512), R("RM4"), R("D%d" % h), ALU.mult, ALU.max)
+        tt(R("DC"), R("PB", 0, 64), R("SELFC", 64 * par, 64 * par + 64), ALU.subtract)
         for qq in range(1, 4):
             ts(R("ZQ", qq, 256, 4), R("HS", 4 * qq + 3, 1024, 16), 0.0, ALU.is_equal)
         scan(R("H2"), R("ZQ"), R("HS", 3, 1024, 4), ALU.mult, ALU.add)
+        scan(R("Q2"), R("ONES"), R("ZQ"), ALU.add, ALU.mult)
         hs = R("H2", 3, 256, 4)
         ts(R("XY", 0, 64), hs, 1.0, ALU.min, 2.0 ** 62, ALU.mult)
         ts(R("XY", 64, 128), hs, 1.0, ALU.max, 2.0 ** -62, ALU.mult)
         act(R("LL"), R("XY"), ACT.Ln, 1e-23)
-        if not last:
-            lists_s()
-        scan(R("Q2"), R("ONES"), R("ZQ"), ALU.add, ALU.mult)
         ts(R("QS", 64, 128), hs, 0.0, ALU.is_equal, -8192.0 * LG, ALU.mult)
         ts(R("QS", 0, 64), R("Q2", 3, 256, 4), -512.0 * LG, ALU.mult, -LW0 - 0.448 * LG, ALU.add)
-        tt(R("T1", 0, 64), R("LL", 0, 64), R("LL", 64, 128), ALU.add)
+        if not last:
+            tr(R("TX"), R("TG"))
+            act(R("TSS"), ind(R("TX"), L2), ACT.Copy)
         tt(R("QS", 0, 64), R("QS", 0, 64), R("QS", 64, 128), ALU.add)
-        cp(R("SBU"), R("PB", 64, 96))
+        tt(R("T1", 0, 64), R("LL", 0, 64), R("LL", 64, 128), ALU.add)
         tt(R("T1", 64, 128), R("T1", 0, 64), R("QS", 0, 64), ALU.add)
-        tt(R("DC"), R("PB", 0, 64), R("SELFC", 64 * par, 64 * par + 64), ALU.subtract)
         ts(R("T1", 128, 192), R("T1", 64, 128), -1.0 / LG, ALU.mult, 2048.0, ALU.min)
         cp(R("ID"), R("T1", 128, 192))
-        ts(R("FF"), R("ID"), 2.0, ALU.mult, float(par), ALU.add)
         ts(R("FU"), R("ID"), 2.0, ALU.mult, float(par), ALU.add)
+        ts(R("FF"), R("ID"), 2.0, ALU.mult, float(par), ALU.add)
         for s in range(4):
             mm(R("PA", 64 * s, 64 * s + 64), R("SELF", 128 * s, 128 * s + 128), R("FF"), True, True)
         act(R("WW"), R("PA", 0, 256), ACT.Copy)
@@ -510,82 +522,85 @@ def rank_program(g, core, T, topo):
         tt(keep, ind(win, R("FU", 32 * npar, 32 * npar + 32)), sd[npar], ALU.max)
         if not last:
             spread(keep, npar, swn, "ssss")
-            tr(R("TX"), R("TG"))
+            cp(R("OFS"), R("TSS"))
+            send("ao%d" % t, [(nxt, R("OFS"), R(offn))], wide)
+            arrive("ao%d" % t, [R(offn)], wide)
         else:
             act(R("OT", npar, 1024, 2), tnp, ACT.Copy)
             act(R("OS", npar, 1024, 2), keep, ACT.Copy)
+        tt(R("SA"), ind(win, R("FU", 32 * par, 32 * par + 32)), own, ALU.max)
         tt(R("EQ"), ind(R("WW"), R("SBU")), R("IDN", 512 * par, 512 * par + 512), ALU.is_equal)
-        if not last:
-            cp(R("OFS"), ind(R("TX"), L2))
-            send("ao%d" % t, [(nxt, R("OFS"), R(offn))], wide)
-            arrive("ao%d" % t, [R(offn)], wide)
         conn = R("PA", 256, 288)
         for l in range(16):
             mm(conn, R("BZ", 15 - l, 143 - l), R("EQ", l, 512, 16), l == 0, l == 15)
-        tt(R("SA"), ind(win, R("FU", 32 * par, 32 * par + 32)), own, ALU.max)
-        tt(R("C1", 0, 32), conn, R("DC", 0, 32), ALU.mult)
-        tt(R("C1", 32, 64), conn, R("DC", 32, 64), ALU.mult)
         tr(R("FY", 0, 64), R("PB", 128, 192))
-        tt(R("C1", 64, 128), R("C1", 0, 64), R("SELFC", 64 * par, 64 * par + 64), ALU.add)
+        sd = [None, None]
+        sd[par], sd[npar] = done, keep
+        a = 32 * npar
         if last:
             for pp in range(2):
                 cp(R("FY", 64 + pp, 128, 2), R("FY", 32 * pp, 32 * pp + 32))
+            ts(R("HY"), R("FY", 64, 128), 4096.0, ALU.is_lt)
+            sel = [lambda: None] * 3
         else:
+            sel = row_select(a, a + 32, R("FY", a, a + 32), R("HY", a, a + 32))
             ts(R("HY"), R("FY", 0, 64), 4096.0, ALU.is_lt)
+        sel[0]()
+        tt(R("C1", 0, 32), conn, R("DC", 0, 32), ALU.mult)
+        tt(R("C1", 32, 64), conn, R("DC", 32, 64), ALU.mult)
+        sel[1]()
+        tt(R("C1", 64, 128), R("C1", 0, 64), R("SELFC", 64 * par, 64 * par + 64), ALU.add)
+        sel[2]()
         cp(R("CU"), R("C1", 64, 128))
-        sd = [None, None]
-        sd[par], sd[npar] = done, keep
         if not last:
+            lra = R("LR", 64 * t, 64 * t + 32)
+            send("ara%d" % t, [(nxt, R("RN", a, a + 32), lra)], wide)
+            arrive("ara%d" % t, [lra], wide)
             tt(done, ind(win, R("CU", 0, 32)), R("SA"), ALU.max)
             spread(done, par, swn, "ssss")
             if flip:
                 hand(R("OLDX", 32, 64), ln, "cpn%d" % t)
-
-            def row_list(t=t, offn=offn, fx=R("OLDX", 32, 64) if flip else ln):
-                cp(R("OLDX", 0, 32), R(offn, 32 * t, 32 * t + 32))
-                ts(R("X1", 0, 32), fx, 4096.0, ALU.is_lt)
-                tt(R("X1", 32, 64), fx, R("OLDX", 0, 32), ALU.subtract)
-                tt(R("X1", 64, 96), R("X1", 32, 64), R("X1", 0, 32), ALU.mult)
-                tt(R("X1", 0, 32), R("X1", 64, 96), R("OLDX", 0, 32), ALU.add)
-                cp(R(offn, 32 * t, 32 * t + 32), R("X1", 0, 32))
-            later2 = [row_list]
-            a = 32 * npar
-            row_select(a, a + 32, R("FY", a, a + 32), R("HY", a, a + 32))
-            lra = R("LR", 64 * t, 64 * t + 32)
-            send("ara%d" % t, [(nxt, R("RN", a, a + 32), lra)], wide)
-            arrive("ara%d" % t, [lra], wide)
             row_fix(tdn, npar, t, lra, "fxa%d" % t)
 
         tt(R("TD_"), ind(R(tw), R("CU", 32, 64)), tpar, ALU.subtract)
+        if last:
+            tt(done, ind(win, R("CU", 0, 32)), R("SA"), ALU.max)
         tt(R("TS"), R("ZN"), R("TD_"), ALU.mult)
         if not last:
             tt(R("TB"), R("TS"), tpar, ALU.add)
             dma(R("RY", 32 * par, 32 * par + 32), R("TB", 0, 512, 1, t, 128, 16), "ryb%d" % t)
             pass_on("ab%d" % t, R("TB"), R("LT", 1024 * t + 512, 1024 * t + 1024), R(tdn, 512 * par, 512 * par + 512), "cpb%d" % t)
+            a = 32 * par
+            sel = row_select(a, a + 32, R("FY", a, a + 32), R("HY", a, a + 32))
 
-            def rest(t=t, par=par, npar=npar, tdn=tdn, twn=twn):
-                a = 32 * par
-                row_select(a, a + 32, R("FY", a, a + 32), R("HY", a, a + 32))
+            def rest(t=t, par=par, npar=npar, tdn=tdn, twn=twn, a=a):
                 lrb = R("LR", 64 * t + 32, 64 * t + 64)
                 send("arb%d" % t, [(nxt, R("RN", a, a + 32), lrb)], wide)
                 arrive("arb%d" % t, [lrb], wide)
-                window(tdn, twn, npar, "twa%d" % (t + 1))
                 row_fix(tdn, par, t, lrb, "fxb%d" % t)
+                window(tdn, twn, npar, "twa%d" % (t + 1))
                 window(tdn, twn, par, "twb%d" % (t + 1))
-            later = [rest]
+
+            def row_list(t=t, offn=offn, fx=R("OLDX", 32, 64) if flip else ln):
+                lst, old = R(offn, 32 * t, 32 * t + 32), R("OLDX", 0, 32)
+                return [lambda: cp(old, lst), lambda: ts(R("X1", 0, 32), fx, 4096.0, ALU.is_lt),
+                        lambda: tt(R("X1", 32, 64), fx, old, ALU.subtract),
+                        lambda: tt(R("X1", 64, 96), R("X1", 32, 64), R("X1", 0, 32), ALU.mult),
+                        lambda: tt(old, R("X1", 64, 96), old, ALU.add), lambda: cp(lst, old)]
+            rl = row_list()
+            later = {1: rl[0:2], 2: [rl[2]], 3: [sel[0], rl[3], sel[1], rl[4], sel[2], rest], 4: [rl[5]]}
             continue
 
+        act(R("OS", par, 1024, 2), done, ACT.Copy)
         tt(R("OT", par, 1024, 2), R("TS"), tpar, ALU.add)
         dma(R("RY"), R("OT", 0, 1024, 1, t, 128, 16), "ryl", "s")
         dma(DR("oT"), R("OT"), "oT")
-        tt(done, ind(win, R("CU", 0, 32)), R("SA"), ALU.max)
-        cp(R("OS", par, 1024, 2), done)
         dma(DR("oS"), R("OS"), "oS", "s")
-        ts(R("HY"), R("FY", 64, 128), 4096.0, ALU.is_lt)
-        row_select(0, 64, R("FY", 64, 128), R("HY"))
-        exchange("aoT", "oT", "loT")
+        for fn in row_select(0, 64, R("FY", 64, 128), R("HY")):
+            fn()
         send("aRI", [(d, R("RN"), R("LRI", 64 * rank, 64 * rank + 64)) for d in others], 2 * w6)
         arrive("aRI", [R("LRI", 64 * d, 64 * d + 64) for d in others], 6 * w6)
+        exchange("aoT", "oT", "loT")
         exchange("aoS", "oS", "loS")
         for mine in (True, False):
             worlds = [gg for gg in range(8) if (gg % n == rank) == mine]

@@ -5,7 +5,7 @@ from concourse.mybir import AluOpType, ActivationFunctionType
 ALU = AluOpType
 ACT = ActivationFunctionType
 NV = 10
-NB = 13
+NB = 12
 RO = 4
 LG = math.log(1.40)
 LW0 = 124 * math.log(2.0)
@@ -161,6 +161,7 @@ def rank_program(g, core, T, topo):
     w6 = wide // 8
     others = [(rank + d) % n for d in range(1, n)]
     pieces = [(d, w) for d in others for w in range(2)]
+    spans = [x for x in ((0, rank), (rank + 1, rank + n), (rank + n + 1, 2 * n)) if x[0] < x[1]]
 
     def exchange(name, src, land):
         send(name, [(d, DR(src, d + n * w, d + n * w + 1), DR(land, rank + n * w, rank + n * w + 1)) for d, w in pieces], w6)
@@ -179,9 +180,10 @@ def rank_program(g, core, T, topo):
     def col(k):
         return R("CF", k, k + 1)
 
-    for be in range(2):
-        dma(DR("dT", 0, 8, 64 * be, 64 * be + 64), ("raw", T.tel[:, 512 * be:512 * be + 512]), "ldT")
-    dma(DR("dS"), ("raw", T.sec[:]), "ldS", "s")
+    for k0, k1 in spans:
+        for be in range(2):
+            dma(DR("dT", k0, k1, 64 * be, 64 * be + 64), ("raw", T.tel[16 * k0:16 * k1, 512 * be:512 * be + 512]), "ldT")
+        dma(DR("dS", k0, k1), ("raw", T.sec[16 * k0:16 * k1, :]), "ldS", "s")
     for w in range(2):
         gg = rank + n * w
         for be in range(2):
@@ -202,7 +204,6 @@ def rank_program(g, core, T, topo):
         for be in range(2):
             p0, c0 = 32 * (gg // 2) + 16 * be, 512 * (gg % 2)
             dma(R("TRA2", c0, c0 + 512, 1, p0, p0 + 16), DR("lT", gg, gg + 1, 64 * be, 64 * be + 64), "rawU")
-    dma(R("SRAW"), DR("lS"), "rawS")
     for be in range(2):
         dma(R("TRAW", 512 * be, 512 * be + 512), DR("lT", 0, 8, 64 * be, 64 * be + 64), "rawT")
 
@@ -275,6 +276,7 @@ def rank_program(g, core, T, topo):
     for par in range(2):
         act(R("SELFC", 64 * par, 64 * par + 32), R("IOF", 0, 32), ACT.Identity, col(CS2 if par else CS0), 32.0)
         act(R("SELFC", 64 * par + 32, 64 * par + 64), R("IOF", 0, 32), ACT.Identity, col(CS3 if par else CS1), 16.0)
+    dma(R("SRAW"), DR("lS"), "rawS", "s")
     tt(R("L0"), R("L0"), R("LS"), ALU.add)
     for rl in range(2):
         iota(R("CR", 256 * rl, 256 * rl + 128, p1=1), [[0, 8], [-256, 16]], 256 * 15 - 128)
@@ -327,19 +329,27 @@ def rank_program(g, core, T, topo):
             lw = 1 - w if flip else w
             dma(R(td, 512 * h, 512 * h + 512, 1, 64 * w + t, 64 * w + 64, 16), R(land[0], land[4], land[5], 1, 64 * lw, 64 * lw + 64), group)
 
+    eight = ["ZN", "PA", "PB", "TS", "D0", "D1", "K0", "K1"]
+    for k in range(8):
+        mm(R(eight[k]), R("SEL", 128 * (k // 2), 128 * (k // 2) + 128), R("SRAW", 512 * (k % 2), 512 * (k % 2) + 512), True, True)
     cp(R("TG"), ind(R("TRA2"), R("CL", 128, 160)))
     cp(R("SD0", 0, 512), R("SRAW", 0, 1024, 2))
-    cp(R("SD0", 512, 1024), R("SRAW", 1, 1024, 2))
     tr(R("TX"), R("TG"))
-    spread(R("SD0", 0, 512), 0, "SW0", "ssss")
+    cp(R("SW0", 512 * 7, 512 * 8), R(eight[7]))
     cp(R("OFF0"), ind(R("TX"), L2))
-    spread(R("SD0", 512, 1024), 1, "SW0", "vvsv")
+    cp(R("SW0", 512 * 5, 512 * 6), R(eight[5]))
+    for k in (6, 0, 1, 2, 3, 4):
+        act(R("SW0", 512 * k, 512 * k + 512), R(eight[k]), ACT.Copy)
     cp(R("TD0", 0, 512), R("TRAW", 0, 1024, 2))
-    cp(R("TD0", 512, 1024), R("TRAW", 1, 1024, 2))
     window("TD0", "TW0", 0, "twa0")
-    window("TD0", "TW0", 1, "twb0")
     sd = [R("SD0", 0, 512), R("SD0", 512, 1024)]
-    later = {}
+
+    def odd_halves():
+        cp(R("TD0", 512, 1024), R("TRAW", 1, 1024, 2))
+        cp(R("SD0", 512, 1024), R("SRAW", 1, 1024, 2))
+        window("TD0", "TW0", 1, "twb0")
+
+    later = {NV - 1: [odd_halves]}
 
     for t in range(RO):
         par, npar, last = t % 2, 1 - t % 2, t == RO - 1
@@ -413,8 +423,11 @@ def rank_program(g, core, T, topo):
         ts(R("NC"), R("KS", 15, 1024, 16), 4096.0, ALU.is_lt, 64.0, ALU.mult)
         ts(R("DG", 0, 64), R("II"), 1, sh, 48, an)
         ts(R("DG", 64, 128), R("II"), 31, an)
-        tt(R("CS"), R("DG", 0, 64), R("NC"), ALU.add)
         ts(R("DG", 192, 256), R("II"), 1, an)
+        ts(R("DG", 128, 192), R("II"), 1, sh, 15, an)
+        tt(R("CS"), R("DG", 0, 64), R("NC"), ALU.add)
+        ts(R("AB", 128, 192), R("DG", 192, 256), 32.0, ALU.mult)
+        tt(R("AB", 0, 56), R("DG", 0, 56), R("DG", 136, 192), ALU.add)
         tt(R("FB", 96, 224), ind(R("CS"), FL), R("STAB"), ALU.is_equal)
         cnt = R("PA", 0, 128)
         mm(cnt, R("L0"), R("FB", 96, 224), True, False)
@@ -426,27 +439,29 @@ def rank_program(g, core, T, topo):
                 for be in range(2):
                     c = 512 * npar + 256 * be
                     mm(R("TS", 256 * q0, 256 * q0 + 256), PM(q0, be, "IF" if nxt == 0 else "IZ"), R(td, c, c + 256), be == 0, be == 1)
+        tt(R("AB", 64, 120), R("DG", 64, 120), R("AB", 136, 192), ALU.add)
+        tt(R("EE", 0, 256), ind(R("DG"), R("CL", 64, 80)), R("EM", 0, 256), ALU.mult)
         for r in range(4):
             act(R("ZP", 128 * r, 128 * r + 128), kcol(r, 0, 128), ACT.Sign, 4095.5, -1.0)
         act(R("ZP"), R("ZP"), ACT.Relu)
-        ts(R("AB", 128, 192), R("DG", 192, 256), 32.0, ALU.mult)
-        ts(R("DG", 128, 192), R("II"), 1, sh, 15, an)
-        tt(R("AB", 64, 120), R("DG", 64, 120), R("AB", 136, 192), ALU.add)
-        tt(R("AB", 0, 56), R("DG", 0, 56), R("DG", 136, 192), ALU.add)
         byS = [(blk + 1) * NB // 16 != blk * NB // 16 for blk in range(16)]
-        tt(R("OK"), cnt, R("THR"), ALU.is_le)
-        tt(R("EE", 0, 256), ind(R("DG"), R("CL", 64, 80)), R("EM", 0, 256), ALU.mult)
-        scan(R("TH", 0, 128), R("RM4", 0, 128), R("OK"), ALU.mult, ALU.max)
-        tt(R("EE", 256, 512), ind(R("DG"), R("CL", 80, 96)), R("EM", 256, 512), ALU.mult)
-        tt(R("TH", 128, 160), R("TH", 3, 128, 4), R("WT", 0, 32), ALU.mult)
+        byV = [k for k in range(32) if not byS[k // 2]]
 
         def bcol(k):
             c = 64 + 16 * (k // 2 % 4) + 4 * (k % 2) + k // 8
             return R("AB", c, c + 1)
 
-        for k in range(32):
-            if not byS[k // 2]:
+        def onehot(ks):
+            for k in ks:
                 ts(R("BB", 64 * k, 64 * k + 64), R("IOT", 64, 128), bcol(k), ALU.is_equal)
+
+        tt(R("OK"), cnt, R("THR"), ALU.is_le)
+        onehot(byV[0:3])
+        scan(R("TH", 0, 128), R("RM4", 0, 128), R("OK"), ALU.mult, ALU.max)
+        onehot(byV[3:6])
+        tt(R("TH", 128, 160), R("TH", 3, 128, 4), R("WT", 0, 32), ALU.mult)
+        onehot(byV[6:])
+
         prev = None
         for blk in [b for b in range(16) if byS[b]] + [None]:
             if blk is not None:
@@ -455,13 +470,10 @@ def rank_program(g, core, T, topo):
             if prev is not None:
                 act(R("BB", 128 * prev, 128 * prev + 128), R("BX", 128 * prev, 128 * prev + 128), ACT.Relu, 1.0, -1.0)
             prev = blk
-        for dg in range(4):
-            mm(R("PB", 0, 96), R("EE", 128 * dg, 128 * dg + 128), R("RHS", 96 * dg, 96 * dg + 96), dg == 0, dg == 3)
-        for r in range(4):
-            mm(R("ZN", r, 512, 4), R("ZP", 128 * r, 128 * r + 128), R("IDB"), True, True)
         if not last:
             pass_on("aa%d" % t, tnp, R("LT", 1024 * t, 1024 * t + 512), R(tdn, 512 * npar, 512 * npar + 512), "cpa%d" % t)
-            dma(R("RY", 32 * npar, 32 * npar + 32), R(td, 512 * npar, 512 * npar + 512, 1, t, 128, 16), "rya%d" % t)
+            if t == 0:
+                dma(R("RY", 32 * npar, 32 * npar + 32), R(td, 512 * npar, 512 * npar + 512, 1, t, 128, 16), "rya%d" % t)
         for blk in range(16):
             q, r = blk // 4, blk % 4
             for w in range(2):
@@ -480,12 +492,19 @@ def rank_program(g, core, T, topo):
             act(R("TG"), ind(R("TSS"), L1), ACT.Copy)
         if t == 0:
             act(R("IDN"), R("IDN"), ACT.Identity, col(Q1K))
-        cp(R("SBU"), R("PB", 64, 96))
+        tt(R("EE", 256, 512), ind(R("DG"), R("CL", 80, 96)), R("EM", 256, 512), ALU.mult)
+        for dg in range(4):
+            mm(R("PB", 0, 96), R("EE", 128 * dg, 128 * dg + 128), R("RHS", 96 * dg, 96 * dg + 96), dg == 0, dg == 3)
+        for r in range(4):
+            mm(R("ZN", r, 512, 4), R("ZP", 128 * r, 128 * r + 128), R("IDB"), True, True)
         for h in range(2):
             scan(R("HS", 512 * h, 512 * h + 512), R("RM4"), R("D%d" % h), ALU.mult, ALU.max)
+        cp(R("SBU"), R("PB", 64, 96))
         tt(R("DC"), R("PB", 0, 64), R("SELFC", 64 * par, 64 * par + 64), ALU.subtract)
         for qq in range(1, 4):
             ts(R("ZQ", qq, 256, 4), R("HS", 4 * qq + 3, 1024, 16), 0.0, ALU.is_equal)
+        if not last:
+            tr(R("TX"), R("TG"))
         scan(R("H2"), R("ZQ"), R("HS", 3, 1024, 4), ALU.mult, ALU.add)
         scan(R("Q2"), R("ONES"), R("ZQ"), ALU.add, ALU.mult)
         hs = R("H2", 3, 256, 4)
@@ -494,20 +513,27 @@ def rank_program(g, core, T, topo):
         act(R("LL"), R("XY"), ACT.Ln, 1e-23)
         ts(R("QS", 64, 128), hs, 0.0, ALU.is_equal, -8192.0 * LG, ALU.mult)
         ts(R("QS", 0, 64), R("Q2", 3, 256, 4), -512.0 * LG, ALU.mult, -LW0 - 0.448 * LG, ALU.add)
-        if not last:
-            tr(R("TX"), R("TG"))
-            act(R("TSS"), ind(R("TX"), L2), ACT.Copy)
+
+        def ofs(a, b):
+            if not last:
+                cp(R("OFS", 16 * a, 16 * b), ind(R("TX"), R("CL", 32 + a, 32 + b)))
+
+        ofs(0, 8)
         tt(R("QS", 0, 64), R("QS", 0, 64), R("QS", 64, 128), ALU.add)
         tt(R("T1", 0, 64), R("LL", 0, 64), R("LL", 64, 128), ALU.add)
+        ofs(8, 16)
         tt(R("T1", 64, 128), R("T1", 0, 64), R("QS", 0, 64), ALU.add)
-        ts(R("T1", 128, 192), R("T1", 64, 128), -1.0 / LG, ALU.mult, 2048.0, ALU.min)
-        cp(R("ID"), R("T1", 128, 192))
-        ts(R("FU"), R("ID"), 2.0, ALU.mult, float(par), ALU.add)
+        ofs(16, 24)
+        ts(R("ID"), R("T1", 64, 128), -1.0 / LG, ALU.mult, 2048.0, ALU.min)
+        ofs(24, 32)
         ts(R("FF"), R("ID"), 2.0, ALU.mult, float(par), ALU.add)
+        ts(R("FU"), R("ID"), 2.0, ALU.mult, float(par), ALU.add)
         for s in range(4):
             mm(R("PA", 64 * s, 64 * s + 64), R("SELF", 128 * s, 128 * s + 128), R("FF"), True, True)
         act(R("WW"), R("PA", 0, 256), ACT.Copy)
         if not last:
+            send("ao%d" % t, [(nxt, R("OFS"), R(offn))], wide)
+            arrive("ao%d" % t, [R(offn)], wide)
             ln = R("LN", 32 * t, 32 * t + 32)
             send("an%d" % t, [(nxt, R("FF", 32 * npar, 32 * npar + 32), ln)], wide)
             arrive("an%d" % t, [ln], wide)
@@ -519,29 +545,31 @@ def rank_program(g, core, T, topo):
 
         keep = R("SD0", 512 * npar, 512 * npar + 512) if sd[npar][0] != "SD0" else R("SB%d" % npar)
         done = R("SD0", 512 * par, 512 * par + 512) if own[0] != "SD0" else R("SB%d" % par)
+
+        def called(h):
+            tt(R("SA", 256 * h, 256 * h + 256), ind(win, R("FU", 32 * par + 16 * h, 32 * par + 16 * h + 16)),
+               R(own[0], own[4] + 256 * h, own[4] + 256 * h + 256), ALU.max)
+
         tt(keep, ind(win, R("FU", 32 * npar, 32 * npar + 32)), sd[npar], ALU.max)
-        if not last:
-            spread(keep, npar, swn, "ssss")
-            cp(R("OFS"), R("TSS"))
-            send("ao%d" % t, [(nxt, R("OFS"), R(offn))], wide)
-            arrive("ao%d" % t, [R(offn)], wide)
-        else:
+        if last:
             act(R("OT", npar, 1024, 2), tnp, ACT.Copy)
             act(R("OS", npar, 1024, 2), keep, ACT.Copy)
-        tt(R("SA"), ind(win, R("FU", 32 * par, 32 * par + 32)), own, ALU.max)
+        else:
+            called(0)
         tt(R("EQ"), ind(R("WW"), R("SBU")), R("IDN", 512 * par, 512 * par + 512), ALU.is_equal)
         conn = R("PA", 256, 288)
         for l in range(16):
             mm(conn, R("BZ", 15 - l, 143 - l), R("EQ", l, 512, 16), l == 0, l == 15)
+        if not last:
+            spread(keep, npar, swn, "ssss")
         tr(R("FY", 0, 64), R("PB", 128, 192))
+        called(0 if last else 1)
         sd = [None, None]
         sd[par], sd[npar] = done, keep
         a = 32 * npar
         if last:
-            for pp in range(2):
-                cp(R("FY", 64 + pp, 128, 2), R("FY", 32 * pp, 32 * pp + 32))
-            ts(R("HY"), R("FY", 64, 128), 4096.0, ALU.is_lt)
-            sel = [lambda: None] * 3
+            sel = [lambda: cp(R("FY", 64, 128, 2), R("FY", 0, 32)), lambda: cp(R("FY", 65, 128, 2), R("FY", 32, 64)),
+                   lambda: called(1)]
         else:
             sel = row_select(a, a + 32, R("FY", a, a + 32), R("HY", a, a + 32))
             ts(R("HY"), R("FY", 0, 64), 4096.0, ALU.is_lt)
@@ -557,16 +585,21 @@ def rank_program(g, core, T, topo):
             send("ara%d" % t, [(nxt, R("RN", a, a + 32), lra)], wide)
             arrive("ara%d" % t, [lra], wide)
             tt(done, ind(win, R("CU", 0, 32)), R("SA"), ALU.max)
-            spread(done, par, swn, "ssss")
             if flip:
                 hand(R("OLDX", 32, 64), ln, "cpn%d" % t)
             row_fix(tdn, npar, t, lra, "fxa%d" % t)
+        else:
+            ts(R("HY"), R("FY", 64, 128), 4096.0, ALU.is_lt)
 
         tt(R("TD_"), ind(R(tw), R("CU", 32, 64)), tpar, ALU.subtract)
         if last:
             tt(done, ind(win, R("CU", 0, 32)), R("SA"), ALU.max)
+        else:
+            spread(done, par, swn, "vsss")
         tt(R("TS"), R("ZN"), R("TD_"), ALU.mult)
         if not last:
+            lst, old, fx = R(offn, 32 * t, 32 * t + 32), R("OLDX", 0, 32), R("OLDX", 32, 64) if flip else ln
+            cp(old, lst)
             tt(R("TB"), R("TS"), tpar, ALU.add)
             dma(R("RY", 32 * par, 32 * par + 32), R("TB", 0, 512, 1, t, 128, 16), "ryb%d" % t)
             pass_on("ab%d" % t, R("TB"), R("LT", 1024 * t + 512, 1024 * t + 1024), R(tdn, 512 * par, 512 * par + 512), "cpb%d" % t)
@@ -578,32 +611,39 @@ def rank_program(g, core, T, topo):
                 send("arb%d" % t, [(nxt, R("RN", a, a + 32), lrb)], wide)
                 arrive("arb%d" % t, [lrb], wide)
                 row_fix(tdn, par, t, lrb, "fxb%d" % t)
+                if t + 2 < RO:
+                    dma(R("RY", a, a + 32), R(tdn, 512 * par, 512 * par + 512, 1, t + 1, 128, 16), "rya%d" % (t + 1))
                 window(tdn, twn, npar, "twa%d" % (t + 1))
                 window(tdn, twn, par, "twb%d" % (t + 1))
 
-            def row_list(t=t, offn=offn, fx=R("OLDX", 32, 64) if flip else ln):
-                lst, old = R(offn, 32 * t, 32 * t + 32), R("OLDX", 0, 32)
-                return [lambda: cp(old, lst), lambda: ts(R("X1", 0, 32), fx, 4096.0, ALU.is_lt),
+            def row_list(lst=lst, old=old, fx=fx):
+                return [lambda: ts(R("X1", 0, 32), fx, 4096.0, ALU.is_lt),
                         lambda: tt(R("X1", 32, 64), fx, old, ALU.subtract),
                         lambda: tt(R("X1", 64, 96), R("X1", 32, 64), R("X1", 0, 32), ALU.mult),
                         lambda: tt(old, R("X1", 64, 96), old, ALU.add), lambda: cp(lst, old)]
             rl = row_list()
-            later = {1: rl[0:2], 2: [rl[2]], 3: [sel[0], rl[3], sel[1], rl[4], sel[2], rest], 4: [rl[5]]}
+            later = {0: rl[0:2], 2: [rl[2]], 3: [rl[3], sel[0]], 4: [rl[4], sel[1]], 5: [sel[2], rest]}
             continue
 
         act(R("OS", par, 1024, 2), done, ACT.Copy)
+        for k0, k1 in spans:
+            dma(DR("oS", k0, k1), R("OS", 0, 1024, 1, 16 * k0, 16 * k1), "oS", "s")
         tt(R("OT", par, 1024, 2), R("TS"), tpar, ALU.add)
         dma(R("RY"), R("OT", 0, 1024, 1, t, 128, 16), "ryl", "s")
-        dma(DR("oT"), R("OT"), "oT")
-        dma(DR("oS"), R("OS"), "oS", "s")
+        for k0, k1 in spans:
+            dma(DR("oT", k0, k1), R("OT", 0, 1024, 1, 16 * k0, 16 * k1), "oT")
         for fn in row_select(0, 64, R("FY", 64, 128), R("HY")):
             fn()
+        exchange("aoS", "oS", "loS")
+        exchange("aoT", "oT", "loT")
         send("aRI", [(d, R("RN"), R("LRI", 64 * rank, 64 * rank + 64)) for d in others], 2 * w6)
         arrive("aRI", [R("LRI", 64 * d, 64 * d + 64) for d in others], 6 * w6)
-        exchange("aoT", "oT", "loT")
-        exchange("aoS", "oS", "loS")
         for mine in (True, False):
             worlds = [gg for gg in range(8) if (gg % n == rank) == mine]
+            for gg in worlds:
+                p0 = 64 * (gg // n) + 16 * rank
+                a = R("OS", 0, 1024, 1, p0, p0 + 16) if mine else DR("loS", gg, gg + 1)
+                dma(("raw", T.ysec[16 * gg:16 * gg + 16, :]), a, "out", "y")
             for gg in worlds:
                 p0 = 64 * (gg // n) + 16 * rank
                 a = R("OT", 0, 1024, 1, p0 + t + 1, p0 + 16) if mine else DR("loT", gg, gg + 1, 8 * t + 8, 128)
@@ -614,8 +654,6 @@ def rank_program(g, core, T, topo):
                 p0 = 64 * (gg // n) + 16 * rank
                 c = R("RN", 0, 64, 1, p0, p0 + 16) if mine else R("LRI", 64 * (gg % n), 64 * (gg % n) + 64, 1, p0, p0 + 16)
                 dma(("raw", T.ytel[16 * gg + t:16 * gg + t + 1, :]), c, "out", "s")
-                a = R("OS", 0, 1024, 1, p0, p0 + 16) if mine else DR("loS", gg, gg + 1)
-                dma(("raw", T.ysec[16 * gg:16 * gg + 16, :]), a, "out", "y")
 
     emit(ops, Q, T, g)
 

@@ -1,6 +1,6 @@
 import math
 from concourse.bass import DstId, RemoteDMATransfer
-from concourse.mybir import AluOpType, ActivationFunctionType
+from concourse.mybir import AluOpType, AxisListType, ActivationFunctionType
 
 ALU = AluOpType
 ACT = ActivationFunctionType
@@ -9,6 +9,7 @@ NB = 12
 RO = 4
 LG = math.log(1.40)
 LW0 = 124 * math.log(2.0)
+EVEN = 1.5 * 2.0 ** 24
 
 F, B, I, U = "float32", "bfloat16", "int32", "uint16"
 SCRATCH = {}
@@ -20,22 +21,22 @@ def _decl(where, dtype, **kw):
 
 
 _decl("psum", F, K0=512, K1=512, D0=512, D1=512, ZN=512, PA=512, PB=512, TS=512)
-_decl("dram", I, dT=[8, 128, 128], lT=[8, 128, 128])
-_decl("dram", B, dS=[8, 128, 128], lS=[8, 128, 128], oS=[8, 128, 128], loS=[8, 128, 128])
-_decl("dram", F, oT=[8, 128, 128], loT=[8, 128, 128])
-_decl("sbuf", I, CI=16, TRAW=1024, TRA2=1024, II=64, DG=256, NC=64, ID=64)
-_decl("sbuf", U, OFF0=512, OFF1=512, OFF2=512, OFF3=512, OFS=512, CL=160, FU=64, SBU=32, CU=64)
-_decl("sbuf", B, SRAW=1024, SW0=4112, SW1=4112, SA=512, SB0=512, SB1=512, SD0=1024, M=8192, G0=512, G1=512, HI=512, IOT=192,
-      IDB=128, NEG=128, HIR=256, SEL=512, SUMR=16, OWNR=256, CR=512, ONE1=128, RM16=512, RM4=512, ONES=256, LS=128, LI=128,
-      L0=128, FB=320, EM=512, RHS=416, BZ=144, AA=4096, BB=2048, BX=2048, EE=512, ZP=512, EQ=512, OS=1024, TMPB=256)
-_decl("sbuf", F, CF=32, TD0=1024, TD1=1024, TD2=1024, TD3=1024, TW0=4096, TW1=4096, LT=3072, LR=192, LN=96, IOF=160, IDF=128,
-      SELF=512, IZ0=160, IZ1=160, IF0=160, IF1=160, WT=64, THR=128, STAB=128, SELFC=128, IDN=1024, KS=1024, CS=64, AB=192, OK=128,
-      TH=160, HS=1024, ZQ=256, H2=256, Q2=256, XY=128, LL=128, QS=128, T1=192, FF=64, WW=256, DC=64, C1=128, TSS=512, TG=512,
-      TX=512, OLDX=64, X1=96, FY=128, HY=64, RY=64, Y1=128, RN=64, TD_=512, TB=512, OT=1024, LRI=256, TMPF=256)
+_decl("dram", B, oS=[8, 128, 128], loS=[8, 128, 128])
+_decl("dram", F, oT0=[8, 128, 64], loT0=[8, 128, 64], oT1=[8, 128, 64], loT1=[8, 128, 64])
+_decl("sbuf", I, CI=16, TL=1024, II=64, DG=320)
+_decl("sbuf", U, OFF0=512, OFF1=512, OFF2=512, OFF3=512, OFS=512, CL=160, FU=64, CU=96)
+_decl("sbuf", B, SL=1024, SR=1024, SW0=4112, SW1=4112, SD=1024, M=8192, G0=512, G1=512, GC=512, HI=512, IOT=192,
+      IDB=128, NEG=128, HIR=256, SEL=512, SE0=512, SUMR=16, OWNR=256, CR=512, RM16=512, RM4=128, ONES=512, LS=128, LI=128,
+      L0=128, FB=320, EM=256, RHS=416, BO=128, BO2=128, AA=4096, BB=2048, BX=2048, EE=512, ZP=512, EQ=512, MK=512, TMPB=128,
+      THR=256, TINY=64, CB=32, CZ=512, NT=512)
+_decl("sbuf", F, CF=48, TE=1024, TR=1024, TD0=1024, TD1=1024, TD2=1024, TD3=1024, TW0=4096, TW1=4096, LT=3072, ONEF=128, IDF=128,
+      NEF=128, SELF=512, IZ0=160, IZ1=160, IF0=160, IF1=160, WT=384, STAB=128, IDN=512, KS=1024, AB=192, OK=128,
+      TH=128, HS=256, ZQ=256, H2=256, Q2=256, XY=128, LQ=256, RMQ=256, T1=256, FF=64, WW=256, TG=512,
+      TX=512, X1=96, FY=64, RY=64, Y1=128, RN=64, DD=512, TB=512, OT=1024, TMPF=256)
 
-_DMA_GROUPS = ["ldT", "ldS", "own", "rawT", "rawU", "rawS", "oS", "oT", "out", "ryl"] + ["%s%d" % (n, t) for t in range(3) for n in
-              ("rya", "ryb", "cpa", "cpb", "fxa", "fxb", "cpn")] + ["tw%s%d" % (h, t) for t in range(4) for h in "ab"]
-_ARRIVE = ["aT", "aS", "aoS", "aoT", "aRI"] + ["%s%d" % (n, t) for t in range(3) for n in ("aa", "ab", "ara", "arb", "ao", "an")]
+_DMA_GROUPS = ["ldT", "ldS", "ownT", "ownS", "rawT0", "rawT1", "rawS", "oS", "oT0", "oT1", "out"] + ["%s%d" % (n, t) for t in range(3) for n in
+              ("cpa", "cpb")] + ["%s%d" % (n, t) for t in range(4) for n in ("twa", "twb", "ry", "cz", "fxa", "fxb")]
+_ARRIVE = ["aT0", "aT1", "aS", "aoS", "aoT0", "aoT1"] + ["%s%d" % (n, t) for t in range(3) for n in ("aa", "ab", "ao")]
 SEMAPHORES = ["ev", "es", "ep", "eg"] + _DMA_GROUPS + _ARRIVE + ["s" + n for n in _ARRIVE]
 ENGSEM = {"v": "ev", "s": "es", "p": "ep", "g": "eg"}
 
@@ -53,7 +54,7 @@ def DR(name, k0=0, k1=8, r0=0, r1=128):
 def _touch(a, b):
     if SCRATCH[a[0]][0] == "psum":
         return True
-    if a[6] == b[6] > 1 and (a[4] - b[4]) % a[6]:
+    if a[6] == b[6] > 1 and (a[4] - b[4]) % a[6] or a[3] == b[3] > 1 and (a[1] - b[1]) % a[3]:
         return False
     return a[1] < b[2] and b[1] < a[2] and a[4] < b[5] and b[4] < a[5]
 
@@ -112,8 +113,11 @@ def rank_program(g, core, T, topo):
     def ms(o, val):
         add("v", lambda: g.vector.memset(ap(o), val), [o], [])
 
-    def scan(o, d0, d1, op0, op1):
-        add("v", lambda: g.vector.tensor_tensor_scan(ap(o), ap(d0), ap(d1), 0.0, op0, op1), [o], [d0, d1])
+    def scan(o, d0, d1, op0, op1, first=0.0):
+        add("v", lambda: g.vector.tensor_tensor_scan(ap(o), ap(d0), ap(d1), ap(first), op0, op1), [o], [d0, d1, first])
+
+    def total(o, a):
+        add("v", lambda: g.vector.tensor_reduce(ap(o), ap(a), AxisListType.X, ALU.add), [o], [a])
 
     def tr(o, a):
         add("v", lambda: g.vector.transpose(ap(o), ap(a)), [o], [a])
@@ -137,20 +141,26 @@ def rank_program(g, core, T, topo):
         else:
             add("g", lambda: g.iota(ap(o), pat, base, cm, allow_small_or_imprecise_dtypes=True), [o], [])
 
+    def pick(o, a, pat, op, base=0, cm=1, fill=0.0):
+        add("g", lambda: g.affine_select(ap(o), ap(a), pat, op, fill, base, cm), [o], [a])
+
     def dma(o, a, group, q="y"):
         add(q, lambda: Q[q].dma_start(ap(o), ap(a)), [o], [a], group, 16)
 
-    def send(name, items, width):
+    def send(name, items, width, after=()):
+        srcs = [x[1] if isinstance(x[1], list) else [x[1]] for x in items]
+
         def fn():
             trs = []
-            for k, (d, src, dst) in enumerate(items):
+            for k, (d, _, dst) in enumerate(items):
                 eng = topo.engines(core, cores[d])[k * width:(k + 1) * width]
                 rid, pid, _ = topo.addr(cores[d])
                 trs.append(RemoteDMATransfer(dst_ids=[DstId(rid=rid, pnc=pid)], dma_engine_mask=sum(1 << e for e in eng),
-                                             remote_sem=T.sem[name], src=ap(src), dst=ap(dst)))
+                                             remote_sem=T.sem[name], srcs=[ap(x) for x in srcs[k]], dsts=[ap(dst)],
+                                             alu_op=1 if len(srcs[k]) > 1 else 0))
             g.remote_dma_fused(trs, local_sem=T.sem["s" + name])
             return None
-        add("g", fn, [], [x[1] for x in items], "s" + name, width * len(items))
+        add("g", fn, [], sum(srcs, list(after)), "s" + name, width * len(items))
 
     def arrive(name, lands, count):
         add("x", None, lands, [], name, count)
@@ -171,8 +181,8 @@ def rank_program(g, core, T, topo):
         for w in range(2):
             dma(R(o[0], o[4], o[5], 1, 64 * w, 64 * w + 64), R(a[0], a[4], a[5], 1, 64 - 64 * w, 128 - 64 * w), group)
 
-    def pass_on(name, src, land, final, group):
-        send(name, [(nxt, src, land if nxt == 0 else final)], wide)
+    def pass_on(name, src, land, final, group, after=()):
+        send(name, [(nxt, src, land if nxt == 0 else final)], wide, after)
         arrive(name, [land if flip else final], wide)
         if flip:
             hand(final, land, group)
@@ -180,136 +190,155 @@ def rank_program(g, core, T, topo):
     def col(k):
         return R("CF", k, k + 1)
 
-    for k0, k1 in spans:
-        for be in range(2):
-            dma(DR("dT", k0, k1, 64 * be, 64 * be + 64), ("raw", T.tel[16 * k0:16 * k1, 512 * be:512 * be + 512]), "ldT")
-        dma(DR("dS", k0, k1), ("raw", T.sec[16 * k0:16 * k1, :]), "ldS", "s")
+    def quarters(nm, c, width, w):
+        return R(nm, c, c + width, 1, 64 * w, 64 * w + 64)
+
+    def rows(src, d, w):
+        return ("raw", src[16 * (d + n * w):16 * (d + n * w) + 16, :])
+
+    for src, out, nm in ((T.sec, "SL", "ldS"), (T.tel, "TL", "ldT")):
+        for k, (d, w) in enumerate(pieces):
+            dma(quarters(out, 256 * (k // 2), 256, w), rows(src, d, w), nm, "ys"[k % 2])
     for w in range(2):
-        gg = rank + n * w
-        for be in range(2):
-            dma(DR("lT", gg, gg + 1, 64 * be, 64 * be + 64), ("raw", T.tel[16 * gg:16 * gg + 16, 512 * be:512 * be + 512]), "own")
-        dma(DR("lS", gg, gg + 1), ("raw", T.sec[16 * gg:16 * gg + 16, :]), "own", "s")
-    P15, PG, PW, PQ, B4, P3, PH, PP, SK, MQ, NB4, P2, Z15, P16, C32, Q1K, CS0, CS1, P316, CS2, CS3 = (
-        0, 1, 2, 3, 4, 5, 6, 7, 8, 9, 13, 14, 15, 16, 17, 18, 19, 20, 21, 24, 25)
+        dma(quarters("SR", 256 * rank, 256, w), rows(T.sec, rank, w), "ownS", "ys"[w])
+        dma(quarters("TL", 768, 256, w), rows(T.tel, rank, w), "ownT", "ys"[w])
+    P15, PG, PQ, P3, PH, P2, P7, B3, C32, P316, LC, WP, Q1K, LNC, W0, RT = 0, 1, 2, 3, 4, 5, 6, 7, 8, 9, 10, 11, 12, 14, 16, 18
+    EQ0, NE0 = ALU.is_equal, ALU.not_equal
+    one, onef = R("ONES", 0, 128), R("ONEF")
+    ms(R("ONES"), 1.0)
+    ms(onef, 1.0)
     iota(R("CI", 8, 9), [[0, 1]], 0, 1)
-    iota(R("IOF"), [[1, 160]])
-    iota(R("IOT"), [[1, 192]], -64)
-    iota(R("TMPF", 0, 128), [[16, 2], [0, 4], [1, 16]])
-    iota(R("TMPF", 128, 160), [[16, 16], [256, 2]])
-    iota(R("TMPF", 160, 192), [[1, 16], [16, 2]])
-    iota(R("TMPB"), [[0, 2], [1, 8], [0, 16]])
-    exchange("aT", "dT", "lT")
-    exchange("aS", "dS", "lS")
-    for gg in range(8):
-        for be in range(2):
-            p0, c0 = 32 * (gg // 2) + 16 * be, 512 * (gg % 2)
-            dma(R("TRA2", c0, c0 + 512, 1, p0, p0 + 16), DR("lT", gg, gg + 1, 64 * be, 64 * be + 64), "rawU")
-    for be in range(2):
-        dma(R("TRAW", 512 * be, 512 * be + 512), DR("lT", 0, 8, 64 * be, 64 * be + 64), "rawT")
+    iota(R("TMPF", 0, 32), [[256, 2], [16, 8], [128, 2]])
+    iota(R("TMPF", 32, 64), [[256, 2], [4, 8], [2, 2]])
+    pick(R("IDB"), one, [[-1, 128]], EQ0)
+    for c in range(2):
+        pick(R("SE0", 128 * c, 128 * c + 128), one, [[-64, 2], [0, 4], [-4, 16]], EQ0, -c)
+
+    def hand_out(nm, out, land, c, width):
+        send(nm, [(d, R(out, c + width * k, c + width * k + width), R(land, c + width * rank, c + width * rank + width))
+                  for k, d in enumerate(others)], 2 * w6)
+        arrive(nm, [R(land, c + width * d, c + width * d + width) for d in others], 6 * w6)
+
+    def by_groups(out, c, land, lc, width, nm):
+        for w in range(2):
+            for q in range(n):
+                dma(R(out, c, c + 4 * width, 1, 64 * w + 16 * q, 64 * w + 16 * q + 16), quarters(land, lc + width * q, width, w), nm)
+
+    def entries(h):
+        cp(R("TE", 512 * h, 512 * h + 384), R("TL", h, 768, 2))
+        cp(R("TR", 512 * h + 128 * rank, 512 * h + 128 * rank + 128), R("TL", 768 + h, 1024, 2))
+
+    hand_out("aS", "SL", "SR", 0, 256)
+    for c in range(2, 4):
+        pick(R("SE0", 128 * c, 128 * c + 128), one, [[-64, 2], [0, 4], [-4, 16]], EQ0, -c)
+    iota(R("TMPF", 64, 96), [[1, 32]])
+    iota(R("TMPB"), [[1, 8], [0, 16]])
 
     pc = R("CI", 8, 9)
     sh, an = ALU.arith_shift_right, ALU.bitwise_and
-    I128 = R("IOT", 64, 192)
-    ms(R("CR", p1=33), 0.0)
-    for k, a, b in ((P15, 0, 15), (PG, 4, 7), (PW, 6, 1), (PQ, 4, 3), (B4, 4, 1), (P3, 0, 3), (PH, 2, 31), (PP, 0, 127), (9, 2, 3)):
+    L1, L2, EL, FL, L3 = R("CL", 0, 32), R("CL", 32, 64), R("CL", 64, 96), R("CL", 96, 104), R("CL", 128, 160)
+    ms(col(W0), 2.0 ** 62)
+    for k, a, b in ((P15, 0, 15), (PG, 4, 7), (PQ, 4, 3), (P3, 0, 3), (PH, 2, 31), (P2, 2, 3), (P7, 0, 7), (B3, 3, 1)):
         ts(R("CI", k, k + 1), pc, a, sh, b, an)
-    ms(R("ONE1", p1=33), 1.0)
+    act(col(LNC + 1), col(W0), ACT.Ln)
+    ms(R("WT", 0, 128), math.exp(-4 * LG))
+    ms(R("WT", 128, 256), 0.0)
     cp(R("CF", 0, 8), R("CI", 0, 8))
-    cp(col(P2), R("CI", 9, 10))
+    ts(col(W0 + 1), col(W0), 2.0 ** 62 * math.exp(4 * LG), ALU.mult)
+    ms(R("CR", p1=33), 0.0)
+    ts(col(C32), col(P15), 32.0, ALU.mult)
+    ts(col(P316), col(P3), 16.0, ALU.mult)
+    for par in range(2):
+        ts(col(Q1K + par), col(PQ), -1024.0, ALU.mult, -float(par), ALU.add)
+    ts(col(LC), col(P7), 32.0, ALU.mult, col(B3), ALU.add)
+    for t in range(RO):
+        ts(col(RT + t), col(P15), float(t), ALU.is_equal)
+    scan(R("WT", 256, 384), R("WT", 0, 128), R("WT", 128, 256), ALU.mult, ALU.add, col(W0 + 1))
     for rl in range(2):
         ms(R("CR", 256 * rl, 256 * rl + 128, 1, 32, 33), -1.0)
         ms(R("CR", 256 * rl + 128, 256 * rl + 256, 1, 32, 33), 32.0)
-    ts(col(SK), col(PW), 16.0, ALU.mult, col(P15), ALU.add)
-    for s in range(4):
-        ts(col(MQ + s), col(PQ), float(s), ALU.is_equal)
-    ts(col(NB4), col(B4), 0.0, ALU.is_equal)
-    ts(col(P16), col(PP), 16.0, ALU.add)
-    ts(col(C32), col(P15), 32.0, ALU.mult)
-    ts(col(22), col(PW), -128.0, ALU.mult, 64.0, ALU.add)
-    ts(col(P316), col(P3), 16.0, ALU.mult)
-    ts(col(Z15), col(PG), 16.0, ALU.mult, 15.0, ALU.add)
-    ts(col(Q1K), col(PQ), 1024.0, ALU.mult)
-    ts(R("IDB"), I128, col(PP), ALU.is_equal)
-    ts(col(23), col(22), col(P16), ALU.add)
-    ts(col(CS1), col(Q1K), col(P15), ALU.add)
-    ts(R("IZ0"), R("IOF"), col(P16), ALU.is_equal, col(NB4), ALU.mult)
-    ts(R("IZ1"), R("IOF"), col(P16), ALU.is_equal, col(B4), ALU.mult)
-    ts(col(CS0), col(CS1), col(P15), ALU.add)
-    ts(col(CS3), col(CS1), 512.0, ALU.add)
-    for s in range(4):
-        ts(R("SEL", 128 * s, 128 * s + 128), R("TMPF", 0, 128), col(SK), ALU.is_equal, col(MQ + s), ALU.mult)
-    ts(col(CS2), col(CS0), 1.0, ALU.add)
-    L1, L2, EL, FL = R("CL", 0, 32), R("CL", 32, 64), R("CL", 64, 96), R("CL", 96, 104)
-    ts(L1, R("TMPF", 128, 160), col(P15), ALU.add)
-    ts(R("CL", 128, 160), R("TMPF", 128, 160), col(P15), ALU.add, 2.0, ALU.mult)
-    ts(L2, R("TMPF", 160, 192), col(C32), ALU.add)
-    ts(R("RHS", 384, 416), R("IOT", 64, 96), col(PH), ALU.is_equal)
+    ts(L1, R("TMPF", 0, 32), col(P15), ALU.add)
+    ts(L3, R("TMPF", 32, 64), col(LC), ALU.add)
+    tt(R("WT", 0, 128), R("WT", 256, 384), R("IDB"), ALU.mult)
     ms(R("SW0", 4096, 4112), 0.0)
     ms(R("SW1", 4096, 4112), 0.0)
-    ts(R("SUMR"), R("TMPB", 0, 256, 16), col(PG), ALU.is_equal, 4096.0, ALU.mult)
-    ts(R("OWNR"), R("TMPB"), col(PG), ALU.is_equal, -4096.0, ALU.mult)
-    ms(R("RM16"), 1.0)
-    ms(R("RM4"), 1.0)
-    for i in range(NV, 16):
-        ms(R("OWNR", i, 256, 16), 0.0)
-    ms(R("RM16", 0, 512, 16), 0.0)
-    ms(R("RM4", 0, 512, 4), 0.0)
-    ms(R("ONES"), 1.0)
-    ms(R("ZQ", 0, 256, 4), 0.0)
-    ms(R("FB", 0, 96), 0.0)
-    ms(R("FB", 224, 320), 0.0)
-    ts(R("LS"), I128, col(PP), ALU.is_gt)
-    ts(R("LI"), I128, col(PP), ALU.is_ge)
-    ts(R("BZ"), R("IOF", 0, 144), col(Z15), ALU.is_equal)
-    if nxt == 0:
-        ts(R("IF0"), R("IOF"), col(23), ALU.is_equal, col(NB4), ALU.mult)
-        ts(R("IF1"), R("IOF"), col(23), ALU.is_equal, col(B4), ALU.mult)
-    act(R("NEG"), R("IDB"), ACT.Copy, None, -1.0)
-    act(R("IDF"), R("IDB"), ACT.Copy)
-    act(R("HIR", 0, 128), R("IDB"), ACT.Copy)
-    act(R("HIR", 128, 256), R("IDB"), ACT.Copy, None, -32.0)
-    act(R("L0"), R("IDB"), ACT.Copy, None, -1024.0)
-    act(R("SELF"), R("SEL"), ACT.Copy)
+    total(col(WP), R("WT", 0, 128))
+    ms(R("TINY", p1=1), math.exp(LW0 - 512 * LG))
+    ms(R("THR", 128, 256, p1=1), -960.0)
+    ts(col(LNC), col(LNC + 1), -2.0, ALU.mult, -0.448 * LG, ALU.add)
+    for h in range(2):
+        entries(h)
+        hand_out("aT%d" % h, "TE", "TR", 512 * h, 128)
+    by_groups("SD", 0, "SR", 0, 256, "rawS")
+    for h in range(2):
+        by_groups("TD0", 512 * h, "TR", 512 * h, 128, "rawT%d" % h)
+    iota(R("EM"), [[0, 16], [1, 4], [0, 4]])
+    iota(R("TMPF", 96, 104), [[16, 4], [4, 2]])
+    iota(R("TMPF", 104, 136), [[136, 2], [64, 2], [1, 8]])
+    ts(R("LQ", 0, 256, 4), R("ONEF", 0, 64), col(LNC), ALU.mult)
+    ts(L2, R("TMPF", 64, 96), col(C32), ALU.add)
+    ts(R("RHS", 384, 416), R("TMPF", 64, 96), col(PH), ALU.is_equal)
+    ts(R("BO"), R("TMPB"), col(PG), ALU.is_equal)
+    for k, val in enumerate((0.0, 1.0, 1.0, -2.0 / LG)):
+        ms(R("RMQ", k, 256, 4), val)
+    ms(R("CZ"), 0.0)
+    for o, sc in ((R("NEG"), -1.0), (R("IDF"), 1.0), (R("HIR", 0, 128), 1.0), (R("HIR", 128, 256), -32.0), (R("NEF"), -1.0)):
+        act(o, R("IDB"), ACT.Copy, None, sc)
+    for t in range(RO):
+        act(R("NT", 128 * t, 128 * t + 128), R("NEG"), ACT.Copy, None, col(RT + t))
+    for k in range(2):
+        act(R("OWNR", 128 * k, 128 * k + 128), R("BO"), ACT.Copy, None, -4096.0)
+        act(R("SUMR", 8 * k, 8 * k + 8), R("BO", 0, 128, 16), ACT.Copy, None, 4096.0)
+    act(R("BO2"), R("BO"), ACT.Copy, None, 256.0)
     for dg, sc in enumerate(((64, 64, 4), (32, 16, 1), (2, 1, 0), (1, 512, 32))):
         for k in range(3):
             act(R("RHS", 96 * dg + 32 * k, 96 * dg + 32 * k + 32), R("RHS", 384, 416), ACT.Copy, None, float(sc[k]))
-    for par in range(2):
-        act(R("SELFC", 64 * par, 64 * par + 32), R("IOF", 0, 32), ACT.Identity, col(CS2 if par else CS0), 32.0)
-        act(R("SELFC", 64 * par + 32, 64 * par + 64), R("IOF", 0, 32), ACT.Identity, col(CS3 if par else CS1), 16.0)
-    dma(R("SRAW"), DR("lS"), "rawS", "s")
-    tt(R("L0"), R("L0"), R("LS"), ALU.add)
+    for i in range(NV, 16):
+        ms(R("OWNR", i, 256, 16), 0.0)
+    ts(R("EM"), R("EM"), col(P3), ALU.is_equal)
+    ts(FL, R("TMPF", 96, 104), col(P2), ALU.add)
+    ts(EL, R("TMPF", 104, 136), col(P316), ALU.add)
     for rl in range(2):
         iota(R("CR", 256 * rl, 256 * rl + 128, p1=1), [[0, 8], [-256, 16]], 256 * 15 - 128)
         iota(R("CR", 256 * rl + 128, 256 * rl + 256, p1=1), [[0, 8], [-256, 16]], 256 * 31)
-    iota(R("TMPF", 192, 200), [[16, 4], [4, 2]])
-    iota(R("TMPF", 208, 240), [[136, 2], [64, 2], [1, 8]])
-    iota(R("THR"), [[0, 8], [-1, 4], [1, 4]])
-    iota(R("WT", 32, 64), [[1, 4], [0, 8]], 0, 4)
-    iota(R("EM"), [[0, 32], [1, 4], [0, 4]])
+    pick(R("RM16"), R("ONES"), [[0, 32], [1, 16]], ALU.is_gt, 0, 0)
+    pick(R("THR", 0, 128, p1=1), R("THR", 128, 256, p1=1), [[0, 8], [-1, 4], [1, 4]], EQ0, 0, 0)
     iota(R("STAB"), [[0, 32], [16, 4]])
-    iota(R("IDN"), [[1, 2], [2, 512]])
-    ts(FL, R("TMPF", 192, 200), col(P2), ALU.add)
-    ts(EL, R("TMPF", 208, 240), col(P316), ALU.add)
-    ts(R("THR"), R("THR"), 0.0, ALU.is_equal, 960.0, ALU.mult)
-    ts(R("EM"), R("EM"), col(P3), ALU.is_equal)
-    act(R("WT", 0, 32), R("WT", 32, 64), ACT.Exp, LW0, -LG)
-    act(R("THR"), R("THR"), ACT.Identity, -961.0)
-
-    BANKS = ["K0", "K1", "D0", "D1"]
+    iota(R("FB", 0, 96), [[0, 96]])
+    iota(R("FB", 224, 320), [[0, 96]])
+    pick(R("LS"), one, [[1, 128]], ALU.is_gt, 0, -1)
+    pick(R("LI"), one, [[1, 128]], ALU.is_ge, 0, -1)
+    pick(R("L0"), R("LS"), [[1, 128]], NE0, 0, -1, -1024.0)
+    iota(R("IOT"), [[1, 192]], -64)
+    pick(R("RM4"), one, [[0, 32], [1, 4]], ALU.is_gt, 0, 0)
+    for nm in (("IF", "IZ") if nxt == 0 else ("IZ",)):
+        for a in range(2):
+            for c in (0, 144):
+                iota(R("%s%d" % (nm, a), c, c + 16), [[0, 16]])
+            for w in range(2):
+                pick(R("%s%d" % (nm, a), 16 + 64 * w, 80 + 64 * w), R("ONEF", 0, 64), [[-32, 2], [-272, 2], [-1, 16]], EQ0,
+                     256 * a - 64 * (1 - w if nm == "IF" else w))
+    iota(R("ZQ", 0, 256, 4), [[0, 64]])
+    for s in range(4):
+        pick(R("SELF", 128 * s, 128 * s + 128), onef, [[-64, 2], [0, 4], [-1, 16]], EQ0, -16 * s)
+    iota(R("IDN", 0, 512), [[2, 512]])
+    for s in range(4):
+        pick(R("SEL", 128 * s, 128 * s + 128), one, [[-64, 2], [0, 4], [-1, 16]], EQ0, -16 * s)
 
     def PM(a, b, nm="IZ"):
         o = 16 + 16 * (a - b)
         return R("%s%d" % (nm, a), o, o + 128)
 
-    def spread(src, par, sw, engines):
-        for s in range(4):
-            mm(R(BANKS[s]), R("SEL", 128 * s, 128 * s + 128), src, True, True)
-        for s in range(4):
-            o = R(sw, 1024 * s + par, 1024 * s + 1024, 2)
-            if engines[s] == "v":
-                cp(o, R(BANKS[s]))
-            else:
-                act(o, R(BANKS[s]), ACT.Copy)
+    def spread(src, banks, ranks):
+        for s in ranks:
+            mm(R(banks[s]), R("SEL", 128 * s, 128 * s + 128), src, True, True)
+
+    def fill(sw, par, s, bank, engine):
+        o = R(sw, 1024 * s + par, 1024 * s + 1024, 2)
+        if engine == "v":
+            cp(o, R(bank))
+        else:
+            act(o, R(bank), ACT.Copy)
 
     def window(td, tw, par, group):
         for w in range(2):
@@ -319,37 +348,44 @@ def rank_program(g, core, T, topo):
                     c = 1024 * s + 512 * par
                     dma(R(tw, c, c + 512, 1, 64 * w + 16 * q, 64 * w + 16 * q + 16), src, group)
 
-    def row_select(a, b, fy, hy):
-        return [lambda: tt(R("Y1", a, b), fy, R("RY", a, b), ALU.subtract),
-                lambda: tt(R("Y1", 64 + a, 64 + b), R("Y1", a, b), hy, ALU.mult),
-                lambda: tt(R("RN", a, b), R("Y1", 64 + a, 64 + b), R("RY", a, b), ALU.add)]
+    def row_select(out, new, old, tmp):
+        h = (tmp[4] + tmp[5]) // 2
+        x, y = R(tmp[0], tmp[4], h), R(tmp[0], h, tmp[5])
+        return [lambda: ts(x, new, 4096.0, ALU.is_lt, 8192.0, ALU.mult), lambda: tt(y, old, x, ALU.add),
+                lambda: tt(out, y, new, ALU.min)]
 
-    def row_fix(td, h, t, land, group):
-        for w in range(2):
-            lw = 1 - w if flip else w
-            dma(R(td, 512 * h, 512 * h + 512, 1, 64 * w + t, 64 * w + 64, 16), R(land[0], land[4], land[5], 1, 64 * lw, 64 * lw + 64), group)
+    def row(td, h, t, s0):
+        return R(td, 512 * h, 512 * h + 512, 1, 16 * s0 + t, 128, 32)
 
-    eight = ["ZN", "PA", "PB", "TS", "D0", "D1", "K0", "K1"]
+    def spread_row(nm, h, s0):
+        return R(nm, 32 * h, 32 * h + 32, 1, s0, 128, 2)
+
+    def old_row(td, t):
+        for h in range(2):
+            for s0 in range(2):
+                dma(spread_row("RY", h, s0), row(td, h, t, s0), "ry%d" % t)
+
+    eight = ["K0", "K1", "D0", "D1", "ZN", "PA", "PB", "TS"]
+    for k in range(16):
+        s, c = k // 4, k % 4
+        mm(R(eight[k // 2], 256 * (k % 2), 256 * (k % 2) + 256), R("SE0", 128 * c, 128 * c + 128), R("SR", 256 * s, 256 * s + 256),
+           True, True)
     for k in range(8):
-        mm(R(eight[k]), R("SEL", 128 * (k // 2), 128 * (k // 2) + 128), R("SRAW", 512 * (k % 2), 512 * (k % 2) + 512), True, True)
-    cp(R("TG"), ind(R("TRA2"), R("CL", 128, 160)))
-    cp(R("SD0", 0, 512), R("SRAW", 0, 1024, 2))
-    tr(R("TX"), R("TG"))
-    cp(R("SW0", 512 * 7, 512 * 8), R(eight[7]))
-    cp(R("OFF0"), ind(R("TX"), L2))
-    cp(R("SW0", 512 * 5, 512 * 6), R(eight[5]))
-    for k in (6, 0, 1, 2, 3, 4):
         act(R("SW0", 512 * k, 512 * k + 512), R(eight[k]), ACT.Copy)
-    cp(R("TD0", 0, 512), R("TRAW", 0, 1024, 2))
-    window("TD0", "TW0", 0, "twa0")
-    sd = [R("SD0", 0, 512), R("SD0", 512, 1024)]
+    cp(R("TG"), ind(R("TR", 0, 512), L1))
+    tr(R("TX"), R("TG"))
+    cp(R("OFS"), ind(R("TX"), L3))
+    for a in range(2):
+        for w in range(2):
+            for b in range(2):
+                cp(R("OFF0", 256 * a, 256 * a + 256, 1, 64 * w + 32 * b, 64 * w + 32 * b + 32),
+                   R("OFS", 256 * b, 256 * b + 256, 1, 64 * w + 32 * a, 64 * w + 32 * a + 32))
+    sd = [R("SD", 0, 1024, 2), R("SD", 1, 1024, 2)]
 
-    def odd_halves():
-        cp(R("TD0", 512, 1024), R("TRAW", 1, 1024, 2))
-        cp(R("SD0", 512, 1024), R("SRAW", 1, 1024, 2))
-        window("TD0", "TW0", 1, "twb0")
-
-    later = {NV - 1: [odd_halves]}
+    for h in range(2):
+        window("TD0", "TW0", h, "tw%s0" % "ab"[h])
+    old_row("TD0", 0)
+    later = {}
 
     for t in range(RO):
         par, npar, last = t % 2, 1 - t % 2, t == RO - 1
@@ -370,10 +406,12 @@ def rank_program(g, core, T, topo):
                 mm(kcol(r, i, 256, 16), R("M", 512 * i + r, 512 * i + 512, 4), R("SUMR"), False, stop and r % 2 == 1)
 
         for k in range(2):
-            mm(R("K%d" % k), R("ONE1", p1=33), R("CR", p1=33), True, False)
+            mm(R("K%d" % k), R("ONES", 0, 128, p1=33), R("CR", p1=33), True, False)
         for r in range(4):
-            mm(kcol(r, 0, 256), R(own[0], own[4] + r, own[5], 4), R("OWNR"), False, False)
-        vrows = [i for i in range(NV) if i != t - 1] + ([t - 1] if t else [])
+            mm(kcol(r, 0, 256), R("SD", par + 2 * r, 1024, 8), R("OWNR"), False, False)
+        for k in range(2):
+            mm(R("D%d" % ((NV + k) % 2)), R("NEG"), own, True, False)
+        vrows = list(range(NV))
         srows = list(range(NV, 16))
         ev, clock = [], 0
         for k, i in enumerate(vrows):
@@ -403,11 +441,12 @@ def rank_program(g, core, T, topo):
                 sums(i, e == lastsum)
             elif e[1] == "g":
                 act(R("G%d" % (i % 2)), ind(win, oi), ACT.Copy)
-                mm(R("D%d" % (i % 2)), R("IDB"), R("G%d" % (i % 2)), True, False)
-                mm(R("D%d" % (i % 2)), R("NEG"), own, False, True)
+                mm(R("D%d" % (i % 2)), R("IDB"), R("G%d" % (i % 2)), False, True)
             elif e[1] == "r":
                 act(mi, R("D%d" % (i % 2)), ACT.Relu)
                 sums(i, e == lastsum)
+                if i + 2 < 16:
+                    mm(R("D%d" % (i % 2)), R("NEG"), own, True, False)
             elif e[1] == "h":
                 act(R("HI"), tpar, ACT.Identity, 129 - 0.484375, 1.0 / 32)
                 for r in range(4):
@@ -417,243 +456,222 @@ def rank_program(g, core, T, topo):
                 for fn in later.get(i, []):
                     fn()
 
+        if not last:
+            tr(R("TX"), tnp)
         for k in range(2):
             scan(R("KS", 512 * k, 512 * k + 512), R("RM16"), R("K%d" % k), ALU.mult, ALU.max)
-        cp(R("II"), R("KS", 15, 1024, 16))
-        ts(R("NC"), R("KS", 15, 1024, 16), 4096.0, ALU.is_lt, 64.0, ALU.mult)
-        ts(R("DG", 0, 64), R("II"), 1, sh, 48, an)
-        ts(R("DG", 64, 128), R("II"), 31, an)
-        ts(R("DG", 192, 256), R("II"), 1, an)
-        ts(R("DG", 128, 192), R("II"), 1, sh, 15, an)
-        tt(R("CS"), R("DG", 0, 64), R("NC"), ALU.add)
-        ts(R("AB", 128, 192), R("DG", 192, 256), 32.0, ALU.mult)
-        tt(R("AB", 0, 56), R("DG", 0, 56), R("DG", 136, 192), ALU.add)
-        tt(R("FB", 96, 224), ind(R("CS"), FL), R("STAB"), ALU.is_equal)
         cnt = R("PA", 0, 128)
-        mm(cnt, R("L0"), R("FB", 96, 224), True, False)
+        one1 = R("ONES", 0, 128, p1=1)
+        mm(cnt, one1, R("THR", 0, 128, p1=1), True, False)
+        mm(R("ZN"), one1, R("ONES", p1=1), True, False)
+        ts(R("II"), R("KS", 15, 1024, 16), 4095.0, ALU.max)
+        for r in range(4):
+            act(R("ZP", 128 * r, 128 * r + 128), kcol(r, 0, 128), ACT.Sign, 4095.5, -1.0)
+        if not last:
+            act(R("TG"), ind(R("TX"), L2), ACT.Copy)
+        ts(R("DG", 256, 320), R("II"), 1, sh, 112, an)
+        ts(R("DG", 192, 256), R("II"), 1, an)
+        ts(R("DG", 64, 128), R("II"), 31, an)
+        tt(R("FB", 96, 224), ind(R("DG", 256, 320), FL), R("STAB"), ALU.is_equal)
+        ts(R("AB", 128, 192), R("DG", 192, 256), 32.0, ALU.mult)
+        ts(R("DG", 0, 64), R("II"), 1, sh, 48, an)
+        ts(R("DG", 128, 192), R("II"), 1, sh, 15, an)
+        mm(cnt, R("L0"), R("FB", 96, 224), False, False)
         for k in range(1, 4):
             mm(cnt, R("LI"), R("FB", 96 - 32 * k, 224 - 32 * k), False, False)
             mm(cnt, R("LS"), R("FB", 96 + 32 * k, 224 + 32 * k), False, k == 3)
-        if not last:
-            for q0 in range(2):
-                for be in range(2):
-                    c = 512 * npar + 256 * be
-                    mm(R("TS", 256 * q0, 256 * q0 + 256), PM(q0, be, "IF" if nxt == 0 else "IZ"), R(td, c, c + 256), be == 0, be == 1)
         tt(R("AB", 64, 120), R("DG", 64, 120), R("AB", 136, 192), ALU.add)
-        tt(R("EE", 0, 256), ind(R("DG"), R("CL", 64, 80)), R("EM", 0, 256), ALU.mult)
-        for r in range(4):
-            act(R("ZP", 128 * r, 128 * r + 128), kcol(r, 0, 128), ACT.Sign, 4095.5, -1.0)
-        act(R("ZP"), R("ZP"), ACT.Relu)
-        byS = [(blk + 1) * NB // 16 != blk * NB // 16 for blk in range(16)]
-        byV = [k for k in range(32) if not byS[k // 2]]
+        tt(R("AB", 0, 56), R("DG", 0, 56), R("DG", 136, 192), ALU.add)
+        tt(R("EE", 0, 256), ind(R("DG", 0, 256), R("CL", 64, 80)), R("EM"), ALU.mult)
+        byV = list(range(2 * NB, 32))
 
         def bcol(k):
-            c = 64 + 16 * (k // 2 % 4) + 4 * (k % 2) + k // 8
+            c = 64 + 16 * (k // 8) + 4 * (k % 2) + k // 2 % 4
             return R("AB", c, c + 1)
+
+        def step(blk):
+            return math.exp(-LG * (blk // 4))
 
         def onehot(ks):
             for k in ks:
-                ts(R("BB", 64 * k, 64 * k + 64), R("IOT", 64, 128), bcol(k), ALU.is_equal)
+                ts(R("BB", 64 * k, 64 * k + 64), R("IOT", 64, 128), bcol(k), ALU.is_equal, step(k // 2), ALU.mult)
 
-        tt(R("OK"), cnt, R("THR"), ALU.is_le)
+        ts(R("OK"), cnt, -961.0, ALU.is_le, col(WP), ALU.mult)
         onehot(byV[0:3])
-        scan(R("TH", 0, 128), R("RM4", 0, 128), R("OK"), ALU.mult, ALU.max)
-        onehot(byV[3:6])
-        tt(R("TH", 128, 160), R("TH", 3, 128, 4), R("WT", 0, 32), ALU.mult)
-        onehot(byV[6:])
-
-        prev = None
-        for blk in [b for b in range(16) if byS[b]] + [None]:
-            if blk is not None:
-                for k in (2 * blk, 2 * blk + 1):
-                    act(R("BX", 64 * k, 64 * k + 64), R("IOT", 64, 128), ACT.Abs, bcol(k), -1.0)
-            if prev is not None:
-                act(R("BB", 128 * prev, 128 * prev + 128), R("BX", 128 * prev, 128 * prev + 128), ACT.Relu, 1.0, -1.0)
-            prev = blk
-        if not last:
-            pass_on("aa%d" % t, tnp, R("LT", 1024 * t, 1024 * t + 512), R(tdn, 512 * npar, 512 * npar + 512), "cpa%d" % t)
-            if t == 0:
-                dma(R("RY", 32 * npar, 32 * npar + 32), R(td, 512 * npar, 512 * npar + 512, 1, t, 128, 16), "rya%d" % t)
-        for blk in range(16):
-            q, r = blk // 4, blk % 4
-            for w in range(2):
-                G, k = 4 * w + q, 2 * blk + w
-                c = 16 * r + G
-                th = 128 + 8 * r + G
-                ts(R("AA", 128 * k, 128 * k + 128), R("IOT", 64 - 64 * w, 192 - 64 * w), R("AB", c, c + 1), ALU.is_equal,
-                   R("TH", th, th + 1), ALU.mult)
-            for h in range(2):
-                o = R("D%d" % h, (3 - q) * 4 + r, 512, 16)
-                for w in range(2):
-                    k = 2 * blk + w
-                    mm(o, R("AA", 128 * k, 128 * k + 128), R("BB", 64 * k + 32 * h, 64 * k + 32 * h + 32), w == 0, w == 1)
-        if not last:
-            act(R("TSS"), R("TS"), ACT.Copy)
-            act(R("TG"), ind(R("TSS"), L1), ACT.Copy)
-        if t == 0:
-            act(R("IDN"), R("IDN"), ACT.Identity, col(Q1K))
-        tt(R("EE", 256, 512), ind(R("DG"), R("CL", 80, 96)), R("EM", 256, 512), ALU.mult)
-        for dg in range(4):
-            mm(R("PB", 0, 96), R("EE", 128 * dg, 128 * dg + 128), R("RHS", 96 * dg, 96 * dg + 96), dg == 0, dg == 3)
+        scan(R("TH"), R("RM4", 0, 128), R("OK"), ALU.mult, ALU.max)
+        onehot(byV[3:])
         for r in range(4):
-            mm(R("ZN", r, 512, 4), R("ZP", 128 * r, 128 * r + 128), R("IDB"), True, True)
-        for h in range(2):
-            scan(R("HS", 512 * h, 512 * h + 512), R("RM4"), R("D%d" % h), ALU.mult, ALU.max)
-        cp(R("SBU"), R("PB", 64, 96))
-        tt(R("DC"), R("PB", 0, 64), R("SELFC", 64 * par, 64 * par + 64), ALU.subtract)
-        for qq in range(1, 4):
-            ts(R("ZQ", qq, 256, 4), R("HS", 4 * qq + 3, 1024, 16), 0.0, ALU.is_equal)
-        if not last:
-            tr(R("TX"), R("TG"))
-        scan(R("H2"), R("ZQ"), R("HS", 3, 1024, 4), ALU.mult, ALU.add)
-        scan(R("Q2"), R("ONES"), R("ZQ"), ALU.add, ALU.mult)
-        hs = R("H2", 3, 256, 4)
-        ts(R("XY", 0, 64), hs, 1.0, ALU.min, 2.0 ** 62, ALU.mult)
-        ts(R("XY", 64, 128), hs, 1.0, ALU.max, 2.0 ** -62, ALU.mult)
-        act(R("LL"), R("XY"), ACT.Ln, 1e-23)
-        ts(R("QS", 64, 128), hs, 0.0, ALU.is_equal, -8192.0 * LG, ALU.mult)
-        ts(R("QS", 0, 64), R("Q2", 3, 256, 4), -512.0 * LG, ALU.mult, -LW0 - 0.448 * LG, ALU.add)
+            mm(R("ZN", r, 512, 4), R("ZP", 128 * r, 128 * r + 128), R("IDB"), False, False)
+
+        def lists(b0, s0):
+            if not last:
+                mm(R("TS", b0, 512, 2), PM(b0, s0, "IF" if nxt == 0 else "IZ"), R("TG", 256 * s0, 256 * s0 + 256), s0 == 0, s0 == 1)
 
         def ofs(a, b):
             if not last:
-                cp(R("OFS", 16 * a, 16 * b), ind(R("TX"), R("CL", 32 + a, 32 + b)))
+                cp(R("OFS", a, b), R("TS", a, b))
 
-        ofs(0, 8)
-        tt(R("QS", 0, 64), R("QS", 0, 64), R("QS", 64, 128), ALU.add)
-        tt(R("T1", 0, 64), R("LL", 0, 64), R("LL", 64, 128), ALU.add)
-        ofs(8, 16)
-        tt(R("T1", 64, 128), R("T1", 0, 64), R("QS", 0, 64), ALU.add)
-        ofs(16, 24)
-        ts(R("ID"), R("T1", 64, 128), -1.0 / LG, ALU.mult, 2048.0, ALU.min)
-        ofs(24, 32)
-        ts(R("FF"), R("ID"), 2.0, ALU.mult, float(par), ALU.add)
-        ts(R("FU"), R("ID"), 2.0, ALU.mult, float(par), ALU.add)
+        lists(0, 0)
+        lists(0, 1)
+
+        rb = ["D0", "D1", "K1", "PA"]
+
+        def column_onehots(blks):
+            for blk in blks:
+                if blk < NB:
+                    for k in (2 * blk, 2 * blk + 1):
+                        act(R("BX", 64 * k, 64 * k + 64), R("IOT", 64, 128), ACT.Abs, bcol(k), -1.0)
+                if blk:
+                    c, f = 128 * blk - 128, step(blk - 1)
+                    act(R("BB", c, c + 128), R("BX", c, c + 128), ACT.Relu, f, -f)
+
+        column_onehots(range(9))
+        for blk in range(16):
+            r, q = blk // 4, blk % 4
+            o = R(rb[r], 3 - q, 256, 4)
+            if blk == 3:
+                mm(o, one1, R("TINY", p1=1), True, False)
+            for w in range(2):
+                G, k = 4 * w + q, 2 * blk + w
+                c = 16 * r + G
+                th = 4 * (8 * r + G) + 3
+                ts(R("AA", 128 * k, 128 * k + 128), R("IOT", 64 - 64 * w, 192 - 64 * w), R("AB", c, c + 1), ALU.is_equal,
+                   R("TH", th, th + 1), ALU.mult)
+            for w in range(2):
+                k = 2 * blk + w
+                mm(o, R("AA", 128 * k, 128 * k + 128), R("BB", 64 * k, 64 * k + 64), w == 0 and blk != 3, w == 1)
+            if blk == 3:
+                tt(R("EE", 256, 512), ind(R("DG", 0, 256), R("CL", 80, 96)), R("EM"), ALU.mult)
+                act(R("HS"), R(rb[0], 0, 256), ACT.Copy)
+                column_onehots(range(9, NB + 1))
+            if blk == 5:
+                for dg in range(4):
+                    mm(R("PB", 0, 96), R("EE", 128 * dg, 128 * dg + 128), R("RHS", 96 * dg, 96 * dg + 96), dg == 0, dg == 3)
+            if blk == 9:
+                cp(R("CU"), R("PB", 0, 96))
+            if blk == 11:
+                tt(R("HS"), R(rb[1], 0, 256), R("HS"), ALU.max)
+            if blk == 14:
+                tt(R("HS"), R(rb[2], 0, 256), R("HS"), ALU.max)
+            if blk in (3, 7):
+                lists(1, blk // 4)
+        act(R("DD"), ind(R(tw), R("CU", 32, 64)), ACT.Copy)
+        act(R("GC"), ind(win, R("CU", 0, 32)), ACT.Identity, -256.0)
+        ofs(256, 512)
+        tt(R("HS"), R(rb[3], 0, 256), R("HS"), ALU.max)
+        mm(R("K0"), R("NEF"), tpar, True, False)
+        mm(R("K0"), R("IDF"), R("DD"), False, True)
+        for qq in range(1, 4):
+            ts(R("ZQ", qq, 256, 4), R("HS", qq, 256, 4), 0.0, ALU.is_equal)
+        scan(R("H2"), R("ZQ"), R("HS"), ALU.mult, ALU.add)
+        scan(R("Q2"), R("ONES", 0, 256), R("ZQ"), ALU.add, ALU.mult)
+        hs = R("H2", 3, 256, 4)
+        ts(R("XY", 0, 64), hs, 1.0, ALU.min, 2.0 ** 62, ALU.mult)
+        ts(R("XY", 64, 128), hs, 1.0, ALU.max, 2.0 ** -62, ALU.mult)
+        for k in range(2):
+            act(R("LQ", 1 + k, 256, 4), R("XY", 64 * k, 64 * k + 64), ACT.Ln)
+        ts(R("LQ", 3, 256, 4), R("Q2", 3, 256, 4), 1024.0, ALU.mult, EVEN, ALU.add)
+        ofs(128, 256)
+        scan(R("T1"), R("RMQ"), R("LQ"), ALU.mult, ALU.add)
+        ts(R("FF"), R("T1", 3, 256, 4), -EVEN, ALU.add, float(par), ALU.add)
+        ts(R("FU"), R("T1", 3, 256, 4), -EVEN, ALU.add, float(par), ALU.add)
+        for s0 in range(2):
+            for h0 in range(2):
+                mm(R("PB", 128 + s0, 192, 2), PM(s0, h0), R("FF", h0, 64, 2), h0 == 0, h0 == 1)
         for s in range(4):
             mm(R("PA", 64 * s, 64 * s + 64), R("SELF", 128 * s, 128 * s + 128), R("FF"), True, True)
-        act(R("WW"), R("PA", 0, 256), ACT.Copy)
+        act(R("WW"), R("PA", 0, 256), ACT.Identity, col(Q1K + par))
+        a = 32 * npar
+        if not last:
+            new, old = R("FF", a, a + 32), R("TS", 32 * t, 32 * t + 32)
+            if nxt == 0:
+                for h in range(2):
+                    cp(R("X1", 64, 96, 1, 64 * h, 64 * h + 64), R("FF", a, a + 32, 1, 64 - 64 * h, 128 - 64 * h))
+                new = R("X1", 64, 96)
+            lst = row_select(old, new, old, R("X1", 0, 64)) + [lambda: cp(R("OFS", 0, 128), R("TS", 0, 128))]
+        else:
+            lst = [lambda: None] * 4
+
+        kb, db = ["K1", "D0", "D1", "TS"], ["PA", "K1", "D0", "ZN"]
+        sel = row_select(R("RN"), R("FY"), R("RY"), R("Y1"))
+        if nxt or last:
+            lst.pop(0)()
+        tt(sd[npar], ind(win, R("FU", a, a + 32)), sd[npar], ALU.max)
+        mm(R("PA"), R("IDB"), R("GC"), True, False)
+        if not last:
+            spread(sd[npar], kb, (0, 1, 2))
+            fill(swn, npar, 0, kb[0], "s")
+        lst.pop(0)()
+        tr(R("FY"), R("PB", 128, 192))
+        lst.pop(0)()
+        sel[0]()
+        ts(R("CB"), R("FY", 32 * par, 32 * par + 32), 4096.0, ALU.is_lt)
+        lst.pop(0)()
+        sel[1]()
+        for fn in lst:
+            fn()
         if not last:
             send("ao%d" % t, [(nxt, R("OFS"), R(offn))], wide)
             arrive("ao%d" % t, [R(offn)], wide)
-            ln = R("LN", 32 * t, 32 * t + 32)
-            send("an%d" % t, [(nxt, R("FF", 32 * npar, 32 * npar + 32), ln)], wide)
-            arrive("an%d" % t, [ln], wide)
-        for pp in range(2):
-            for s0 in range(2):
-                for h0 in range(2):
-                    c = 128 + 32 * pp + 16 * s0
-                    mm(R("PB", c, c + 16), PM(s0, h0), R("FF", 32 * pp + h0, 32 * pp + 32, 2), h0 == 0, h0 == 1)
-
-        keep = R("SD0", 512 * npar, 512 * npar + 512) if sd[npar][0] != "SD0" else R("SB%d" % npar)
-        done = R("SD0", 512 * par, 512 * par + 512) if own[0] != "SD0" else R("SB%d" % par)
-
-        def called(h):
-            tt(R("SA", 256 * h, 256 * h + 256), ind(win, R("FU", 32 * par + 16 * h, 32 * par + 16 * h + 16)),
-               R(own[0], own[4] + 256 * h, own[4] + 256 * h + 256), ALU.max)
-
-        tt(keep, ind(win, R("FU", 32 * npar, 32 * npar + 32)), sd[npar], ALU.max)
-        if last:
-            act(R("OT", npar, 1024, 2), tnp, ACT.Copy)
-            act(R("OS", npar, 1024, 2), keep, ACT.Copy)
-        else:
-            called(0)
-        tt(R("EQ"), ind(R("WW"), R("SBU")), R("IDN", 512 * par, 512 * par + 512), ALU.is_equal)
-        conn = R("PA", 256, 288)
-        for l in range(16):
-            mm(conn, R("BZ", 15 - l, 143 - l), R("EQ", l, 512, 16), l == 0, l == 15)
-        if not last:
-            spread(keep, npar, swn, "ssss")
-        tr(R("FY", 0, 64), R("PB", 128, 192))
-        called(0 if last else 1)
-        sd = [None, None]
-        sd[par], sd[npar] = done, keep
-        a = 32 * npar
-        if last:
-            sel = [lambda: cp(R("FY", 64, 128, 2), R("FY", 0, 32)), lambda: cp(R("FY", 65, 128, 2), R("FY", 32, 64)),
-                   lambda: called(1)]
-        else:
-            sel = row_select(a, a + 32, R("FY", a, a + 32), R("HY", a, a + 32))
-            ts(R("HY"), R("FY", 0, 64), 4096.0, ALU.is_lt)
-        sel[0]()
-        tt(R("C1", 0, 32), conn, R("DC", 0, 32), ALU.mult)
-        tt(R("C1", 32, 64), conn, R("DC", 32, 64), ALU.mult)
-        sel[1]()
-        tt(R("C1", 64, 128), R("C1", 0, 64), R("SELFC", 64 * par, 64 * par + 64), ALU.add)
+            spread(sd[npar], kb, (3,))
+        for s0 in range(2):
+            dma(R("CZ", 0, 512, 1, 16 * s0 + t, 128, 32), R("CB", 0, 32, 1, s0, 128, 2), "cz%d" % t)
         sel[2]()
-        cp(R("CU"), R("C1", 64, 128))
+        for h in (npar, par):
+            for s0 in range(2):
+                dma(row(td, h, t, s0), spread_row("RN", h, s0), "fx%s%d" % ("ab"[h], t))
         if not last:
-            lra = R("LR", 64 * t, 64 * t + 32)
-            send("ara%d" % t, [(nxt, R("RN", a, a + 32), lra)], wide)
-            arrive("ara%d" % t, [lra], wide)
-            tt(done, ind(win, R("CU", 0, 32)), R("SA"), ALU.max)
-            if flip:
-                hand(R("OLDX", 32, 64), ln, "cpn%d" % t)
-            row_fix(tdn, npar, t, lra, "fxa%d" % t)
-        else:
-            ts(R("HY"), R("FY", 64, 128), 4096.0, ALU.is_lt)
-
-        tt(R("TD_"), ind(R(tw), R("CU", 32, 64)), tpar, ALU.subtract)
+            pass_on("aa%d" % t, tnp, R("LT", 1024 * t, 1024 * t + 512), R(tdn, 512 * npar, 512 * npar + 512), "cpa%d" % t)
+        tt(R("EQ"), ind(R("WW"), R("CU", 64, 96)), R("IDN"), ALU.is_equal)
+        if not last:
+            mm(R("PA"), R("BO2"), R("EQ"), False, True)
+        mm(R("ZN"), R("BO"), R("EQ"), False, False)
+        mm(R("ZN"), R("NT", 128 * t, 128 * t + 128), R("CZ"), False, True)
         if last:
-            tt(done, ind(win, R("CU", 0, 32)), R("SA"), ALU.max)
-        else:
-            spread(done, par, swn, "vsss")
-        tt(R("TS"), R("ZN"), R("TD_"), ALU.mult)
+            mm(R("PA"), R("BO2"), R("EQ"), False, True)
+        tt(own, ind(win, R("FU", 32 * par, 32 * par + 32)), own, ALU.max)
         if not last:
-            lst, old, fx = R(offn, 32 * t, 32 * t + 32), R("OLDX", 0, 32), R("OLDX", 32, 64) if flip else ln
-            cp(old, lst)
-            tt(R("TB"), R("TS"), tpar, ALU.add)
-            dma(R("RY", 32 * par, 32 * par + 32), R("TB", 0, 512, 1, t, 128, 16), "ryb%d" % t)
-            pass_on("ab%d" % t, R("TB"), R("LT", 1024 * t + 512, 1024 * t + 1024), R(tdn, 512 * par, 512 * par + 512), "cpb%d" % t)
-            a = 32 * par
-            sel = row_select(a, a + 32, R("FY", a, a + 32), R("HY", a, a + 32))
-
-            def rest(t=t, par=par, npar=npar, tdn=tdn, twn=twn, a=a):
-                lrb = R("LR", 64 * t + 32, 64 * t + 64)
-                send("arb%d" % t, [(nxt, R("RN", a, a + 32), lrb)], wide)
-                arrive("arb%d" % t, [lrb], wide)
-                row_fix(tdn, par, t, lrb, "fxb%d" % t)
-                if t + 2 < RO:
-                    dma(R("RY", a, a + 32), R(tdn, 512 * par, 512 * par + 512, 1, t + 1, 128, 16), "rya%d" % (t + 1))
+            for s in (1, 2):
+                fill(swn, npar, s, kb[s], "s")
+        act(R("MK"), R("ZN"), ACT.Relu, -2.0)
+        if not last:
+            tt(own, R("PA"), own, ALU.max)
+            fill(swn, npar, 3, kb[3], "s")
+            spread(own, db, range(4))
+            tt(R("TB"), R("K0"), R("MK"), ALU.mult)
+            fill(swn, par, 0, db[0], "v")
+            for s in (1, 2):
+                fill(swn, par, s, db[s], "s")
+            fill(swn, par, 3, db[3], "v")
+            if not flip:
                 window(tdn, twn, npar, "twa%d" % (t + 1))
-                window(tdn, twn, par, "twb%d" % (t + 1))
-
-            def row_list(lst=lst, old=old, fx=fx):
-                return [lambda: ts(R("X1", 0, 32), fx, 4096.0, ALU.is_lt),
-                        lambda: tt(R("X1", 32, 64), fx, old, ALU.subtract),
-                        lambda: tt(R("X1", 64, 96), R("X1", 32, 64), R("X1", 0, 32), ALU.mult),
-                        lambda: tt(old, R("X1", 64, 96), old, ALU.add), lambda: cp(lst, old)]
-            rl = row_list()
-            later = {0: rl[0:2], 2: [rl[2]], 3: [rl[3], sel[0]], 4: [rl[4], sel[1]], 5: [sel[2], rest]}
+            pass_on("ab%d" % t, [R("TB"), tpar], R("LT", 1024 * t + 512, 1024 * t + 1024), R(tdn, 512 * par, 512 * par + 512), "cpb%d" % t)
+            if flip:
+                window(tdn, twn, npar, "twa%d" % (t + 1))
+            window(tdn, twn, par, "twb%d" % (t + 1))
+            old_row(tdn, t + 1)
+            later = {}
             continue
 
-        act(R("OS", par, 1024, 2), done, ACT.Copy)
-        for k0, k1 in spans:
-            dma(DR("oS", k0, k1), R("OS", 0, 1024, 1, 16 * k0, 16 * k1), "oS", "s")
-        tt(R("OT", par, 1024, 2), R("TS"), tpar, ALU.add)
-        dma(R("RY"), R("OT", 0, 1024, 1, t, 128, 16), "ryl", "s")
-        for k0, k1 in spans:
-            dma(DR("oT", k0, k1), R("OT", 0, 1024, 1, 16 * k0, 16 * k1), "oT")
-        for fn in row_select(0, 64, R("FY", 64, 128), R("HY")):
-            fn()
-        exchange("aoS", "oS", "loS")
-        exchange("aoT", "oT", "loT")
-        send("aRI", [(d, R("RN"), R("LRI", 64 * rank, 64 * rank + 64)) for d in others], 2 * w6)
-        arrive("aRI", [R("LRI", 64 * d, 64 * d + 64) for d in others], 6 * w6)
+        act(R("OT", npar, 1024, 2), tnp, ACT.Copy)
+        tt(R("K0"), R("K0"), R("MK"), ALU.mult)
+        parts = (("T0", "OT", 0, 512, T.ytel), ("T1", "OT", 512, 512, T.ytel), ("S", "SD", 0, 1024, T.ysec))
+        for nm, src, c, width, y in parts:
+            if nm == "S":
+                tt(own, R("PA"), own, ALU.max)
+            else:
+                h = c // 2
+                tt(R("OT", c + par, c + 512, 2), R("K0", h, h + 256), R(td, 512 * par + h, 512 * par + h + 256), ALU.add)
+            for k, (k0, k1) in enumerate(spans):
+                dma(DR("o" + nm, k0, k1), R(src, c, c + width, 1, 16 * k0, 16 * k1), "o" + nm, "ys"[k % 2])
+        for nm, src, c, width, y in parts:
+            exchange("ao" + nm, "o" + nm, "lo" + nm)
         for mine in (True, False):
-            worlds = [gg for gg in range(8) if (gg % n == rank) == mine]
-            for gg in worlds:
-                p0 = 64 * (gg // n) + 16 * rank
-                a = R("OS", 0, 1024, 1, p0, p0 + 16) if mine else DR("loS", gg, gg + 1)
-                dma(("raw", T.ysec[16 * gg:16 * gg + 16, :]), a, "out", "y")
-            for gg in worlds:
-                p0 = 64 * (gg // n) + 16 * rank
-                a = R("OT", 0, 1024, 1, p0 + t + 1, p0 + 16) if mine else DR("loT", gg, gg + 1, 8 * t + 8, 128)
-                b = R("OT", 0, 1024, 1, p0, p0 + t) if mine else DR("loT", gg, gg + 1, 0, 8 * t)
-                dma(("raw", T.ytel[16 * gg + t + 1:16 * gg + 16, :]), a, "out", "y")
-                dma(("raw", T.ytel[16 * gg:16 * gg + t, :]), b, "out", "s")
-            for gg in worlds:
-                p0 = 64 * (gg // n) + 16 * rank
-                c = R("RN", 0, 64, 1, p0, p0 + 16) if mine else R("LRI", 64 * (gg % n), 64 * (gg % n) + 64, 1, p0, p0 + 16)
-                dma(("raw", T.ytel[16 * gg + t:16 * gg + t + 1, :]), c, "out", "s")
+            for nm, src, c, width, y in parts:
+                for k, gg in enumerate(gg for gg in range(8) if (gg % n == rank) == mine):
+                    p0 = 64 * (gg // n) + 16 * rank
+                    a = R(src, c, c + width, 1, p0, p0 + 16) if mine else DR("lo" + nm, gg, gg + 1)
+                    dma(("raw", y[16 * gg:16 * gg + 16, c:c + width]), a, "out", "ys"[k % 2])
 
     emit(ops, Q, T, g)
 

@@ -5,10 +5,12 @@ from concourse.mybir import AluOpType, AxisListType, ActivationFunctionType
 ALU = AluOpType
 ACT = ActivationFunctionType
 NV = 10
-NB = 12
+NB = 11
+GATHER, PASS = 8, 5
+HIAT = 2
 RO = 4
-LG = math.log(1.40)
-LW0 = 124 * math.log(2.0)
+LG = math.log(1.398)
+LW0 = 122 * math.log(2.0)
 EVEN = 1.5 * 2.0 ** 24
 
 F, B, I, U = "float32", "bfloat16", "int32", "uint16"
@@ -23,20 +25,20 @@ def _decl(where, dtype, **kw):
 _decl("psum", F, K0=512, K1=512, D0=512, D1=512, ZN=512, PA=512, PB=512, TS=512)
 _decl("dram", B, oS=[8, 128, 128], loS=[8, 128, 128])
 _decl("dram", F, oT0=[8, 128, 64], loT0=[8, 128, 64], oT1=[8, 128, 64], loT1=[8, 128, 64])
-_decl("sbuf", I, CI=16, TL=1024, II=64, DG=320)
-_decl("sbuf", U, OFF0=512, OFF1=512, OFF2=512, OFF3=512, OFS=512, CL=160, FU=64, CU=96)
+_decl("sbuf", I, CI=16, TL=1024, II=64, DG=128)
+_decl("sbuf", U, OFF0=512, OFF1=512, OFF2=512, OFF3=512, OFS=512, OFT=128, CL=160, FU=64, CU=96)
 _decl("sbuf", B, SL=1024, SR=1024, SW0=4112, SW1=4112, SD=1024, M=8192, G0=512, G1=512, GC=512, HI=512, IOT=192,
-      IDB=128, NEG=128, HIR=256, SEL=512, SE0=512, SUMR=16, OWNR=256, CR=512, RM16=512, RM4=128, ONES=512, LS=128, LI=128,
-      L0=128, FB=320, EM=256, RHS=416, BO=128, BO2=128, AA=4096, BB=2048, BX=2048, EE=512, ZP=512, EQ=512, MK=512, TMPB=128,
-      THR=256, TINY=64, CB=32, CZ=512, NT=512)
-_decl("sbuf", F, CF=48, TE=1024, TR=1024, TD0=1024, TD1=1024, TD2=1024, TD3=1024, TW0=4096, TW1=4096, LT=3072, ONEF=128, IDF=128,
-      NEF=128, SELF=512, IZ0=160, IZ1=160, IF0=160, IF1=160, WT=384, STAB=128, IDN=512, KS=1024, AB=192, OK=128,
-      TH=128, HS=256, ZQ=256, H2=256, Q2=256, XY=128, LQ=256, RMQ=256, T1=256, FF=64, WW=256, TG=512,
-      TX=512, X1=96, FY=64, RY=64, Y1=128, RN=64, DD=512, TB=512, OT=1024, TMPF=256)
+      IDB=128, NEG=128, HIR=512, SEL=512, SE0=512, SUMR=16, OWNR=256, CR=512, RM16=256, RM4=128, ONES=512, LS=128, LI=128,
+      L0=128, FB=320, RHS=416, BO=256, BO2=128, AA=4096, BB=2048, BX=2048, ZP=512, EQ=512, MK=512, TMPB=128,
+      THR=256, TINY=64, CB=32, TOROW=4128, EE=[128, 32, 16])
+_decl("sbuf", F, CF=48, TE=1024, TR=1024, TD0=1024, TD1=1024, TD2=1024, TD3=1024, TW0=4096, TW1=4096, ONEF=128, IDF=256,
+      NEF=128, SELF=512, IZ0=160, IZ1=160, IF0=160, IF1=160, WT=384, STAB=128, IDN=512, KS=[128, 256, 4], AB=96, OK=128,
+      TH=160, HS=256, ZQ=256, H2=256, Q2=256, XY=128, LQ=256, RMQ=256, T1=256, FF=64, WW=512, TG=512,
+      TX=512, X1=32, FY=64, RY=64, Y1=128, RN=64, DD=512, TB=512, OT=1024, TMPF=256)
 
-_DMA_GROUPS = ["ldT", "ldS", "ownT", "ownS", "rawT0", "rawT1", "rawS", "oS", "oT0", "oT1", "out"] + ["%s%d" % (n, t) for t in range(3) for n in
-              ("cpa", "cpb")] + ["%s%d" % (n, t) for t in range(4) for n in ("twa", "twb", "ry", "cz", "fxa", "fxb")]
-_ARRIVE = ["aT0", "aT1", "aS", "aoS", "aoT0", "aoT1"] + ["%s%d" % (n, t) for t in range(3) for n in ("aa", "ab", "ao")]
+_DMA_GROUPS = ["ldT", "ldS", "ownT", "ownS", "rawT0", "rawT1", "rawS", "oS", "oT0", "oT1", "out"]
+_DMA_GROUPS += ["%s%d" % (n, t) for t in range(4) for n in ("twa", "twb", "ry", "fxa", "fxb")]
+_ARRIVE = ["aT0", "aT1", "aS", "aoS", "aoT0", "aoT1"] + ["%s%d" % (n, t) for t in range(3) for n in ("aa", "ab", "ao", "an")]
 SEMAPHORES = ["ev", "es", "ep", "eg"] + _DMA_GROUPS + _ARRIVE + ["s" + n for n in _ARRIVE]
 ENGSEM = {"v": "ev", "s": "es", "p": "ep", "g": "eg"}
 
@@ -45,6 +47,10 @@ def R(name, c0=None, c1=None, st=1, p0=0, p1=128, ps=1):
     if c0 is None:
         c0, c1 = 0, SCRATCH[name][1][1]
     return (name, p0, p1, ps, c0, c1, st)
+
+
+def part3(name, pattern, k=None):
+    return (name, 0, 128, 1, k or 0, 4 if k is None else k + 1, 1, pattern)
 
 
 def DR(name, k0=0, k1=8, r0=0, r1=128):
@@ -75,6 +81,8 @@ def rank_program(g, core, T, topo):
             return ap(x[1]).indirect(ap(x[2]))
         if x[0] == "raw":
             return x[1]
+        if len(x) == 8:
+            return x[7]
         nm, p0, p1, ps, c0, c1, st = x
         if SCRATCH[nm][0] == "dram":
             return T[nm][p0, c0:c1, :] if p1 == p0 + 1 else T[nm][p0:p1, c0:c1, :]
@@ -166,26 +174,23 @@ def rank_program(g, core, T, topo):
         add("x", None, lands, [], name, count)
 
     nxt = (rank + 1) % n
-    flip = rank == 0
+
+    def crossed(t):
+        return int(rank < t)
+
     wide = len(topo.engines(core, cores[nxt]))
     w6 = wide // 8
     others = [(rank + d) % n for d in range(1, n)]
     pieces = [(d, w) for d in others for w in range(2)]
     spans = [x for x in ((0, rank), (rank + 1, rank + n), (rank + n + 1, 2 * n)) if x[0] < x[1]]
 
-    def exchange(name, src, land):
-        send(name, [(d, DR(src, d + n * w, d + n * w + 1), DR(land, rank + n * w, rank + n * w + 1)) for d, w in pieces], w6)
+    def exchange(name, src, land, x):
+        send(name, [(d, DR(src, d + n * (w ^ x), d + n * (w ^ x) + 1), DR(land, rank + n * w, rank + n * w + 1)) for d, w in pieces], w6)
         arrive(name, [DR(land, d + n * w, d + n * w + 1) for d, w in pieces], 6 * w6)
 
-    def hand(o, a, group):
-        for w in range(2):
-            dma(R(o[0], o[4], o[5], 1, 64 * w, 64 * w + 64), R(a[0], a[4], a[5], 1, 64 - 64 * w, 128 - 64 * w), group)
-
-    def pass_on(name, src, land, final, group, after=()):
-        send(name, [(nxt, src, land if nxt == 0 else final)], wide, after)
-        arrive(name, [land if flip else final], wide)
-        if flip:
-            hand(final, land, group)
+    def pass_on(name, src, land):
+        send(name, [(nxt, src, land)], wide)
+        arrive(name, [land], wide)
 
     def col(k):
         return R("CF", k, k + 1)
@@ -202,7 +207,7 @@ def rank_program(g, core, T, topo):
     for w in range(2):
         dma(quarters("SR", 256 * rank, 256, w), rows(T.sec, rank, w), "ownS", "ys"[w])
         dma(quarters("TL", 768, 256, w), rows(T.tel, rank, w), "ownT", "ys"[w])
-    P15, PG, PQ, P3, PH, P2, P7, B3, C32, P316, LC, WP, Q1K, LNC, W0, RT = 0, 1, 2, 3, 4, 5, 6, 7, 8, 9, 10, 11, 12, 14, 16, 18
+    P15, PG, PQ, P3, PH, P2, P7, B3, C32, P24, LC, WP, Q1K, LNC, W0, MC = 0, 1, 2, 3, 4, 5, 6, 7, 8, 9, 10, 11, 12, 14, 16, 18
     EQ0, NE0 = ALU.is_equal, ALU.not_equal
     one, onef = R("ONES", 0, 128), R("ONEF")
     ms(R("ONES"), 1.0)
@@ -236,23 +241,23 @@ def rank_program(g, core, T, topo):
 
     pc = R("CI", 8, 9)
     sh, an = ALU.arith_shift_right, ALU.bitwise_and
-    L1, L2, EL, FL, L3 = R("CL", 0, 32), R("CL", 32, 64), R("CL", 64, 96), R("CL", 96, 104), R("CL", 128, 160)
-    ms(col(W0), 2.0 ** 62)
+    L1, L2, L3, FL = R("CL", 0, 32), R("CL", 32, 64), R("CL", 64, 96), R("CL", 96, 104)
+    ms(col(W0), 2.0 ** 61)
     for k, a, b in ((P15, 0, 15), (PG, 4, 7), (PQ, 4, 3), (P3, 0, 3), (PH, 2, 31), (P2, 2, 3), (P7, 0, 7), (B3, 3, 1)):
         ts(R("CI", k, k + 1), pc, a, sh, b, an)
     act(col(LNC + 1), col(W0), ACT.Ln)
     ms(R("WT", 0, 128), math.exp(-4 * LG))
     ms(R("WT", 128, 256), 0.0)
     cp(R("CF", 0, 8), R("CI", 0, 8))
-    ts(col(W0 + 1), col(W0), 2.0 ** 62 * math.exp(4 * LG), ALU.mult)
+    ts(col(W0 + 1), col(W0), 2.0 ** 61 * math.exp(4 * LG), ALU.mult)
     ms(R("CR", p1=33), 0.0)
     ts(col(C32), col(P15), 32.0, ALU.mult)
-    ts(col(P316), col(P3), 16.0, ALU.mult)
+    ts(col(P24), col(P2), 4.0, ALU.mult)
+    for k in range(4):
+        ts(col(MC + k), col(P3), float(k), ALU.is_equal)
     for par in range(2):
         ts(col(Q1K + par), col(PQ), -1024.0, ALU.mult, -float(par), ALU.add)
     ts(col(LC), col(P7), 32.0, ALU.mult, col(B3), ALU.add)
-    for t in range(RO):
-        ts(col(RT + t), col(P15), float(t), ALU.is_equal)
     scan(R("WT", 256, 384), R("WT", 0, 128), R("WT", 128, 256), ALU.mult, ALU.add, col(W0 + 1))
     for rl in range(2):
         ms(R("CR", 256 * rl, 256 * rl + 128, 1, 32, 33), -1.0)
@@ -265,43 +270,37 @@ def rank_program(g, core, T, topo):
     total(col(WP), R("WT", 0, 128))
     ms(R("TINY", p1=1), math.exp(LW0 - 512 * LG))
     ms(R("THR", 128, 256, p1=1), -960.0)
-    ts(col(LNC), col(LNC + 1), -2.0, ALU.mult, -0.448 * LG, ALU.add)
+    ts(col(LNC), col(LNC + 1), -2.0, ALU.mult, -0.453 * LG, ALU.add)
     for h in range(2):
         entries(h)
         hand_out("aT%d" % h, "TE", "TR", 512 * h, 128)
     by_groups("SD", 0, "SR", 0, 256, "rawS")
     for h in range(2):
         by_groups("TD0", 512 * h, "TR", 512 * h, 128, "rawT%d" % h)
-    iota(R("EM"), [[0, 16], [1, 4], [0, 4]])
-    iota(R("TMPF", 96, 104), [[16, 4], [4, 2]])
-    iota(R("TMPF", 104, 136), [[136, 2], [64, 2], [1, 8]])
+    iota(R("TMPF", 96, 104), [[1, 4], [16, 2]])
     ts(R("LQ", 0, 256, 4), R("ONEF", 0, 64), col(LNC), ALU.mult)
     ts(L2, R("TMPF", 64, 96), col(C32), ALU.add)
     ts(R("RHS", 384, 416), R("TMPF", 64, 96), col(PH), ALU.is_equal)
-    ts(R("BO"), R("TMPB"), col(PG), ALU.is_equal)
+    ts(R("BO", 0, 128), R("TMPB"), col(PG), ALU.is_equal)
     for k, val in enumerate((0.0, 1.0, 1.0, -2.0 / LG)):
         ms(R("RMQ", k, 256, 4), val)
-    ms(R("CZ"), 0.0)
-    for o, sc in ((R("NEG"), -1.0), (R("IDF"), 1.0), (R("HIR", 0, 128), 1.0), (R("HIR", 128, 256), -32.0), (R("NEF"), -1.0)):
+    ms(R("TOROW", 0, 2064), 0.0)
+    for o, sc in ((R("NEG"), -1.0), (R("IDF", 0, 128), 1.0), (R("HIR", 0, 128), 1.0), (R("HIR", 128, 256), -32.0), (R("NEF"), -1.0)):
         act(o, R("IDB"), ACT.Copy, None, sc)
-    for t in range(RO):
-        act(R("NT", 128 * t, 128 * t + 128), R("NEG"), ACT.Copy, None, col(RT + t))
     for k in range(2):
-        act(R("OWNR", 128 * k, 128 * k + 128), R("BO"), ACT.Copy, None, -4096.0)
+        act(R("OWNR", 128 * k, 128 * k + 128), R("BO", 0, 128), ACT.Copy, None, -4096.0)
         act(R("SUMR", 8 * k, 8 * k + 8), R("BO", 0, 128, 16), ACT.Copy, None, 4096.0)
-    act(R("BO2"), R("BO"), ACT.Copy, None, 256.0)
+    act(R("BO2"), R("BO", 0, 128), ACT.Copy, None, 256.0)
     for dg, sc in enumerate(((64, 64, 4), (32, 16, 1), (2, 1, 0), (1, 512, 32))):
         for k in range(3):
             act(R("RHS", 96 * dg + 32 * k, 96 * dg + 32 * k + 32), R("RHS", 384, 416), ACT.Copy, None, float(sc[k]))
     for i in range(NV, 16):
         ms(R("OWNR", i, 256, 16), 0.0)
-    ts(R("EM"), R("EM"), col(P3), ALU.is_equal)
-    ts(FL, R("TMPF", 96, 104), col(P2), ALU.add)
-    ts(EL, R("TMPF", 104, 136), col(P316), ALU.add)
+    ts(FL, R("TMPF", 96, 104), col(P24), ALU.add)
     for rl in range(2):
         iota(R("CR", 256 * rl, 256 * rl + 128, p1=1), [[0, 8], [-256, 16]], 256 * 15 - 128)
         iota(R("CR", 256 * rl + 128, 256 * rl + 256, p1=1), [[0, 8], [-256, 16]], 256 * 31)
-    pick(R("RM16"), R("ONES"), [[0, 32], [1, 16]], ALU.is_gt, 0, 0)
+    pick(R("RM16"), R("ONES", 0, 256), [[0, 16], [1, 16]], ALU.is_gt, 0, 0)
     pick(R("THR", 0, 128, p1=1), R("THR", 128, 256, p1=1), [[0, 8], [-1, 4], [1, 4]], EQ0, 0, 0)
     iota(R("STAB"), [[0, 32], [16, 4]])
     iota(R("FB", 0, 96), [[0, 96]])
@@ -311,7 +310,7 @@ def rank_program(g, core, T, topo):
     pick(R("L0"), R("LS"), [[1, 128]], NE0, 0, -1, -1024.0)
     iota(R("IOT"), [[1, 192]], -64)
     pick(R("RM4"), one, [[0, 32], [1, 4]], ALU.is_gt, 0, 0)
-    for nm in (("IF", "IZ") if nxt == 0 else ("IZ",)):
+    for nm in (("IF", "IZ") if nxt == 0 else ("IZ", "IF")):
         for a in range(2):
             for c in (0, 144):
                 iota(R("%s%d" % (nm, a), c, c + 16), [[0, 16]])
@@ -319,31 +318,40 @@ def rank_program(g, core, T, topo):
                 pick(R("%s%d" % (nm, a), 16 + 64 * w, 80 + 64 * w), R("ONEF", 0, 64), [[-32, 2], [-272, 2], [-1, 16]], EQ0,
                      256 * a - 64 * (1 - w if nm == "IF" else w))
     iota(R("ZQ", 0, 256, 4), [[0, 64]])
+    iota(R("WW", 256, 512), [[0, 256]], -1)
     for s in range(4):
         pick(R("SELF", 128 * s, 128 * s + 128), onef, [[-64, 2], [0, 4], [-1, 16]], EQ0, -16 * s)
     iota(R("IDN", 0, 512), [[2, 512]])
+    pick(R("TOROW", 15, 2063, 16), one, [[-1, 16], [-16, 8]], EQ0)
     for s in range(4):
         pick(R("SEL", 128 * s, 128 * s + 128), one, [[-64, 2], [0, 4], [-1, 16]], EQ0, -16 * s)
+    if crossed(RO - 1):
+        iota(R("TOROW", 2064, 4128), [[0, 2064]])
+        pick(R("TOROW", 2064 + 15, 2064 + 2063, 16), one, [[-1, 16], [64, 2], [-16, 4]], EQ0, -64)
+        iota(R("TMPB", 0, 128), [[0, 128]], -32)
+        for o, a in ((R("IDF", 128, 256), onef), (R("HIR", 256, 384), one), (R("HIR", 384, 512), R("TMPB"))):
+            pick(o, a, [[64, 2], [-1, 64]], EQ0, -64)
+        pick(R("BO", 128, 256), one, [[64, 2], [-16, 4], [0, 16]], ALU.is_ge, -64)
+        pick(R("BO", 128, 256), R("BO", 128, 256), [[-64, 2], [16, 4], [0, 16]], ALU.is_ge, 79, -1)
 
-    def PM(a, b, nm="IZ"):
+    def PM(a, b, x):
         o = 16 + 16 * (a - b)
-        return R("%s%d" % (nm, a), o, o + 128)
+        return R("%s%d" % ("IF" if x else "IZ", a), o, o + 128)
 
-    def spread(src, banks, ranks):
-        for s in ranks:
-            mm(R(banks[s]), R("SEL", 128 * s, 128 * s + 128), src, True, True)
+    def spread(bank, c, s, src):
+        mm(R(bank, c, c + (src[5] - src[4] + 1) // 2), R("SEL", 128 * s, 128 * s + 128), src, True, True)
 
-    def fill(sw, par, s, bank, engine):
-        o = R(sw, 1024 * s + par, 1024 * s + 1024, 2)
+    def fill(sw, c, src, engine):
+        o = R(sw, c, c - 1 + 2 * (src[5] - src[4]), 2)
         if engine == "v":
-            cp(o, R(bank))
+            cp(o, src)
         else:
-            act(o, R(bank), ACT.Copy)
+            act(o, src, ACT.Copy)
 
-    def window(td, tw, par, group):
+    def window(td, tw, par, group, x):
         for w in range(2):
             for s in range(4):
-                src = R(td, 512 * par, 512 * par + 512, 1, 64 * w + 16 * s, 64 * w + 16 * s + 16)
+                src = R(td, 512 * par, 512 * par + 512, 1, 64 * (w ^ x) + 16 * s, 64 * (w ^ x) + 16 * s + 16)
                 for q in range(4):
                     c = 1024 * s + 512 * par
                     dma(R(tw, c, c + 512, 1, 64 * w + 16 * q, 64 * w + 16 * q + 16), src, group)
@@ -354,16 +362,16 @@ def rank_program(g, core, T, topo):
         return [lambda: ts(x, new, 4096.0, ALU.is_lt, 8192.0, ALU.mult), lambda: tt(y, old, x, ALU.add),
                 lambda: tt(out, y, new, ALU.min)]
 
-    def row(td, h, t, s0):
-        return R(td, 512 * h, 512 * h + 512, 1, 16 * s0 + t, 128, 32)
-
-    def spread_row(nm, h, s0):
-        return R(nm, 32 * h, 32 * h + 32, 1, s0, 128, 2)
-
-    def old_row(td, t):
-        for h in range(2):
+    def row_pieces(td, t, nm, h):
+        x = crossed(t)
+        for w0, w1 in ((0, 64), (64, 128)) if x else ((0, 128),):
             for s0 in range(2):
-                dma(spread_row("RY", h, s0), row(td, h, t, s0), "ry%d" % t)
+                yield (R(td, 512 * h, 512 * h + 512, 1, (w0 ^ 64 * x) + 16 * s0 + t, (w0 ^ 64 * x) + w1 - w0, 32),
+                       R(nm, 32 * h + 16 * s0, 32 * h + 16 * s0 + 16, 1, w0, w1))
+
+    def old_row(td, t, h):
+        for a, b in row_pieces(td, t, "RY", h):
+            dma(b, a, "ry%d" % t)
 
     eight = ["K0", "K1", "D0", "D1", "ZN", "PA", "PB", "TS"]
     for k in range(16):
@@ -383,9 +391,8 @@ def rank_program(g, core, T, topo):
     sd = [R("SD", 0, 1024, 2), R("SD", 1, 1024, 2)]
 
     for h in range(2):
-        window("TD0", "TW0", h, "tw%s0" % "ab"[h])
-    old_row("TD0", 0)
-    later = {}
+        old_row("TD0", 0, h)
+        window("TD0", "TW0", h, "tw%s0" % "ab"[h], 0)
 
     for t in range(RO):
         par, npar, last = t % 2, 1 - t % 2, t == RO - 1
@@ -395,6 +402,8 @@ def rank_program(g, core, T, topo):
         off, offn = "OFF%d" % t, "OFF%d" % (t + 1)
         own = sd[par]
         win = R(sw)
+        x = crossed(t)
+        idf = R("IDF", 128 * x, 128 * x + 128)
         tpar = R(td, 512 * par, 512 * par + 512)
         tnp = R(td, 512 * npar, 512 * npar + 512)
 
@@ -411,101 +420,119 @@ def rank_program(g, core, T, topo):
             mm(kcol(r, 0, 256), R("SD", par + 2 * r, 1024, 8), R("OWNR"), False, False)
         for k in range(2):
             mm(R("D%d" % ((NV + k) % 2)), R("NEG"), own, True, False)
-        vrows = list(range(NV))
+        vrows = sorted(range(NV), key=lambda i: i == t - 1)
         srows = list(range(NV, 16))
-        ev, clock = [], 0
-        for k, i in enumerate(vrows):
-            clock += 860
-            ev.append((clock, "v", i))
-            ev.append((clock + 1, "l", k))
-            clock += 110 * len(later.get(k, []))
+        ev = [(GATHER * (k + 1), "v", i) for k, i in enumerate(vrows)] + [(GATHER * NV + PASS, "r", srows[-1])]
         clock = 0
-        for m, i in enumerate(srows):
-            clock += 860
-            ev.append((clock, "g", i))
+        for m, i in enumerate(srows[:-1]):
+            for j in srows[-2:] if i == srows[-2] else [i]:
+                clock += GATHER
+                ev.append((clock, "g", j))
             if m > 0:
-                clock += 540
+                clock += PASS
                 ev.append((clock, "r", srows[m - 1]))
-            if m == 3:
-                clock += 540
-                ev.append((clock, "h", 0))
-        ev.append((clock + 600, "r", srows[-1]))
+            if i == srows[-2]:
+                ev.append((clock + PASS, "r", i))
+            if m == HIAT:
+                clock += PASS
+                ev += [(clock, "h", 0)] + [(clock + GATHER * k // 2 + 1, "d", k) for k in range(4)]
         ev.sort()
-        lastsum = [e for e in ev if e[1] in "vr"][-1]
         for e in ev:
             i = e[2]
             mi = R("M", 512 * i, 512 * i + 512)
-            oi = R(off, 32 * i, 32 * i + 32)
+            oi = R("OFT", 32 * t, 32 * t + 32) if i == t - 1 else R(off, 32 * i, 32 * i + 32)
+            got, bank = (R("GC"), R("PB")) if i == 15 else (R("G%d" % (i % 2)), R("D%d" % (i % 2)))
             if e[1] == "v":
                 tt(mi, ind(win, oi), own, ALU.max)
-                sums(i, e == lastsum)
+                sums(i, False)
             elif e[1] == "g":
-                act(R("G%d" % (i % 2)), ind(win, oi), ACT.Copy)
-                mm(R("D%d" % (i % 2)), R("IDB"), R("G%d" % (i % 2)), False, True)
+                act(got, ind(win, oi), ACT.Copy)
+                mm(bank, R("IDB"), got, False, True)
             elif e[1] == "r":
-                act(mi, R("D%d" % (i % 2)), ACT.Relu)
-                sums(i, e == lastsum)
-                if i + 2 < 16:
-                    mm(R("D%d" % (i % 2)), R("NEG"), own, True, False)
+                act(mi, bank, ACT.Relu)
+                sums(i, i == srows[-1])
+                if i + 2 < 15:
+                    mm(bank, R("NEG"), own, True, False)
+                if i == NV:
+                    mm(R("PB"), R("NEG"), own, True, False)
             elif e[1] == "h":
                 act(R("HI"), tpar, ACT.Identity, 129 - 0.484375, 1.0 / 32)
-                for r in range(4):
-                    mm(kcol(r, 128, 256), R(td, 512 * par + r, 512 * par + 512, 4), R("IDF"), False, False)
-                    mm(kcol(r, 0, 256), R("HI", r, 512, 4), R("HIR"), False, False)
             else:
-                for fn in later.get(i, []):
-                    fn()
+                mm(kcol(i, 128, 256), R(td, 512 * par + i, 512 * par + 512, 4), idf, False, False)
+                mm(kcol(i, 0, 256), R("HI", i, 512, 4), R("HIR", 256 * x, 256 * x + 256), False, False)
+
+        def spread_digits(a, b):
+            for k in range(a, b):
+                ts(part3("EE", T.EE[:, :, 4 * k:4 * k + 4], k), R("DG"), col(MC + k), ALU.mult)
 
         if not last:
             tr(R("TX"), tnp)
-        for k in range(2):
-            scan(R("KS", 512 * k, 512 * k + 512), R("RM16"), R("K%d" % k), ALU.mult, ALU.max)
+        for r in range(4):
+            scan(part3("KS", T.KS[:, :, r], r), R("RM16"), kcol(r, 0, 256), ALU.mult, ALU.max)
         cnt = R("PA", 0, 128)
         one1 = R("ONES", 0, 128, p1=1)
         mm(cnt, one1, R("THR", 0, 128, p1=1), True, False)
         mm(R("ZN"), one1, R("ONES", p1=1), True, False)
-        ts(R("II"), R("KS", 15, 1024, 16), 4095.0, ALU.max)
+        ts(R("II"), part3("KS", T.KS[:, 15:256:16, :]), 4095.0, ALU.max)
         for r in range(4):
-            act(R("ZP", 128 * r, 128 * r + 128), kcol(r, 0, 128), ACT.Sign, 4095.5, -1.0)
+            for w in range(1 + x):
+                a, c = 128 >> x, 128 * r + 64 * (w ^ x)
+                act(R("ZP", c, c + a), kcol(r, 64 * w, 64 * w + a), ACT.Sign, 4095.5, -1.0)
         if not last:
             act(R("TG"), ind(R("TX"), L2), ACT.Copy)
-        ts(R("DG", 256, 320), R("II"), 1, sh, 112, an)
-        ts(R("DG", 192, 256), R("II"), 1, an)
-        ts(R("DG", 64, 128), R("II"), 31, an)
-        tt(R("FB", 96, 224), ind(R("DG", 256, 320), FL), R("STAB"), ALU.is_equal)
-        ts(R("AB", 128, 192), R("DG", 192, 256), 32.0, ALU.mult)
-        ts(R("DG", 0, 64), R("II"), 1, sh, 48, an)
-        ts(R("DG", 128, 192), R("II"), 1, sh, 15, an)
+        ts(R("DG", 0, 32), R("II", 0, 32), 1, sh, 112, an)
+        ts(R("DG", 96, 128), R("II", 32, 64), 1, an)
+        ts(R("DG", 64, 96), R("II", 32, 64), 1, sh, 15, an)
+        ts(R("DG", 32, 64), R("II", 0, 32), 31, an)
+        tt(R("FB", 96, 224), ind(R("DG", 0, 32), FL), R("STAB"), ALU.is_equal)
+        ts(R("AB", 64, 96), R("DG", 96, 128), 32.0, ALU.mult)
+        tt(R("AB", 0, 32), R("DG", 0, 32), R("DG", 64, 96), ALU.add)
+        spread_digits(0, 1)
         mm(cnt, R("L0"), R("FB", 96, 224), False, False)
         for k in range(1, 4):
             mm(cnt, R("LI"), R("FB", 96 - 32 * k, 224 - 32 * k), False, False)
             mm(cnt, R("LS"), R("FB", 96 + 32 * k, 224 + 32 * k), False, k == 3)
-        tt(R("AB", 64, 120), R("DG", 64, 120), R("AB", 136, 192), ALU.add)
-        tt(R("AB", 0, 56), R("DG", 0, 56), R("DG", 136, 192), ALU.add)
-        tt(R("EE", 0, 256), ind(R("DG", 0, 256), R("CL", 64, 80)), R("EM"), ALU.mult)
-        byV = list(range(2 * NB, 32))
+        tt(R("AB", 32, 64), R("DG", 32, 64), R("AB", 64, 96), ALU.add)
 
-        def bcol(k):
-            c = 64 + 16 * (k // 8) + 4 * (k % 2) + k // 2 % 4
+        def digit(k, c0):
+            c = c0 + 16 * (k % 2) + 4 * (k // 2 % 4) + k // 8
             return R("AB", c, c + 1)
 
-        def step(blk):
-            return math.exp(-LG * (blk // 4))
+        def weight(k, c0=3, st=4):
+            c = c0 + st * (8 * (k // 8) + 4 * (k % 2) + k // 2 % 4)
+            return R("TH", c, c + 1)
 
-        def onehot(ks):
+        def rows_of(ks):
             for k in ks:
-                ts(R("BB", 64 * k, 64 * k + 64), R("IOT", 64, 128), bcol(k), ALU.is_equal, step(k // 2), ALU.mult)
+                ts(R("AA", 128 * k, 128 * k + 128), R("IOT", 64 - 64 * (k % 2), 192 - 64 * (k % 2)), digit(k, 0), ALU.is_equal,
+                   math.exp(-LG * (k // 8)), ALU.mult)
 
+        def columns_of(ks):
+            for k in ks:
+                o = R("BB", 64 * k, 64 * k + 64)
+                if k < 2 * NB:
+                    act(o, R("BX", 64 * k, 64 * k + 64), ACT.Relu, weight(k), weight(k, 128, 1))
+                else:
+                    ts(o, R("IOT", 64, 128), digit(k, 32), ALU.is_equal, weight(k), ALU.mult)
+
+        def distances(ks):
+            for k in ks:
+                act(R("BX", 64 * k, 64 * k + 64), R("IOT", 64, 128), ACT.Abs, digit(k, 32), -1.0)
+
+        distances(range(2 * NB - 4))
+        rows_of(range(0, 9))
         ts(R("OK"), cnt, -961.0, ALU.is_le, col(WP), ALU.mult)
-        onehot(byV[0:3])
-        scan(R("TH"), R("RM4", 0, 128), R("OK"), ALU.mult, ALU.max)
-        onehot(byV[3:])
+        rows_of(range(9, 13))
+        scan(R("TH", 0, 128), R("RM4", 0, 128), R("OK"), ALU.mult, ALU.max)
+        rows_of(range(13, 17))
+        act(R("TH", 128, 160), R("TH", 3, 128, 4), ACT.Copy, None, -1.0)
+        distances(range(2 * NB - 4, 2 * NB))
         for r in range(4):
             mm(R("ZN", r, 512, 4), R("ZP", 128 * r, 128 * r + 128), R("IDB"), False, False)
 
         def lists(b0, s0):
             if not last:
-                mm(R("TS", b0, 512, 2), PM(b0, s0, "IF" if nxt == 0 else "IZ"), R("TG", 256 * s0, 256 * s0 + 256), s0 == 0, s0 == 1)
+                mm(R("TS", b0, 512, 2), PM(b0, s0, x ^ (nxt == 0)), R("TG", 256 * s0, 256 * s0 + 256), s0 == 0, s0 == 1)
 
         def ofs(a, b):
             if not last:
@@ -516,53 +543,45 @@ def rank_program(g, core, T, topo):
 
         rb = ["D0", "D1", "K1", "PA"]
 
-        def column_onehots(blks):
-            for blk in blks:
-                if blk < NB:
-                    for k in (2 * blk, 2 * blk + 1):
-                        act(R("BX", 64 * k, 64 * k + 64), R("IOT", 64, 128), ACT.Abs, bcol(k), -1.0)
-                if blk:
-                    c, f = 128 * blk - 128, step(blk - 1)
-                    act(R("BB", c, c + 128), R("BX", c, c + 128), ACT.Relu, f, -f)
+        def products(r):
+            for q in range(4):
+                o, first = R(rb[r], 3 - q, 256, 4), True
+                if (r, q) == (0, 3):
+                    mm(o, one1, R("TINY", p1=1), True, False)
+                    first = False
+                for w in range(2):
+                    k = 8 * r + 2 * q + w
+                    mm(o, R("AA", 128 * k, 128 * k + 128), R("BB", 64 * k, 64 * k + 64), first and w == 0, w == 1)
 
-        column_onehots(range(9))
-        for blk in range(16):
-            r, q = blk // 4, blk % 4
-            o = R(rb[r], 3 - q, 256, 4)
-            if blk == 3:
-                mm(o, one1, R("TINY", p1=1), True, False)
-            for w in range(2):
-                G, k = 4 * w + q, 2 * blk + w
-                c = 16 * r + G
-                th = 4 * (8 * r + G) + 3
-                ts(R("AA", 128 * k, 128 * k + 128), R("IOT", 64 - 64 * w, 192 - 64 * w), R("AB", c, c + 1), ALU.is_equal,
-                   R("TH", th, th + 1), ALU.mult)
-            for w in range(2):
-                k = 2 * blk + w
-                mm(o, R("AA", 128 * k, 128 * k + 128), R("BB", 64 * k, 64 * k + 64), w == 0 and blk != 3, w == 1)
-            if blk == 3:
-                tt(R("EE", 256, 512), ind(R("DG", 0, 256), R("CL", 80, 96)), R("EM"), ALU.mult)
-                act(R("HS"), R(rb[0], 0, 256), ACT.Copy)
-                column_onehots(range(9, NB + 1))
-            if blk == 5:
-                for dg in range(4):
-                    mm(R("PB", 0, 96), R("EE", 128 * dg, 128 * dg + 128), R("RHS", 96 * dg, 96 * dg + 96), dg == 0, dg == 3)
-            if blk == 9:
-                cp(R("CU"), R("PB", 0, 96))
-            if blk == 11:
-                tt(R("HS"), R(rb[1], 0, 256), R("HS"), ALU.max)
-            if blk == 14:
-                tt(R("HS"), R(rb[2], 0, 256), R("HS"), ALU.max)
-            if blk in (3, 7):
-                lists(1, blk // 4)
-        act(R("DD"), ind(R(tw), R("CU", 32, 64)), ACT.Copy)
-        act(R("GC"), ind(win, R("CU", 0, 32)), ACT.Identity, -256.0)
-        ofs(256, 512)
-        tt(R("HS"), R(rb[3], 0, 256), R("HS"), ALU.max)
+        def larger(r):
+            tt(R("HS"), R(rb[r], 0, 256), R("HS"), ALU.max)
+
+        rows_of(range(17, 32))
+        columns_of(range(0, 8))
+        products(0)
+        columns_of(range(2 * NB, 32))
+        columns_of(range(8, 16))
+        act(R("HS"), R(rb[0], 0, 256), ACT.Copy)
+        products(1)
+        products(3)
+        lists(1, 0)
+        columns_of(range(16, 2 * NB))
+        spread_digits(1, 2)
+        larger(1)
+        spread_digits(2, 3)
+        products(2)
+        larger(3)
+        spread_digits(3, 4)
+        for dg in range(4):
+            mm(R("PB", 0, 96), part3("EE", T.EE[:, 8 * dg:8 * dg + 8, :]), R("RHS", 96 * dg, 96 * dg + 96), dg == 0, dg == 3)
+        lists(1, 1)
         mm(R("K0"), R("NEF"), tpar, True, False)
-        mm(R("K0"), R("IDF"), R("DD"), False, True)
+        larger(2)
         for qq in range(1, 4):
             ts(R("ZQ", qq, 256, 4), R("HS", qq, 256, 4), 0.0, ALU.is_equal)
+        ts(R("CU"), R("PB", 0, 96), 4095.0, ALU.min)
+        act(R("GC"), ind(win, R("CU", 0, 32)), ACT.Identity, -256.0)
+        mm(R("PA"), R("IDB"), R("GC"), True, False)
         scan(R("H2"), R("ZQ"), R("HS"), ALU.mult, ALU.add)
         scan(R("Q2"), R("ONES", 0, 256), R("ZQ"), ALU.add, ALU.mult)
         hs = R("H2", 3, 256, 4)
@@ -571,105 +590,126 @@ def rank_program(g, core, T, topo):
         for k in range(2):
             act(R("LQ", 1 + k, 256, 4), R("XY", 64 * k, 64 * k + 64), ACT.Ln)
         ts(R("LQ", 3, 256, 4), R("Q2", 3, 256, 4), 1024.0, ALU.mult, EVEN, ALU.add)
-        ofs(128, 256)
+        act(R("DD"), ind(R(tw), R("CU", 32, 64)), ACT.Copy)
+        ofs(0, 256)
         scan(R("T1"), R("RMQ"), R("LQ"), ALU.mult, ALU.add)
-        ts(R("FF"), R("T1", 3, 256, 4), -EVEN, ALU.add, float(par), ALU.add)
+        ofs(256, 384)
         ts(R("FU"), R("T1", 3, 256, 4), -EVEN, ALU.add, float(par), ALU.add)
-        for s0 in range(2):
-            for h0 in range(2):
-                mm(R("PB", 128 + s0, 192, 2), PM(s0, h0), R("FF", h0, 64, 2), h0 == 0, h0 == 1)
-        for s in range(4):
-            mm(R("PA", 64 * s, 64 * s + 64), R("SELF", 128 * s, 128 * s + 128), R("FF"), True, True)
-        act(R("WW"), R("PA", 0, 256), ACT.Identity, col(Q1K + par))
-        a = 32 * npar
+        ts(R("FF"), R("T1", 3, 256, 4), -EVEN, ALU.add, float(par), ALU.add)
+        ofs(384, 512)
         if not last:
-            new, old = R("FF", a, a + 32), R("TS", 32 * t, 32 * t + 32)
-            if nxt == 0:
-                for h in range(2):
-                    cp(R("X1", 64, 96, 1, 64 * h, 64 * h + 64), R("FF", a, a + 32, 1, 64 - 64 * h, 128 - 64 * h))
-                new = R("X1", 64, 96)
-            lst = row_select(old, new, old, R("X1", 0, 64)) + [lambda: cp(R("OFS", 0, 128), R("TS", 0, 128))]
-        else:
-            lst = [lambda: None] * 4
+            pass_on("ao%d" % t, R("OFS"), R(offn))
 
-        kb, db = ["K1", "D0", "D1", "TS"], ["PA", "K1", "D0", "ZN"]
+        def table():
+            for s in range(4):
+                mm(R("PB", 64 * s, 64 * s + 64), R("SELF", 128 * s, 128 * s + 128), R("FF"), True, True)
+            act(R("WW", 0, 256), R("PB", 0, 256), ACT.Identity, col(Q1K + par))
+
+        def from_caller(h, a, b):
+            part = R("SD", h + 32 * a, 32 * b, 2)
+            tt(part, ind(win, R("FU", 32 * h + a, 32 * h + b)), part, ALU.max)
+
+        def called():
+            ts(R("CB"), R("FF", 32 * par, 32 * par + 32), 4096.0, ALU.is_lt, -1.0, ALU.mult)
+
+        def leave_out():
+            for l in range(16):
+                c = 2064 * x + 128 * l + 15 - t
+                mm(R("ZN", l, 512, 16), R("TOROW", c, c + 128), R("CB"), False, False)
+
+        def connected():
+            tt(R("EQ"), ind(R("WW"), R("CU", 64, 96)), R("IDN"), ALU.is_equal)
+            sums = ((R("PA"), R("BO2")), (R("ZN"), R("BO", 128 * x, 128 * x + 128)))
+            for bank, ones in sums[::-1] if last else sums:
+                mm(bank, ones, R("EQ"), False, True)
+
         sel = row_select(R("RN"), R("FY"), R("RY"), R("Y1"))
-        if nxt or last:
-            lst.pop(0)()
-        tt(sd[npar], ind(win, R("FU", a, a + 32)), sd[npar], ALU.max)
-        mm(R("PA"), R("IDB"), R("GC"), True, False)
+
+        def fixed_row():
+            sel[2]()
+            for h in (npar, par):
+                for a, b in row_pieces(td, t, "RN", h):
+                    dma(a, b, "fx%s%d" % ("ab"[h], t))
+
         if not last:
-            spread(sd[npar], kb, (0, 1, 2))
-            fill(swn, npar, 0, kb[0], "s")
-        lst.pop(0)()
-        tr(R("FY"), R("PB", 128, 192))
-        lst.pop(0)()
-        sel[0]()
-        ts(R("CB"), R("FY", 32 * par, 32 * par + 32), 4096.0, ALU.is_lt)
-        lst.pop(0)()
-        sel[1]()
-        for fn in lst:
-            fn()
-        if not last:
-            send("ao%d" % t, [(nxt, R("OFS"), R(offn))], wide)
-            arrive("ao%d" % t, [R(offn)], wide)
-            spread(sd[npar], kb, (3,))
-        for s0 in range(2):
-            dma(R("CZ", 0, 512, 1, 16 * s0 + t, 128, 32), R("CB", 0, 32, 1, s0, 128, 2), "cz%d" % t)
-        sel[2]()
-        for h in (npar, par):
-            for s0 in range(2):
-                dma(row(td, h, t, s0), spread_row("RN", h, s0), "fx%s%d" % ("ab"[h], t))
-        if not last:
-            pass_on("aa%d" % t, tnp, R("LT", 1024 * t, 1024 * t + 512), R(tdn, 512 * npar, 512 * npar + 512), "cpa%d" % t)
-        tt(R("EQ"), ind(R("WW"), R("CU", 64, 96)), R("IDN"), ALU.is_equal)
-        if not last:
-            mm(R("PA"), R("BO2"), R("EQ"), False, True)
-        mm(R("ZN"), R("BO"), R("EQ"), False, False)
-        mm(R("ZN"), R("NT", 128 * t, 128 * t + 128), R("CZ"), False, True)
-        if last:
-            mm(R("PA"), R("BO2"), R("EQ"), False, True)
-        tt(own, ind(win, R("FU", 32 * par, 32 * par + 32)), own, ALU.max)
-        if not last:
-            for s in (1, 2):
-                fill(swn, npar, s, kb[s], "s")
-        act(R("MK"), R("ZN"), ACT.Relu, -2.0)
-        if not last:
-            tt(own, R("PA"), own, ALU.max)
-            fill(swn, npar, 3, kb[3], "s")
-            spread(own, db, range(4))
+            table()
+            mm(R("K0", 0, 256), idf, R("DD", 0, 256), False, False)
+            a, kb = 32 * npar, ["K1", "D0", "D1", "PB"]
+            from_caller(npar, 0, 16)
+            tr(R("FY"), R("FF"))
+            called()
+            from_caller(npar, 16, 24)
+            sel[0]()
+            from_caller(npar, 24, 32)
+            sel[1]()
+            leave_out()
+            for s in range(3):
+                spread(kb[s], 0, s, sd[npar])
+            fill(swn, npar, R(kb[0]), "s")
+            connected()
+            spread(kb[3], 0, 3, sd[npar])
+            mm(R("K0", 256, 512), idf, R("DD", 256, 512), False, True)
+            fixed_row()
+            fill(swn, npar + 1024, R(kb[1]), "s")
+            pass_on("aa%d" % t, tnp, R(tdn, 512 * npar, 512 * npar + 512))
+            from_caller(par, 0, 24)
+            tr(R("X1"), R("RN", a, a + 32))
+            from_caller(par, 24, 32)
+            for w0, w1 in ((0, 64), (64, 128)) if nxt == 0 else ((0, 128),):
+                c = w0 ^ 64 * (nxt == 0)
+                cp(R("OFT", 0, 32, 1, c, c + w1 - w0), R("X1", 0, 32, 1, w0, w1))
+            act(R("MK"), R("ZN"), ACT.Relu, -2.0)
+            for s in (2, 3):
+                fill(swn, npar + 1024 * s, R(kb[s]), "s")
+            db = [["D0", "K1"], ["ZN", "PA"]]
+            for h in range(2):
+                part = R("SD", par + 512 * h, 512 * h + 512, 2)
+                tt(part, R("PA", 256 * h, 256 * h + 256), part, ALU.max)
+                for s in range(4):
+                    spread(db[h][s // 2], 256 * (s % 2), s, part)
             tt(R("TB"), R("K0"), R("MK"), ALU.mult)
-            fill(swn, par, 0, db[0], "v")
-            for s in (1, 2):
-                fill(swn, par, s, db[s], "s")
-            fill(swn, par, 3, db[3], "v")
-            if not flip:
-                window(tdn, twn, npar, "twa%d" % (t + 1))
-            pass_on("ab%d" % t, [R("TB"), tpar], R("LT", 1024 * t + 512, 1024 * t + 1024), R(tdn, 512 * par, 512 * par + 512), "cpb%d" % t)
-            if flip:
-                window(tdn, twn, npar, "twa%d" % (t + 1))
-            window(tdn, twn, par, "twb%d" % (t + 1))
-            old_row(tdn, t + 1)
-            later = {}
+            for h in range(2):
+                for s in range(4):
+                    fill(swn, par + 1024 * s + 512 * h, R(db[h][s // 2], 256 * (s % 2), 256 * (s % 2) + 256), "sv"[s // 2])
+            pass_on("ab%d" % t, [R("TB"), tpar], R(tdn, 512 * par, 512 * par + 512))
+            pass_on("an%d" % t, R("OFT", 0, 32), R("OFT", 32 * t + 32, 32 * t + 64))
+            for h in (npar, par):
+                old_row(tdn, t + 1, h)
+                window(tdn, twn, h, "tw%s%d" % ("ab"[h], t + 1), crossed(t + 1))
             continue
 
+        table()
+        from_caller(npar, 0, 8)
+        tr(R("FY"), R("FF"))
+        called()
+        from_caller(npar, 8, 16)
+        sel[0]()
+        from_caller(npar, 16, 24)
+        sel[1]()
+        from_caller(npar, 24, 32)
+        fixed_row()
+        mm(R("K0"), idf, R("DD"), False, True)
+        leave_out()
+        connected()
+        from_caller(par, 0, 32)
+        act(R("MK"), R("ZN"), ACT.Relu, -2.0)
         act(R("OT", npar, 1024, 2), tnp, ACT.Copy)
-        tt(R("K0"), R("K0"), R("MK"), ALU.mult)
-        parts = (("T0", "OT", 0, 512, T.ytel), ("T1", "OT", 512, 512, T.ytel), ("S", "SD", 0, 1024, T.ysec))
+        parts = (("S", "SD", 0, 1024, T.ysec), ("T0", "OT", 0, 512, T.ytel), ("T1", "OT", 512, 512, T.ytel))
         for nm, src, c, width, y in parts:
             if nm == "S":
                 tt(own, R("PA"), own, ALU.max)
+                tt(R("K0"), R("K0"), R("MK"), ALU.mult)
             else:
                 h = c // 2
                 tt(R("OT", c + par, c + 512, 2), R("K0", h, h + 256), R(td, 512 * par + h, 512 * par + h + 256), ALU.add)
             for k, (k0, k1) in enumerate(spans):
-                dma(DR("o" + nm, k0, k1), R(src, c, c + width, 1, 16 * k0, 16 * k1), "o" + nm, "ys"[k % 2])
+                dma(DR("o" + nm, k0, k1), R(src, c, c + width, 1, 16 * k0, 16 * k1), "o" + nm, "y" if nm == "S" else "ys"[k % 2])
         for nm, src, c, width, y in parts:
-            exchange("ao" + nm, "o" + nm, "lo" + nm)
+            exchange("ao" + nm, "o" + nm, "lo" + nm, x * (nm != "S"))
         for mine in (True, False):
             for nm, src, c, width, y in parts:
                 for k, gg in enumerate(gg for gg in range(8) if (gg % n == rank) == mine):
-                    p0 = 64 * (gg // n) + 16 * rank
+                    p0 = 64 * (gg // n ^ x * (nm != "S")) + 16 * rank
                     a = R(src, c, c + width, 1, p0, p0 + 16) if mine else DR("lo" + nm, gg, gg + 1)
                     dma(("raw", y[16 * gg:16 * gg + 16, c:c + width]), a, "out", "ys"[k % 2])
 

@@ -5,9 +5,9 @@ from concourse.mybir import AluOpType, AxisListType, ActivationFunctionType
 ALU = AluOpType
 ACT = ActivationFunctionType
 NV = 10
-NB = 11
+NB = 10
 GATHER, PASS = 8, 5
-HIAT = 2
+HIAT = 1
 RO = 4
 LG = math.log(1.398)
 LW0 = 122 * math.log(2.0)
@@ -25,16 +25,16 @@ def _decl(where, dtype, **kw):
 _decl("psum", F, K0=512, K1=512, D0=512, D1=512, ZN=512, PA=512, PB=512, TS=512)
 _decl("dram", B, oS=[8, 128, 128], loS=[8, 128, 128])
 _decl("dram", F, oT0=[8, 128, 64], loT0=[8, 128, 64], oT1=[8, 128, 64], loT1=[8, 128, 64])
-_decl("sbuf", I, CI=16, TL=1024, II=64, DG=128)
+_decl("sbuf", I, CI=16, TL=1024, II=64, DG=128, PO=64)
 _decl("sbuf", U, OFF0=512, OFF1=512, OFF2=512, OFF3=512, OFS=512, OFT=128, CL=160, FU=64, CU=96)
-_decl("sbuf", B, SL=1024, SR=1024, SW0=4112, SW1=4112, SD=1024, M=8192, G0=512, G1=512, GC=512, HI=512, IOT=192,
-      IDB=128, NEG=128, HIR=512, SEL=512, SE0=512, SUMR=16, OWNR=256, CR=512, RM16=256, RM4=128, ONES=512, LS=128, LI=128,
-      L0=128, FB=320, RHS=416, BO=256, BO2=128, AA=4096, BB=2048, BX=2048, ZP=512, EQ=512, MK=512, TMPB=128,
+_decl("sbuf", B, SL=1024, SR=1024, SW0=4112, SW1=4112, SD=1024, M=8192, G=1536, GC=512, HI=512, IOT=192,
+      IDB=128, NEG=128, HIR=512, SEL=512, SE0=512, SUMR=16, OWNR=256, RM16=128, RM4=128, ONES=256, LS=128, LI=128,
+      L0=128, FB=320, RHS=512, BO=256, BO2=128, AA=4096, BB=2048, BX=2048, ZP=512, EQ=512, MK=512, TMPB=128,
       THR=256, TINY=64, CB=32, TOROW=4128, EE=[128, 32, 16])
-_decl("sbuf", F, CF=48, TE=1024, TR=1024, TD0=1024, TD1=1024, TD2=1024, TD3=1024, TW0=4096, TW1=4096, ONEF=128, IDF=256,
-      NEF=128, SELF=512, IZ0=160, IZ1=160, IF0=160, IF1=160, WT=384, STAB=128, IDN=512, KS=[128, 256, 4], AB=96, OK=128,
-      TH=160, HS=256, ZQ=256, H2=256, Q2=256, XY=128, LQ=256, RMQ=256, T1=256, FF=64, WW=512, TG=512,
-      TX=512, X1=32, FY=64, RY=64, Y1=128, RN=64, DD=512, TB=512, OT=1024, TMPF=256)
+_decl("sbuf", F, CF=48, TE=1024, TR=1024, TD0=4096, TD1=4096, TD2=4096, TD3=4096, ONEF=128, IDF=256,
+      NEF=128, SELF=512, IZ0=160, IZ1=160, IF0=160, IF1=160, WT=384, STAB=128, IDN=512, KS=[128, 256, 4], AB=128, OK=128,
+      TH=64, HS=256, HT=256, ZQ=256, H2=256, Q2=256, XY=128, LQ=256, RMQ=256, T1=256, FF=64, WW=512, TG=512,
+      TX=512, X1=32, FY=64, RY=64, Y1=192, RN=64, DD=512, TB=512, OT=1024, TMPF=256)
 
 _DMA_GROUPS = ["ldT", "ldS", "ownT", "ownS", "rawT0", "rawT1", "rawS", "oS", "oT0", "oT1", "out"]
 _DMA_GROUPS += ["%s%d" % (n, t) for t in range(4) for n in ("twa", "twb", "ry", "fxa", "fxb")]
@@ -49,8 +49,8 @@ def R(name, c0=None, c1=None, st=1, p0=0, p1=128, ps=1):
     return (name, p0, p1, ps, c0, c1, st)
 
 
-def part3(name, pattern, k=None):
-    return (name, 0, 128, 1, k or 0, 4 if k is None else k + 1, 1, pattern)
+def part3(name, pattern, k0=0, k1=8):
+    return (name, 0, 128, 1, k0, k1, 1, pattern)
 
 
 def DR(name, k0=0, k1=8, r0=0, r1=128):
@@ -207,21 +207,21 @@ def rank_program(g, core, T, topo):
     for w in range(2):
         dma(quarters("SR", 256 * rank, 256, w), rows(T.sec, rank, w), "ownS", "ys"[w])
         dma(quarters("TL", 768, 256, w), rows(T.tel, rank, w), "ownT", "ys"[w])
-    P15, PG, PQ, P3, PH, P2, P7, B3, C32, P24, LC, WP, Q1K, LNC, W0, MC = 0, 1, 2, 3, 4, 5, 6, 7, 8, 9, 10, 11, 12, 14, 16, 18
+    P15, PG, PQ, P3, PH, P2, P7, B3, C32, P24, LC, WP, Q1K, LNC, W0, MC = 0, 1, 2, 3, 4, 5, 6, 7, 8, 9, 10, 22, 12, 14, 16, 18
     EQ0, NE0 = ALU.is_equal, ALU.not_equal
     one, onef = R("ONES", 0, 128), R("ONEF")
     ms(R("ONES"), 1.0)
     ms(onef, 1.0)
     iota(R("CI", 8, 9), [[0, 1]], 0, 1)
     iota(R("TMPF", 0, 32), [[256, 2], [16, 8], [128, 2]])
-    iota(R("TMPF", 32, 64), [[256, 2], [4, 8], [2, 2]])
+    iota(R("TMPF", 32, 48), [[4, 8], [2, 2]])
     pick(R("IDB"), one, [[-1, 128]], EQ0)
     for c in range(2):
         pick(R("SE0", 128 * c, 128 * c + 128), one, [[-64, 2], [0, 4], [-4, 16]], EQ0, -c)
 
-    def hand_out(nm, out, land, c, width):
+    def hand_out(nm, out, land, c, width, after=()):
         send(nm, [(d, R(out, c + width * k, c + width * k + width), R(land, c + width * rank, c + width * rank + width))
-                  for k, d in enumerate(others)], 2 * w6)
+                  for k, d in enumerate(others)], 2 * w6, after)
         arrive(nm, [R(land, c + width * d, c + width * d + width) for d in others], 6 * w6)
 
     def by_groups(out, c, land, lc, width, nm):
@@ -241,7 +241,7 @@ def rank_program(g, core, T, topo):
 
     pc = R("CI", 8, 9)
     sh, an = ALU.arith_shift_right, ALU.bitwise_and
-    L1, L2, L3, FL = R("CL", 0, 32), R("CL", 32, 64), R("CL", 64, 96), R("CL", 96, 104)
+    L1, L2, L3, FL = R("CL", 0, 32), R("CL", 32, 64), R("CL", 64, 80), R("CL", 96, 104)
     ms(col(W0), 2.0 ** 61)
     for k, a, b in ((P15, 0, 15), (PG, 4, 7), (PQ, 4, 3), (P3, 0, 3), (PH, 2, 31), (P2, 2, 3), (P7, 0, 7), (B3, 3, 1)):
         ts(R("CI", k, k + 1), pc, a, sh, b, an)
@@ -250,37 +250,35 @@ def rank_program(g, core, T, topo):
     ms(R("WT", 128, 256), 0.0)
     cp(R("CF", 0, 8), R("CI", 0, 8))
     ts(col(W0 + 1), col(W0), 2.0 ** 61 * math.exp(4 * LG), ALU.mult)
-    ms(R("CR", p1=33), 0.0)
+    ms(R("RM16"), 256.0)
     ts(col(C32), col(P15), 32.0, ALU.mult)
     ts(col(P24), col(P2), 4.0, ALU.mult)
     for k in range(4):
         ts(col(MC + k), col(P3), float(k), ALU.is_equal)
-    for par in range(2):
-        ts(col(Q1K + par), col(PQ), -1024.0, ALU.mult, -float(par), ALU.add)
+    for k in range(2):
+        ts(col(Q1K + k), col(PQ), -1024.0, ALU.mult, -EVEN * k, ALU.add)
     ts(col(LC), col(P7), 32.0, ALU.mult, col(B3), ALU.add)
     scan(R("WT", 256, 384), R("WT", 0, 128), R("WT", 128, 256), ALU.mult, ALU.add, col(W0 + 1))
-    for rl in range(2):
-        ms(R("CR", 256 * rl, 256 * rl + 128, 1, 32, 33), -1.0)
-        ms(R("CR", 256 * rl + 128, 256 * rl + 256, 1, 32, 33), 32.0)
+    ms(R("RM16", 0, 128, 16), -2.0 ** 30)
     ts(L1, R("TMPF", 0, 32), col(P15), ALU.add)
-    ts(L3, R("TMPF", 32, 64), col(LC), ALU.add)
+    ts(L3, R("TMPF", 32, 48), col(LC), ALU.add)
     tt(R("WT", 0, 128), R("WT", 256, 384), R("IDB"), ALU.mult)
     ms(R("SW0", 4096, 4112), 0.0)
     ms(R("SW1", 4096, 4112), 0.0)
     total(col(WP), R("WT", 0, 128))
     ms(R("TINY", p1=1), math.exp(LW0 - 512 * LG))
     ms(R("THR", 128, 256, p1=1), -960.0)
+    ts(col(WP + 1), col(WP), -1.0, ALU.mult)
     ts(col(LNC), col(LNC + 1), -2.0, ALU.mult, -0.453 * LG, ALU.add)
-    for h in range(2):
-        entries(h)
-        hand_out("aT%d" % h, "TE", "TR", 512 * h, 128)
+    entries(0)
+    hand_out("aT0", "TE", "TR", 0, 128)
+    entries(1)
     by_groups("SD", 0, "SR", 0, 256, "rawS")
-    for h in range(2):
-        by_groups("TD0", 512 * h, "TR", 512 * h, 128, "rawT%d" % h)
+    by_groups("TD0", 0, "TR", 0, 128, "rawT0")
     iota(R("TMPF", 96, 104), [[1, 4], [16, 2]])
     ts(R("LQ", 0, 256, 4), R("ONEF", 0, 64), col(LNC), ALU.mult)
     ts(L2, R("TMPF", 64, 96), col(C32), ALU.add)
-    ts(R("RHS", 384, 416), R("TMPF", 64, 96), col(PH), ALU.is_equal)
+    ts(R("RHS", 480, 512), R("TMPF", 64, 96), col(PH), ALU.is_equal)
     ts(R("BO", 0, 128), R("TMPB"), col(PG), ALU.is_equal)
     for k, val in enumerate((0.0, 1.0, 1.0, -2.0 / LG)):
         ms(R("RMQ", k, 256, 4), val)
@@ -291,16 +289,13 @@ def rank_program(g, core, T, topo):
         act(R("OWNR", 128 * k, 128 * k + 128), R("BO", 0, 128), ACT.Copy, None, -4096.0)
         act(R("SUMR", 8 * k, 8 * k + 8), R("BO", 0, 128, 16), ACT.Copy, None, 4096.0)
     act(R("BO2"), R("BO", 0, 128), ACT.Copy, None, 256.0)
-    for dg, sc in enumerate(((64, 64, 4), (32, 16, 1), (2, 1, 0), (1, 512, 32))):
+    DIGITS = (0, 1, 2, 2, 3)
+    for dg, sc in enumerate(((2, 0, 1), (32, 1, 16), (-32, 0, 0), (1 / 32, 0, 0), (62, 4, 63))):
         for k in range(3):
-            act(R("RHS", 96 * dg + 32 * k, 96 * dg + 32 * k + 32), R("RHS", 384, 416), ACT.Copy, None, float(sc[k]))
+            act(R("RHS", 96 * dg + 32 * k, 96 * dg + 32 * k + 32), R("RHS", 480, 512), ACT.Copy, None, float(sc[k]))
     for i in range(NV, 16):
         ms(R("OWNR", i, 256, 16), 0.0)
     ts(FL, R("TMPF", 96, 104), col(P24), ALU.add)
-    for rl in range(2):
-        iota(R("CR", 256 * rl, 256 * rl + 128, p1=1), [[0, 8], [-256, 16]], 256 * 15 - 128)
-        iota(R("CR", 256 * rl + 128, 256 * rl + 256, p1=1), [[0, 8], [-256, 16]], 256 * 31)
-    pick(R("RM16"), R("ONES", 0, 256), [[0, 16], [1, 16]], ALU.is_gt, 0, 0)
     pick(R("THR", 0, 128, p1=1), R("THR", 128, 256, p1=1), [[0, 8], [-1, 4], [1, 4]], EQ0, 0, 0)
     iota(R("STAB"), [[0, 32], [16, 4]])
     iota(R("FB", 0, 96), [[0, 96]])
@@ -317,7 +312,7 @@ def rank_program(g, core, T, topo):
             for w in range(2):
                 pick(R("%s%d" % (nm, a), 16 + 64 * w, 80 + 64 * w), R("ONEF", 0, 64), [[-32, 2], [-272, 2], [-1, 16]], EQ0,
                      256 * a - 64 * (1 - w if nm == "IF" else w))
-    iota(R("ZQ", 0, 256, 4), [[0, 64]])
+    hand_out("aT1", "TE", "TR", 512, 128, [R("SD")])
     iota(R("WW", 256, 512), [[0, 256]], -1)
     for s in range(4):
         pick(R("SELF", 128 * s, 128 * s + 128), onef, [[-64, 2], [0, 4], [-1, 16]], EQ0, -16 * s)
@@ -348,19 +343,13 @@ def rank_program(g, core, T, topo):
         else:
             act(o, src, ACT.Copy)
 
-    def window(td, tw, par, group, x):
+    def window(td, par, group):
         for w in range(2):
             for s in range(4):
-                src = R(td, 512 * par, 512 * par + 512, 1, 64 * (w ^ x) + 16 * s, 64 * (w ^ x) + 16 * s + 16)
-                for q in range(4):
-                    c = 1024 * s + 512 * par
-                    dma(R(tw, c, c + 512, 1, 64 * w + 16 * q, 64 * w + 16 * q + 16), src, group)
-
-    def row_select(out, new, old, tmp):
-        h = (tmp[4] + tmp[5]) // 2
-        x, y = R(tmp[0], tmp[4], h), R(tmp[0], h, tmp[5])
-        return [lambda: ts(x, new, 4096.0, ALU.is_lt, 8192.0, ALU.mult), lambda: tt(y, old, x, ALU.add),
-                lambda: tt(out, y, new, ALU.min)]
+                src = R(td, 512 * par, 512 * par + 512, 1, 64 * w + 16 * s, 64 * w + 16 * s + 16)
+                for k in range(1, 4):
+                    c, q = 1024 * k + 512 * par, (s - k) % 4
+                    dma(R(td, c, c + 512, 1, 64 * w + 16 * q, 64 * w + 16 * q + 16), src, group)
 
     def row_pieces(td, t, nm, h):
         x = crossed(t)
@@ -378,26 +367,32 @@ def rank_program(g, core, T, topo):
         s, c = k // 4, k % 4
         mm(R(eight[k // 2], 256 * (k % 2), 256 * (k % 2) + 256), R("SE0", 128 * c, 128 * c + 128), R("SR", 256 * s, 256 * s + 256),
            True, True)
-    for k in range(8):
+    cp(R("SW0", 512, 1024), R(eight[1]))
+    for k in (0, 2):
         act(R("SW0", 512 * k, 512 * k + 512), R(eight[k]), ACT.Copy)
-    cp(R("TG"), ind(R("TR", 0, 512), L1))
-    tr(R("TX"), R("TG"))
-    cp(R("OFS"), ind(R("TX"), L3))
-    for a in range(2):
-        for w in range(2):
-            for b in range(2):
+    cp(R("TG", 0, 256), ind(R("TR", 0, 512), R("CL", 0, 16)))
+    act(R("TG", 256, 512), ind(R("TR", 0, 512), R("CL", 16, 32)), ACT.Copy)
+    for k in range(3, 8):
+        act(R("SW0", 512 * k, 512 * k + 512), R(eight[k]), ACT.Copy)
+    for h in range(2):
+        tr(R("TX", 256 * h, 256 * h + 256), R("TG", 256 * h, 256 * h + 256))
+    for h in range(2):
+        cp(R("OFS", 256 * h, 256 * h + 256), ind(R("TX", 256 * h, 256 * h + 256), L3))
+    for a in (1, 0):
+        for b in range(2):
+            for w in range(2):
                 cp(R("OFF0", 256 * a, 256 * a + 256, 1, 64 * w + 32 * b, 64 * w + 32 * b + 32),
                    R("OFS", 256 * b, 256 * b + 256, 1, 64 * w + 32 * a, 64 * w + 32 * a + 32))
     sd = [R("SD", 0, 1024, 2), R("SD", 1, 1024, 2)]
 
+    by_groups("TD0", 512, "TR", 512, 128, "rawT1")
     for h in range(2):
         old_row("TD0", 0, h)
-        window("TD0", "TW0", h, "tw%s0" % "ab"[h], 0)
+        window("TD0", h, "tw%s0" % "ab"[h])
 
     for t in range(RO):
         par, npar, last = t % 2, 1 - t % 2, t == RO - 1
         td, tdn = "TD%d" % t, "TD%d" % (t + 1)
-        tw, twn = "TW%d" % par, "TW%d" % npar
         sw, swn = "SW%d" % par, "SW%d" % npar
         off, offn = "OFF%d" % t, "OFF%d" % (t + 1)
         own = sd[par]
@@ -414,80 +409,92 @@ def rank_program(g, core, T, topo):
             for r in range(4):
                 mm(kcol(r, i, 256, 16), R("M", 512 * i + r, 512 * i + 512, 4), R("SUMR"), False, stop and r % 2 == 1)
 
-        for k in range(2):
-            mm(R("K%d" % k), R("ONES", 0, 128, p1=33), R("CR", p1=33), True, False)
-        for r in range(4):
-            mm(kcol(r, 0, 256), R("SD", par + 2 * r, 1024, 8), R("OWNR"), False, False)
-        for k in range(2):
-            mm(R("D%d" % ((NV + k) % 2)), R("NEG"), own, True, False)
-        vrows = sorted(range(NV), key=lambda i: i == t - 1)
+        vrows = sorted(range(NV), key=lambda i: i == t - 1 if t else i < 8)
         srows = list(range(NV, 16))
-        ev = [(GATHER * (k + 1), "v", i) for k, i in enumerate(vrows)] + [(GATHER * NV + PASS, "r", srows[-1])]
-        clock = 0
-        for m, i in enumerate(srows[:-1]):
-            for j in srows[-2:] if i == srows[-2] else [i]:
-                clock += GATHER
-                ev.append((clock, "g", j))
-            if m > 0:
-                clock += PASS
-                ev.append((clock, "r", srows[m - 1]))
-            if i == srows[-2]:
-                ev.append((clock + PASS, "r", i))
-            if m == HIAT:
-                clock += PASS
-                ev += [(clock, "h", 0)] + [(clock + GATHER * k // 2 + 1, "d", k) for k in range(4)]
-        ev.sort()
-        for e in ev:
-            i = e[2]
-            mi = R("M", 512 * i, 512 * i + 512)
-            oi = R("OFT", 32 * t, 32 * t + 32) if i == t - 1 else R(off, 32 * i, 32 * i + 32)
-            got, bank = (R("GC"), R("PB")) if i == 15 else (R("G%d" % (i % 2)), R("D%d" % (i % 2)))
-            if e[1] == "v":
-                tt(mi, ind(win, oi), own, ALU.max)
-                sums(i, False)
-            elif e[1] == "g":
-                act(got, ind(win, oi), ACT.Copy)
-                mm(bank, R("IDB"), got, False, True)
-            elif e[1] == "r":
-                act(mi, bank, ACT.Relu)
-                sums(i, i == srows[-1])
-                if i + 2 < 15:
-                    mm(bank, R("NEG"), own, True, False)
-                if i == NV:
-                    mm(R("PB"), R("NEG"), own, True, False)
-            elif e[1] == "h":
-                act(R("HI"), tpar, ACT.Identity, 129 - 0.484375, 1.0 / 32)
-            else:
-                mm(kcol(i, 128, 256), R(td, 512 * par + i, 512 * par + 512, 4), idf, False, False)
-                mm(kcol(i, 0, 256), R("HI", i, 512, 4), R("HIR", 256 * x, 256 * x + 256), False, False)
+        banks = dict(zip(srows, ("ZN", "PB", "D0", "D1", "TS", "PA")))
 
-        def spread_digits(a, b):
-            for k in range(a, b):
-                ts(part3("EE", T.EE[:, :, 4 * k:4 * k + 4], k), R("DG"), col(MC + k), ALU.mult)
+        def lines(i):
+            return (R("M", 512 * i, 512 * i + 512), R("OFT", 32 * t, 32 * t + 32) if i == t - 1 else R(off, 32 * i, 32 * i + 32),
+                    R("G", 512 * (i % 3), 512 * (i % 3) + 512))
+
+        def by_vector(i):
+            tt(lines(i)[0], ind(win, lines(i)[1]), own, ALU.max)
+            sums(i, False)
+
+        def by_scalar(i):
+            act(lines(i)[2], ind(win, lines(i)[1]), ACT.Copy)
+            mm(R(banks[i]), R("IDB"), lines(i)[2], False, True)
+
+        def positive(i):
+            act(lines(i)[0], R(banks[i]), ACT.Relu)
+            sums(i, i == srows[-1])
+
+        def less_own(i):
+            mm(R(banks[i]), R("NEG"), own, True, False)
+
+        def high(i):
+            act(R("HI"), tpar, ACT.Identity, 129 - 0.484375, 1.0 / 32)
+
+        def entry(r):
+            mm(kcol(r, 128, 256), R(td, 512 * par + r, 512 * par + 512, 4), idf, False, False)
+
+        def entry_high(r):
+            mm(kcol(r, 0, 256), R("HI", r, 512, 4), R("HIR", 256 * x, 256 * x + 256), False, False)
+
+        steps = [(by_scalar, i) for i in srows[:3]]
+        for m, i in enumerate(srows[3:]):
+            steps += [(positive, i - 3)] + [(high, 0)] * (m == HIAT) + [(by_scalar, i)]
+        steps += [(positive, i) for i in srows[-3:]]
+        spare = [(less_own, i) for i in srows[3:]] + [(entry, r) for r in range(4)] + [(entry_high, r) for r in range(4)]
+        for i in srows[:3]:
+            less_own(i)
+        for r in range(4):
+            mm(kcol(r, 0, 256), R("SD", par + 2 * r, 1024, 8), R("OWNR"), r % 2 == 0, False)
+        ev, clock = [(GATHER * (k + 1), k, by_vector, i) for k, i in enumerate(vrows)], 0
+        for k, (fn, i) in enumerate(steps):
+            clock += GATHER if fn is by_scalar else PASS
+            ev.append((clock, 20 + 2 * k, fn, i))
+            if k < len(spare):
+                ev.append((clock, 21 + 2 * k) + spare[k])
+        for e in sorted(ev, key=lambda e: (e[0], e[1] < 20, e[1])):
+            e[2](e[3])
+
+        def spread_digits():
+            for k in range(4):
+                act(part3("EE", T.EE[:, :, 4 * k:4 * k + 4], k, k + 1), R("AB"), ACT.Copy, None, col(MC + k))
 
         if not last:
             tr(R("TX"), tnp)
-        for r in range(4):
-            scan(part3("KS", T.KS[:, :, r], r), R("RM16"), kcol(r, 0, 256), ALU.mult, ALU.max)
+            act(R("TG"), ind(R("TX"), L2), ACT.Copy)
+        for k in range(8):
+            a = 128 * (k // 4)
+            scan(part3("KS", T.KS[:, a:a + 128, k % 4], k, k + 1), R("RM16"), kcol(k % 4, a, a + 128), ALU.add, ALU.max)
+            if k == 6:
+                ts(R("II", 0, 32), part3("KS", T.KS[:, 15:128:16, :], 0, 4), -129.0, ALU.add, 4095.0, ALU.max)
+
+        def lists(*parts):
+            for k in parts if not last else ():
+                h, b0, s0 = k // 4, k // 2 % 2, k % 2
+                mm(R("TS", 256 * h + b0, 256 * h + 256, 2), PM(b0, s0, x ^ (nxt == 0)),
+                   R("TG", 256 * s0 + 128 * h, 256 * s0 + 128 * h + 128), s0 == 0, s0 == 1)
+
+        lists(0, 1, 2)
         cnt = R("PA", 0, 128)
         one1 = R("ONES", 0, 128, p1=1)
         mm(cnt, one1, R("THR", 0, 128, p1=1), True, False)
-        mm(R("ZN"), one1, R("ONES", p1=1), True, False)
-        ts(R("II"), part3("KS", T.KS[:, 15:256:16, :]), 4095.0, ALU.max)
         for r in range(4):
             for w in range(1 + x):
                 a, c = 128 >> x, 128 * r + 64 * (w ^ x)
                 act(R("ZP", c, c + a), kcol(r, 64 * w, 64 * w + a), ACT.Sign, 4095.5, -1.0)
-        if not last:
-            act(R("TG"), ind(R("TX"), L2), ACT.Copy)
         ts(R("DG", 0, 32), R("II", 0, 32), 1, sh, 112, an)
-        ts(R("DG", 96, 128), R("II", 32, 64), 1, an)
-        ts(R("DG", 64, 96), R("II", 32, 64), 1, sh, 15, an)
+        cp(R("II", 32, 64), part3("KS", T.KS[:, 143:256:16, :], 4, 8))
         ts(R("DG", 32, 64), R("II", 0, 32), 31, an)
         tt(R("FB", 96, 224), ind(R("DG", 0, 32), FL), R("STAB"), ALU.is_equal)
+        ts(R("DG", 96, 128), R("II", 32, 64), 1, an)
+        ts(R("DG", 64, 96), R("II", 32, 64), 1, sh, 15, an)
         ts(R("AB", 64, 96), R("DG", 96, 128), 32.0, ALU.mult)
         tt(R("AB", 0, 32), R("DG", 0, 32), R("DG", 64, 96), ALU.add)
-        spread_digits(0, 1)
+        cp(R("AB", 96, 128), R("DG", 0, 32))
         mm(cnt, R("L0"), R("FB", 96, 224), False, False)
         for k in range(1, 4):
             mm(cnt, R("LI"), R("FB", 96 - 32 * k, 224 - 32 * k), False, False)
@@ -498,8 +505,8 @@ def rank_program(g, core, T, topo):
             c = c0 + 16 * (k % 2) + 4 * (k // 2 % 4) + k // 8
             return R("AB", c, c + 1)
 
-        def weight(k, c0=3, st=4):
-            c = c0 + st * (8 * (k // 8) + 4 * (k % 2) + k // 2 % 4)
+        def weight(k, c0=0):
+            c = c0 + 8 * (k // 8) + 4 * (k % 2) + k // 2 % 4
             return R("TH", c, c + 1)
 
         def rows_of(ks):
@@ -511,7 +518,7 @@ def rank_program(g, core, T, topo):
             for k in ks:
                 o = R("BB", 64 * k, 64 * k + 64)
                 if k < 2 * NB:
-                    act(o, R("BX", 64 * k, 64 * k + 64), ACT.Relu, weight(k), weight(k, 128, 1))
+                    act(o, R("BX", 64 * k, 64 * k + 64), ACT.Relu, weight(k), weight(k, 32))
                 else:
                     ts(o, R("IOT", 64, 128), digit(k, 32), ALU.is_equal, weight(k), ALU.mult)
 
@@ -519,27 +526,22 @@ def rank_program(g, core, T, topo):
             for k in ks:
                 act(R("BX", 64 * k, 64 * k + 64), R("IOT", 64, 128), ACT.Abs, digit(k, 32), -1.0)
 
-        distances(range(2 * NB - 4))
-        rows_of(range(0, 9))
-        ts(R("OK"), cnt, -961.0, ALU.is_le, col(WP), ALU.mult)
-        rows_of(range(9, 13))
-        scan(R("TH", 0, 128), R("RM4", 0, 128), R("OK"), ALU.mult, ALU.max)
-        rows_of(range(13, 17))
-        act(R("TH", 128, 160), R("TH", 3, 128, 4), ACT.Copy, None, -1.0)
-        distances(range(2 * NB - 4, 2 * NB))
+        distances(range(10))
+        rows_of(range(0, 7))
+        scan(R("OK"), R("RM4"), cnt, ALU.mult, ALU.min)
+        rows_of(range(7, 12))
+        for k in range(2):
+            ts(R("TH", 32 * k, 32 * k + 32), R("OK", 3, 128, 4), -961.0, ALU.is_le, col(WP + k), ALU.mult)
+        rows_of(range(12, 16))
         for r in range(4):
-            mm(R("ZN", r, 512, 4), R("ZP", 128 * r, 128 * r + 128), R("IDB"), False, False)
-
-        def lists(b0, s0):
-            if not last:
-                mm(R("TS", b0, 512, 2), PM(b0, s0, x ^ (nxt == 0)), R("TG", 256 * s0, 256 * s0 + 256), s0 == 0, s0 == 1)
+            mm(R("ZN", r, 512, 4), R("ZP", 128 * r, 128 * r + 128), R("IDB"), r == 0, False)
 
         def ofs(a, b):
             if not last:
                 cp(R("OFS", a, b), R("TS", a, b))
 
-        lists(0, 0)
-        lists(0, 1)
+        lists(3, 4, 5)
+        mm(R("K0", 0, 256), R("NEF"), R(td, 512 * par, 512 * par + 256), True, False)
 
         rb = ["D0", "D1", "K1", "PA"]
 
@@ -556,152 +558,153 @@ def rank_program(g, core, T, topo):
         def larger(r):
             tt(R("HS"), R(rb[r], 0, 256), R("HS"), ALU.max)
 
-        rows_of(range(17, 32))
-        columns_of(range(0, 8))
-        products(0)
+        spread_digits()
         columns_of(range(2 * NB, 32))
-        columns_of(range(8, 16))
-        act(R("HS"), R(rb[0], 0, 256), ACT.Copy)
-        products(1)
+        rows_of(range(24, 32))
+        columns_of(range(0, 8))
+        distances(range(10, 2 * NB))
+        products(0)
         products(3)
-        lists(1, 0)
+        for c0, c1, w0, w1, y in ((0, 64, 0, 2, 0), (64, 96, 0, 1, 1), (64, 96, 1, 2, 1)) if x else ((0, 96, 0, 2, 0),):
+            for k, dg in enumerate(DIGITS):
+                a = 8 * dg + 4 * (w0 ^ y)
+                mm(R("PB", c0, c1, 1, 64 * w0, 64 * w1), part3("EE", T.EE[:, a:a + 4 * (w1 - w0), :]),
+                   R("RHS", 96 * k + c0, 96 * k + c1), k == 0, k == 4)
+        columns_of(range(8, 16))
+        products(1)
         columns_of(range(16, 2 * NB))
-        spread_digits(1, 2)
-        larger(1)
-        spread_digits(2, 3)
-        products(2)
+        cp(R("HS"), R(rb[0], 0, 256))
+        rows_of(range(16, 21))
         larger(3)
-        spread_digits(3, 4)
-        for dg in range(4):
-            mm(R("PB", 0, 96), part3("EE", T.EE[:, 8 * dg:8 * dg + 8, :]), R("RHS", 96 * dg, 96 * dg + 96), dg == 0, dg == 3)
-        lists(1, 1)
-        mm(R("K0"), R("NEF"), tpar, True, False)
-        larger(2)
-        for qq in range(1, 4):
-            ts(R("ZQ", qq, 256, 4), R("HS", qq, 256, 4), 0.0, ALU.is_equal)
-        ts(R("CU"), R("PB", 0, 96), 4095.0, ALU.min)
+        rows_of(range(21, 24))
+        products(2)
+        ts(R("CU", 0, 64), R("PB", 0, 64), 4095.0, ALU.min)
+        larger(1)
+        ts(R("PO", 0, 32), R("PB", 64, 96), col(Q1K), ALU.add)
         act(R("GC"), ind(win, R("CU", 0, 32)), ACT.Identity, -256.0)
+        ofs(0, 128)
+        mm(R("K0", 256, 512), R("NEF"), R(td, 512 * par + 256, 512 * par + 512), False, False)
+        tt(R("HT"), R(rb[2], 0, 256), R("HS"), ALU.max)
+        tt(R("ZQ"), R(rb[2], 0, 256), R("HS"), ALU.is_equal)
+        ts(R("PO", 32, 64), R("PO", 0, 32), 4095, an)
+        ofs(128, 256)
+        lists(6, 7)
         mm(R("PA"), R("IDB"), R("GC"), True, False)
-        scan(R("H2"), R("ZQ"), R("HS"), ALU.mult, ALU.add)
+        scan(R("H2"), R("ZQ"), R("HT"), ALU.mult, ALU.add)
         scan(R("Q2"), R("ONES", 0, 256), R("ZQ"), ALU.add, ALU.mult)
         hs = R("H2", 3, 256, 4)
         ts(R("XY", 0, 64), hs, 1.0, ALU.min, 2.0 ** 62, ALU.mult)
         ts(R("XY", 64, 128), hs, 1.0, ALU.max, 2.0 ** -62, ALU.mult)
+        ts(R("CB"), R("H2", 128 * par + 3, 128 * par + 128, 4), math.exp(LW0 - 511.5 * LG), ALU.is_gt, -1.0, ALU.mult)
         for k in range(2):
             act(R("LQ", 1 + k, 256, 4), R("XY", 64 * k, 64 * k + 64), ACT.Ln)
         ts(R("LQ", 3, 256, 4), R("Q2", 3, 256, 4), 1024.0, ALU.mult, EVEN, ALU.add)
-        act(R("DD"), ind(R(tw), R("CU", 32, 64)), ACT.Copy)
-        ofs(0, 256)
-        scan(R("T1"), R("RMQ"), R("LQ"), ALU.mult, ALU.add)
+        cp(R("CU", 64, 96), R("PO", 32, 64))
+        act(R("DD"), ind(R(td), R("CU", 64, 96)), ACT.Copy)
+        for l in range(16):
+            c = 2064 * x + 128 * l + 15 - t
+            mm(R("ZN", l, 512, 16), R("TOROW", c, c + 128), R("CB"), False, False)
+        ts(R("Y1", 0, 64), hs, math.exp(LW0 - 511.5 * LG), ALU.is_gt, 8192.0, ALU.mult)
         ofs(256, 384)
+        scan(R("T1"), R("RMQ"), R("LQ"), ALU.mult, ALU.add)
+        tr(R("Y1", 64, 128), R("Y1", 0, 64))
+        ofs(384, 512)
         ts(R("FU"), R("T1", 3, 256, 4), -EVEN, ALU.add, float(par), ALU.add)
         ts(R("FF"), R("T1", 3, 256, 4), -EVEN, ALU.add, float(par), ALU.add)
-        ofs(384, 512)
+        tt(R("Y1", 128, 192), R("RY"), R("Y1", 64, 128), ALU.add)
         if not last:
             pass_on("ao%d" % t, R("OFS"), R(offn))
 
         def table():
             for s in range(4):
-                mm(R("PB", 64 * s, 64 * s + 64), R("SELF", 128 * s, 128 * s + 128), R("FF"), True, True)
-            act(R("WW", 0, 256), R("PB", 0, 256), ACT.Identity, col(Q1K + par))
+                mm(R("PB", 64 * s, 64 * s + 64), R("SELF", 128 * s, 128 * s + 128), R("T1", 3, 256, 4), True, True)
+            act(R("G", 0, 256), ind(win, R("FU", 32 * par, 32 * par + 16)), ACT.Copy)
+            act(R("WW", 0, 256), R("PB", 0, 256), ACT.Identity, col(Q1K + 1))
+            act(R("G", 256, 512), ind(win, R("FU", 32 * par + 16, 32 * par + 32)), ACT.Copy)
 
         def from_caller(h, a, b):
             part = R("SD", h + 32 * a, 32 * b, 2)
-            tt(part, ind(win, R("FU", 32 * h + a, 32 * h + b)), part, ALU.max)
-
-        def called():
-            ts(R("CB"), R("FF", 32 * par, 32 * par + 32), 4096.0, ALU.is_lt, -1.0, ALU.mult)
-
-        def leave_out():
-            for l in range(16):
-                c = 2064 * x + 128 * l + 15 - t
-                mm(R("ZN", l, 512, 16), R("TOROW", c, c + 128), R("CB"), False, False)
+            if h == par:
+                tt(part, R("TS", 16 * a, 16 * b), part, ALU.max)
+            else:
+                tt(part, ind(win, R("FU", 32 * h + a, 32 * h + b)), part, ALU.max)
 
         def connected():
-            tt(R("EQ"), ind(R("WW"), R("CU", 64, 96)), R("IDN"), ALU.is_equal)
+            tt(R("EQ"), ind(R("WW"), R("CU", 32, 64)), R("IDN"), ALU.is_equal)
             sums = ((R("PA"), R("BO2")), (R("ZN"), R("BO", 128 * x, 128 * x + 128)))
             for bank, ones in sums[::-1] if last else sums:
                 mm(bank, ones, R("EQ"), False, True)
 
-        sel = row_select(R("RN"), R("FY"), R("RY"), R("Y1"))
-
         def fixed_row():
-            sel[2]()
+            tt(R("RN"), R("Y1", 128, 192), R("FY"), ALU.min)
             for h in (npar, par):
                 for a, b in row_pieces(td, t, "RN", h):
                     dma(a, b, "fx%s%d" % ("ab"[h], t))
 
         if not last:
             table()
-            mm(R("K0", 0, 256), idf, R("DD", 0, 256), False, False)
+            mm(R("K0", 0, 256), R("IDF", 0, 128), R("DD", 0, 256), False, False)
+            mm(R("TS", 0, 256), R("IDB"), R("G", 0, 256), True, True)
             a, kb = 32 * npar, ["K1", "D0", "D1", "PB"]
-            from_caller(npar, 0, 16)
+            from_caller(npar, 0, 32)
             tr(R("FY"), R("FF"))
-            called()
-            from_caller(npar, 16, 24)
-            sel[0]()
-            from_caller(npar, 24, 32)
-            sel[1]()
-            leave_out()
             for s in range(3):
                 spread(kb[s], 0, s, sd[npar])
-            fill(swn, npar, R(kb[0]), "s")
+                if s == 0:
+                    mm(R("TS", 256, 512), R("IDB"), R("G", 256, 512), True, True)
+            for s in range(3):
+                fill(swn, npar + 1024 * s, R(kb[s]), "s")
             connected()
             spread(kb[3], 0, 3, sd[npar])
-            mm(R("K0", 256, 512), idf, R("DD", 256, 512), False, True)
+            mm(R("K0", 256, 512), R("IDF", 0, 128), R("DD", 256, 512), False, True)
             fixed_row()
-            fill(swn, npar + 1024, R(kb[1]), "s")
+            from_caller(par, 0, 16)
+            from_caller(par, 16, 32)
             pass_on("aa%d" % t, tnp, R(tdn, 512 * npar, 512 * npar + 512))
-            from_caller(par, 0, 24)
-            tr(R("X1"), R("RN", a, a + 32))
-            from_caller(par, 24, 32)
-            for w0, w1 in ((0, 64), (64, 128)) if nxt == 0 else ((0, 128),):
-                c = w0 ^ 64 * (nxt == 0)
-                cp(R("OFT", 0, 32, 1, c, c + w1 - w0), R("X1", 0, 32, 1, w0, w1))
-            act(R("MK"), R("ZN"), ACT.Relu, -2.0)
-            for s in (2, 3):
-                fill(swn, npar + 1024 * s, R(kb[s]), "s")
-            db = [["D0", "K1"], ["ZN", "PA"]]
+            act(R("MK"), R("ZN"), ACT.Relu, -1.0)
+            db = [["D0", "D1"], ["TS", "PA"]]
             for h in range(2):
                 part = R("SD", par + 512 * h, 512 * h + 512, 2)
                 tt(part, R("PA", 256 * h, 256 * h + 256), part, ALU.max)
                 for s in range(4):
                     spread(db[h][s // 2], 256 * (s % 2), s, part)
-            tt(R("TB"), R("K0"), R("MK"), ALU.mult)
+            tr(R("X1"), R("RN", a, a + 32))
+            fill(swn, npar + 1024 * 3, R(kb[3]), "v")
+            tt(R("TB", 0, 256), R("K0", 0, 256), R("MK", 0, 256), ALU.mult)
+            for w0, w1 in ((0, 64), (64, 128)) if nxt == 0 else ((0, 128),):
+                c = w0 ^ 64 * (nxt == 0)
+                cp(R("OFT", 0, 32, 1, c, c + w1 - w0), R("X1", 0, 32, 1, w0, w1))
             for h in range(2):
                 for s in range(4):
                     fill(swn, par + 1024 * s + 512 * h, R(db[h][s // 2], 256 * (s % 2), 256 * (s % 2) + 256), "sv"[s // 2])
+            tt(R("TB", 256, 512), R("K0", 256, 512), R("MK", 256, 512), ALU.mult)
             pass_on("ab%d" % t, [R("TB"), tpar], R(tdn, 512 * par, 512 * par + 512))
             pass_on("an%d" % t, R("OFT", 0, 32), R("OFT", 32 * t + 32, 32 * t + 64))
             for h in (npar, par):
                 old_row(tdn, t + 1, h)
-                window(tdn, twn, h, "tw%s%d" % ("ab"[h], t + 1), crossed(t + 1))
+                window(tdn, h, "tw%s%d" % ("ab"[h], t + 1))
             continue
 
         table()
-        from_caller(npar, 0, 8)
         tr(R("FY"), R("FF"))
-        called()
-        from_caller(npar, 8, 16)
-        sel[0]()
-        from_caller(npar, 16, 24)
-        sel[1]()
-        from_caller(npar, 24, 32)
+        from_caller(npar, 0, 12)
         fixed_row()
-        mm(R("K0"), idf, R("DD"), False, True)
-        leave_out()
+        from_caller(npar, 12, 32)
+        mm(R("K0"), R("IDF", 0, 128), R("DD"), False, True)
+        mm(R("TS"), R("IDB"), R("G", 0, 512), True, True)
         connected()
         from_caller(par, 0, 32)
-        act(R("MK"), R("ZN"), ACT.Relu, -2.0)
+        act(R("MK"), R("ZN"), ACT.Relu, -1.0)
         act(R("OT", npar, 1024, 2), tnp, ACT.Copy)
         parts = (("S", "SD", 0, 1024, T.ysec), ("T0", "OT", 0, 512, T.ytel), ("T1", "OT", 512, 512, T.ytel))
         for nm, src, c, width, y in parts:
             if nm == "S":
                 tt(own, R("PA"), own, ALU.max)
-                tt(R("K0"), R("K0"), R("MK"), ALU.mult)
+                for h in (0, 256):
+                    tt(R("D%d" % (h // 256), 0, 256), R("K0", h, h + 256), R("MK", h, h + 256), ALU.mult)
             else:
                 h = c // 2
-                tt(R("OT", c + par, c + 512, 2), R("K0", h, h + 256), R(td, 512 * par + h, 512 * par + h + 256), ALU.add)
+                tt(R("OT", c + par, c + 512, 2), R("D%d" % (h // 256), 0, 256), R(td, 512 * par + h, 512 * par + h + 256), ALU.add)
             for k, (k0, k1) in enumerate(spans):
                 dma(DR("o" + nm, k0, k1), R(src, c, c + width, 1, 16 * k0, 16 * k1), "o" + nm, "y" if nm == "S" else "ys"[k % 2])
         for nm, src, c, width, y in parts:

import math
from concourse.bass import DstId, RemoteDMATransfer
from concourse.mybir import AluOpType, AxisListType, ActivationFunctionType

ALU = AluOpType
ACT = ActivationFunctionType
NV = 10
NB = 10
GATHER, PASS = 8, 5
HIAT = 1
RO = 4
LG = math.log(1.398)
LW0 = 122 * math.log(2.0)
EVEN = 1.5 * 2.0 ** 24

F, B, I, U = "float32", "bfloat16", "int32", "uint16"
SCRATCH = {}


def _decl(where, dtype, **kw):
    for k in kw:
        SCRATCH[k] = (where, kw[k] if isinstance(kw[k], list) else [128, kw[k]], dtype)


_decl("psum", F, K0=512, K1=512, D0=512, D1=512, ZN=512, PA=512, PB=512, TS=512)
_decl("dram", B, oS=[8, 128, 128], loS=[8, 128, 128])
_decl("dram", F, oT0=[8, 128, 64], loT0=[8, 128, 64], oT1=[8, 128, 64], loT1=[8, 128, 64])
_decl("sbuf", I, CI=16, TL=1024, II=64, DG=128, PO=64)
_decl("sbuf", U, OFF0=512, OFF1=512, OFF2=512, OFF3=512, OFS=512, OFT=128, CL=160, FU=64, CU=96)
_decl("sbuf", B, SL=1024, SR=1024, SW0=4112, SW1=4112, SD=1024, M=8192, G=1536, GC=512, HI=512, IOT=192,
      IDB=128, NEG=128, HIR=512, SEL=512, SE0=512, SUMR=16, OWNR=256, RM16=128, RM4=128, ONES=256, LS=128, LI=128,
      L0=128, FB=320, RHS=512, BO=256, BO2=128, AA=4096, BB=2048, BX=2048, ZP=512, EQ=512, MK=512, TMPB=128,
      THR=256, TINY=64, CB=32, TOROW=4128, EE=[128, 32, 16])
_decl("sbuf", F, CF=48, TE=1024, TR=1024, TD0=4096, TD1=4096, TD2=4096, TD3=4096, ONEF=128, IDF=256,
      NEF=128, SELF=512, IZ0=160, IZ1=160, IF0=160, IF1=160, WT=384, STAB=128, IDN=512, KS=[128, 256, 4], AB=128, OK=128,
      TH=64, HS=256, HT=256, ZQ=256, H2=256, Q2=256, XY=128, LQ=256, RMQ=256, T1=256, FF=64, WW=512, TG=512,
      TX=512, X1=32, FY=64, RY=64, Y1=192, RN=64, DD=512, TB=512, OT=1024, TMPF=256)

_DMA_GROUPS = ["ldT", "ldS", "ownT", "ownS", "rawT0", "rawT1", "rawS", "oS", "oT0", "oT1", "out"]
_DMA_GROUPS += ["%s%d" % (n, t) for t in range(4) for n in ("twa", "twb", "ry", "fxa", "fxb")]
_ARRIVE = ["aT0", "aT1", "aS", "aoS", "aoT0", "aoT1"] + ["%s%d" % (n, t) for t in range(3) for n in ("aa", "ab", "ao", "an")]
SEMAPHORES = ["ev", "es", "ep", "eg"] + _DMA_GROUPS + _ARRIVE + ["s" + n for n in _ARRIVE]
ENGSEM = {"v": "ev", "s": "es", "p": "ep", "g": "eg"}


def R(name, c0=None, c1=None, st=1, p0=0, p1=128, ps=1):
    if c0 is None:
        c0, c1 = 0, SCRATCH[name][1][1]
    return (name, p0, p1, ps, c0, c1, st)


def part3(name, pattern, k0=0, k1=8):
    return (name, 0, 128, 1, k0, k1, 1, pattern)


def DR(name, k0=0, k1=8, r0=0, r1=128):
    return (name, k0, k1, 1, r0, r1, 1)


def _touch(a, b):
    if SCRATCH[a[0]][0] == "psum":
        return True
    if a[6] == b[6] > 1 and (a[4] - b[4]) % a[6] or a[3] == b[3] > 1 and (a[1] - b[1]) % a[3]:
        return False
    return a[1] < b[2] and b[1] < a[2] and a[4] < b[5] and b[4] < a[5]


def rank_program(g, core, T, topo):
    rank = T.rank_of(core)
    if rank is None:
        return
    cores = T.cores
    n = len(cores)
    ops = []
    Q = {"v": g.vector, "s": g.scalar, "p": g.tensor, "g": g, "y": g.sync}

    def ap(x):
        if not isinstance(x, tuple):
            return x
        if x[0] == "ind":
            return ap(x[1]).indirect(ap(x[2]))
        if x[0] == "raw":
            return x[1]
        if len(x) == 8:
            return x[7]
        nm, p0, p1, ps, c0, c1, st = x
        if SCRATCH[nm][0] == "dram":
            return T[nm][p0, c0:c1, :] if p1 == p0 + 1 else T[nm][p0:p1, c0:c1, :]
        a = slice(p0, p1) if ps == 1 else slice(p0, p1, ps)
        b = slice(c0, c1) if st == 1 else slice(c0, c1, st)
        return T[nm][a, b]

    def regs(xs):
        out = []
        for x in xs:
            if isinstance(x, tuple):
                if x[0] == "ind":
                    out += [x[1], x[2]]
                elif x[0] != "raw":
                    out.append(x)
        return out

    def add(eng, fn, w, r, group=None, count=0):
        ops.append({"e": eng, "f": fn, "w": regs(w), "r": regs(r), "grp": group, "n": count})

    def ind(win, off):
        return ("ind", win, off)

    def tt(o, a, b, op):
        add("v", lambda: g.vector.tensor_tensor(ap(o), ap(a), ap(b), op), [o], [a, b])

    def ts(o, a, s1, op0, s2=None, op1=None):
        if op1 is None:
            add("v", lambda: g.vector.tensor_scalar(ap(o), ap(a), ap(s1), None, op0), [o], [a, s1])
        else:
            add("v", lambda: g.vector.tensor_scalar(ap(o), ap(a), ap(s1), ap(s2), op0, op1), [o], [a, s1, s2])

    def cp(o, a):
        add("v", lambda: g.vector.tensor_copy(ap(o), ap(a)), [o], [a])

    def ms(o, val):
        add("v", lambda: g.vector.memset(ap(o), val), [o], [])

    def scan(o, d0, d1, op0, op1, first=0.0):
        add("v", lambda: g.vector.tensor_tensor_scan(ap(o), ap(d0), ap(d1), ap(first), op0, op1), [o], [d0, d1, first])

    def total(o, a):
        add("v", lambda: g.vector.tensor_reduce(ap(o), ap(a), AxisListType.X, ALU.add), [o], [a])

    def tr(o, a):
        add("v", lambda: g.vector.transpose(ap(o), ap(a)), [o], [a])

    def act(o, a, fn, bias=None, scale=None):
        def call():
            kw = {}
            if bias is not None:
                kw["bias"] = ap(bias)
            if scale is not None:
                kw["scale"] = ap(scale)
            return g.scalar.activation(ap(o), ap(a), fn, **kw)
        add("s", call, [o], [a, bias, scale])

    def mm(o, l, r, start, stop):
        add("p", lambda: g.tensor.matmul(ap(o), ap(l), ap(r), start, stop), [o], [l, r])

    def iota(o, pat, base=0, cm=0):
        if SCRATCH[o[0]][2] == I:
            add("g", lambda: g.iota(ap(o), pat, base, cm), [o], [])
        else:
            add("g", lambda: g.iota(ap(o), pat, base, cm, allow_small_or_imprecise_dtypes=True), [o], [])

    def pick(o, a, pat, op, base=0, cm=1, fill=0.0):
        add("g", lambda: g.affine_select(ap(o), ap(a), pat, op, fill, base, cm), [o], [a])

    def dma(o, a, group, q="y"):
        add(q, lambda: Q[q].dma_start(ap(o), ap(a)), [o], [a], group, 16)

    def send(name, items, width, after=()):
        srcs = [x[1] if isinstance(x[1], list) else [x[1]] for x in items]

        def fn():
            trs = []
            for k, (d, _, dst) in enumerate(items):
                eng = topo.engines(core, cores[d])[k * width:(k + 1) * width]
                rid, pid, _ = topo.addr(cores[d])
                trs.append(RemoteDMATransfer(dst_ids=[DstId(rid=rid, pnc=pid)], dma_engine_mask=sum(1 << e for e in eng),
                                             remote_sem=T.sem[name], srcs=[ap(x) for x in srcs[k]], dsts=[ap(dst)],
                                             alu_op=1 if len(srcs[k]) > 1 else 0))
            g.remote_dma_fused(trs, local_sem=T.sem["s" + name])
            return None
        add("g", fn, [], sum(srcs, list(after)), "s" + name, width * len(items))

    def arrive(name, lands, count):
        add("x", None, lands, [], name, count)

    nxt = (rank + 1) % n

    def crossed(t):
        return int(rank < t)

    wide = len(topo.engines(core, cores[nxt]))
    w6 = wide // 8
    others = [(rank + d) % n for d in range(1, n)]
    pieces = [(d, w) for d in others for w in range(2)]
    spans = [x for x in ((0, rank), (rank + 1, rank + n), (rank + n + 1, 2 * n)) if x[0] < x[1]]

    def exchange(name, src, land, x):
        send(name, [(d, DR(src, d + n * (w ^ x), d + n * (w ^ x) + 1), DR(land, rank + n * w, rank + n * w + 1)) for d, w in pieces], w6)
        arrive(name, [DR(land, d + n * w, d + n * w + 1) for d, w in pieces], 6 * w6)

    def pass_on(name, src, land):
        send(name, [(nxt, src, land)], wide)
        arrive(name, [land], wide)

    def col(k):
        return R("CF", k, k + 1)

    def quarters(nm, c, width, w):
        return R(nm, c, c + width, 1, 64 * w, 64 * w + 64)

    def rows(src, d, w):
        return ("raw", src[16 * (d + n * w):16 * (d + n * w) + 16, :])

    for src, out, nm in ((T.sec, "SL", "ldS"), (T.tel, "TL", "ldT")):
        for k, (d, w) in enumerate(pieces):
            dma(quarters(out, 256 * (k // 2), 256, w), rows(src, d, w), nm, "ys"[k % 2])
    for w in range(2):
        dma(quarters("SR", 256 * rank, 256, w), rows(T.sec, rank, w), "ownS", "ys"[w])
        dma(quarters("TL", 768, 256, w), rows(T.tel, rank, w), "ownT", "ys"[w])
    P15, PG, PQ, P3, PH, P2, P7, B3, C32, P24, LC, WP, Q1K, LNC, W0, MC = 0, 1, 2, 3, 4, 5, 6, 7, 8, 9, 10, 22, 12, 14, 16, 18
    EQ0, NE0 = ALU.is_equal, ALU.not_equal
    one, onef = R("ONES", 0, 128), R("ONEF")
    ms(R("ONES"), 1.0)
    ms(onef, 1.0)
    iota(R("CI", 8, 9), [[0, 1]], 0, 1)
    iota(R("TMPF", 0, 32), [[256, 2], [16, 8], [128, 2]])
    iota(R("TMPF", 32, 48), [[4, 8], [2, 2]])
    pick(R("IDB"), one, [[-1, 128]], EQ0)
    for c in range(2):
        pick(R("SE0", 128 * c, 128 * c + 128), one, [[-64, 2], [0, 4], [-4, 16]], EQ0, -c)

    def hand_out(nm, out, land, c, width, after=()):
        send(nm, [(d, R(out, c + width * k, c + width * k + width), R(land, c + width * rank, c + width * rank + width))
                  for k, d in enumerate(others)], 2 * w6, after)
        arrive(nm, [R(land, c + width * d, c + width * d + width) for d in others], 6 * w6)

    def by_groups(out, c, land, lc, width, nm):
        for w in range(2):
            for q in range(n):
                dma(R(out, c, c + 4 * width, 1, 64 * w + 16 * q, 64 * w + 16 * q + 16), quarters(land, lc + width * q, width, w), nm)

    def entries(h):
        cp(R("TE", 512 * h, 512 * h + 384), R("TL", h, 768, 2))
        cp(R("TR", 512 * h + 128 * rank, 512 * h + 128 * rank + 128), R("TL", 768 + h, 1024, 2))

    hand_out("aS", "SL", "SR", 0, 256)
    for c in range(2, 4):
        pick(R("SE0", 128 * c, 128 * c + 128), one, [[-64, 2], [0, 4], [-4, 16]], EQ0, -c)
    iota(R("TMPF", 64, 96), [[1, 32]])
    iota(R("TMPB"), [[1, 8], [0, 16]])

    pc = R("CI", 8, 9)
    sh, an = ALU.arith_shift_right, ALU.bitwise_and
    L1, L2, L3, FL = R("CL", 0, 32), R("CL", 32, 64), R("CL", 64, 80), R("CL", 96, 104)
    ms(col(W0), 2.0 ** 61)
    for k, a, b in ((P15, 0, 15), (PG, 4, 7), (PQ, 4, 3), (P3, 0, 3), (PH, 2, 31), (P2, 2, 3), (P7, 0, 7), (B3, 3, 1)):
        ts(R("CI", k, k + 1), pc, a, sh, b, an)
    act(col(LNC + 1), col(W0), ACT.Ln)
    ms(R("WT", 0, 128), math.exp(-4 * LG))
    ms(R("WT", 128, 256), 0.0)
    cp(R("CF", 0, 8), R("CI", 0, 8))
    ts(col(W0 + 1), col(W0), 2.0 ** 61 * math.exp(4 * LG), ALU.mult)
    ms(R("RM16"), 256.0)
    ts(col(C32), col(P15), 32.0, ALU.mult)
    ts(col(P24), col(P2), 4.0, ALU.mult)
    for k in range(4):
        ts(col(MC + k), col(P3), float(k), ALU.is_equal)
    for k in range(2):
        ts(col(Q1K + k), col(PQ), -1024.0, ALU.mult, -EVEN * k, ALU.add)
    ts(col(LC), col(P7), 32.0, ALU.mult, col(B3), ALU.add)
    scan(R("WT", 256, 384), R("WT", 0, 128), R("WT", 128, 256), ALU.mult, ALU.add, col(W0 + 1))
    ms(R("RM16", 0, 128, 16), -2.0 ** 30)
    ts(L1, R("TMPF", 0, 32), col(P15), ALU.add)
    ts(L3, R("TMPF", 32, 48), col(LC), ALU.add)
    tt(R("WT", 0, 128), R("WT", 256, 384), R("IDB"), ALU.mult)
    ms(R("SW0", 4096, 4112), 0.0)
    ms(R("SW1", 4096, 4112), 0.0)
    total(col(WP), R("WT", 0, 128))
    ms(R("TINY", p1=1), math.exp(LW0 - 512 * LG))
    ms(R("THR", 128, 256, p1=1), -960.0)
    ts(col(WP + 1), col(WP), -1.0, ALU.mult)
    ts(col(LNC), col(LNC + 1), -2.0, ALU.mult, -0.453 * LG, ALU.add)
    entries(0)
    hand_out("aT0", "TE", "TR", 0, 128)
    entries(1)
    by_groups("SD", 0, "SR", 0, 256, "rawS")
    by_groups("TD0", 0, "TR", 0, 128, "rawT0")
    iota(R("TMPF", 96, 104), [[1, 4], [16, 2]])
    ts(R("LQ", 0, 256, 4), R("ONEF", 0, 64), col(LNC), ALU.mult)
    ts(L2, R("TMPF", 64, 96), col(C32), ALU.add)
    ts(R("RHS", 480, 512), R("TMPF", 64, 96), col(PH), ALU.is_equal)
    ts(R("BO", 0, 128), R("TMPB"), col(PG), ALU.is_equal)
    for k, val in enumerate((0.0, 1.0, 1.0, -2.0 / LG)):
        ms(R("RMQ", k, 256, 4), val)
    ms(R("TOROW", 0, 2064), 0.0)
    for o, sc in ((R("NEG"), -1.0), (R("IDF", 0, 128), 1.0), (R("HIR", 0, 128), 1.0), (R("HIR", 128, 256), -32.0), (R("NEF"), -1.0)):
        act(o, R("IDB"), ACT.Copy, None, sc)
    for k in range(2):
        act(R("OWNR", 128 * k, 128 * k + 128), R("BO", 0, 128), ACT.Copy, None, -4096.0)
        act(R("SUMR", 8 * k, 8 * k + 8), R("BO", 0, 128, 16), ACT.Copy, None, 4096.0)
    act(R("BO2"), R("BO", 0, 128), ACT.Copy, None, 256.0)
    DIGITS = (0, 1, 2, 2, 3)
    for dg, sc in enumerate(((2, 0, 1), (32, 1, 16), (-32, 0, 0), (1 / 32, 0, 0), (62, 4, 63))):
        for k in range(3):
            act(R("RHS", 96 * dg + 32 * k, 96 * dg + 32 * k + 32), R("RHS", 480, 512), ACT.Copy, None, float(sc[k]))
    for i in range(NV, 16):
        ms(R("OWNR", i, 256, 16), 0.0)
    ts(FL, R("TMPF", 96, 104), col(P24), ALU.add)
    pick(R("THR", 0, 128, p1=1), R("THR", 128, 256, p1=1), [[0, 8], [-1, 4], [1, 4]], EQ0, 0, 0)
    iota(R("STAB"), [[0, 32], [16, 4]])
    iota(R("FB", 0, 96), [[0, 96]])
    iota(R("FB", 224, 320), [[0, 96]])
    pick(R("LS"), one, [[1, 128]], ALU.is_gt, 0, -1)
    pick(R("LI"), one, [[1, 128]], ALU.is_ge, 0, -1)
    pick(R("L0"), R("LS"), [[1, 128]], NE0, 0, -1, -1024.0)
    iota(R("IOT"), [[1, 192]], -64)
    pick(R("RM4"), one, [[0, 32], [1, 4]], ALU.is_gt, 0, 0)
    for nm in (("IF", "IZ") if nxt == 0 else ("IZ", "IF")):
        for a in range(2):
            for c in (0, 144):
                iota(R("%s%d" % (nm, a), c, c + 16), [[0, 16]])
            for w in range(2):
                pick(R("%s%d" % (nm, a), 16 + 64 * w, 80 + 64 * w), R("ONEF", 0, 64), [[-32, 2], [-272, 2], [-1, 16]], EQ0,
                     256 * a - 64 * (1 - w if nm == "IF" else w))
    hand_out("aT1", "TE", "TR", 512, 128, [R("SD")])
    iota(R("WW", 256, 512), [[0, 256]], -1)
    for s in range(4):
        pick(R("SELF", 128 * s, 128 * s + 128), onef, [[-64, 2], [0, 4], [-1, 16]], EQ0, -16 * s)
    iota(R("IDN", 0, 512), [[2, 512]])
    pick(R("TOROW", 15, 2063, 16), one, [[-1, 16], [-16, 8]], EQ0)
    for s in range(4):
        pick(R("SEL", 128 * s, 128 * s + 128), one, [[-64, 2], [0, 4], [-1, 16]], EQ0, -16 * s)
    if crossed(RO - 1):
        iota(R("TOROW", 2064, 4128), [[0, 2064]])
        pick(R("TOROW", 2064 + 15, 2064 + 2063, 16), one, [[-1, 16], [64, 2], [-16, 4]], EQ0, -64)
        iota(R("TMPB", 0, 128), [[0, 128]], -32)
        for o, a in ((R("IDF", 128, 256), onef), (R("HIR", 256, 384), one), (R("HIR", 384, 512), R("TMPB"))):
            pick(o, a, [[64, 2], [-1, 64]], EQ0, -64)
        pick(R("BO", 128, 256), one, [[64, 2], [-16, 4], [0, 16]], ALU.is_ge, -64)
        pick(R("BO", 128, 256), R("BO", 128, 256), [[-64, 2], [16, 4], [0, 16]], ALU.is_ge, 79, -1)

    def PM(a, b, x):
        o = 16 + 16 * (a - b)
        return R("%s%d" % ("IF" if x else "IZ", a), o, o + 128)

    def spread(bank, c, s, src):
        mm(R(bank, c, c + (src[5] - src[4] + 1) // 2), R("SEL", 128 * s, 128 * s + 128), src, True, True)

    def fill(sw, c, src, engine):
        o = R(sw, c, c - 1 + 2 * (src[5] - src[4]), 2)
        if engine == "v":
            cp(o, src)
        else:
            act(o, src, ACT.Copy)

    def window(td, par, group):
        for w in range(2):
            for s in range(4):
                src = R(td, 512 * par, 512 * par + 512, 1, 64 * w + 16 * s, 64 * w + 16 * s + 16)
                for k in range(1, 4):
                    c, q = 1024 * k + 512 * par, (s - k) % 4
                    dma(R(td, c, c + 512, 1, 64 * w + 16 * q, 64 * w + 16 * q + 16), src, group)

    def row_pieces(td, t, nm, h):
        x = crossed(t)
        for w0, w1 in ((0, 64), (64, 128)) if x else ((0, 128),):
            for s0 in range(2):
                yield (R(td, 512 * h, 512 * h + 512, 1, (w0 ^ 64 * x) + 16 * s0 + t, (w0 ^ 64 * x) + w1 - w0, 32),
                       R(nm, 32 * h + 16 * s0, 32 * h + 16 * s0 + 16, 1, w0, w1))

    def old_row(td, t, h):
        for a, b in row_pieces(td, t, "RY", h):
            dma(b, a, "ry%d" % t)

    eight = ["K0", "K1", "D0", "D1", "ZN", "PA", "PB", "TS"]
    for k in range(16):
        s, c = k // 4, k % 4
        mm(R(eight[k // 2], 256 * (k % 2), 256 * (k % 2) + 256), R("SE0", 128 * c, 128 * c + 128), R("SR", 256 * s, 256 * s + 256),
           True, True)
    cp(R("SW0", 512, 1024), R(eight[1]))
    for k in (0, 2):
        act(R("SW0", 512 * k, 512 * k + 512), R(eight[k]), ACT.Copy)
    cp(R("TG", 0, 256), ind(R("TR", 0, 512), R("CL", 0, 16)))
    act(R("TG", 256, 512), ind(R("TR", 0, 512), R("CL", 16, 32)), ACT.Copy)
    for k in range(3, 8):
        act(R("SW0", 512 * k, 512 * k + 512), R(eight[k]), ACT.Copy)
    for h in range(2):
        tr(R("TX", 256 * h, 256 * h + 256), R("TG", 256 * h, 256 * h + 256))
    for h in range(2):
        cp(R("OFS", 256 * h, 256 * h + 256), ind(R("TX", 256 * h, 256 * h + 256), L3))
    for a in (1, 0):
        for b in range(2):
            for w in range(2):
                cp(R("OFF0", 256 * a, 256 * a + 256, 1, 64 * w + 32 * b, 64 * w + 32 * b + 32),
                   R("OFS", 256 * b, 256 * b + 256, 1, 64 * w + 32 * a, 64 * w + 32 * a + 32))
    sd = [R("SD", 0, 1024, 2), R("SD", 1, 1024, 2)]

    by_groups("TD0", 512, "TR", 512, 128, "rawT1")
    for h in range(2):
        old_row("TD0", 0, h)
        window("TD0", h, "tw%s0" % "ab"[h])

    for t in range(RO):
        par, npar, last = t % 2, 1 - t % 2, t == RO - 1
        td, tdn = "TD%d" % t, "TD%d" % (t + 1)
        sw, swn = "SW%d" % par, "SW%d" % npar
        off, offn = "OFF%d" % t, "OFF%d" % (t + 1)
        own = sd[par]
        win = R(sw)
        x = crossed(t)
        idf = R("IDF", 128 * x, 128 * x + 128)
        tpar = R(td, 512 * par, 512 * par + 512)
        tnp = R(td, 512 * npar, 512 * npar + 512)

        def kcol(r, c0, c1, st=1):
            return R("K%d" % (r // 2), 256 * (r % 2) + c0, 256 * (r % 2) + c1, st)

        def sums(i, stop):
            for r in range(4):
                mm(kcol(r, i, 256, 16), R("M", 512 * i + r, 512 * i + 512, 4), R("SUMR"), False, stop and r % 2 == 1)

        vrows = sorted(range(NV), key=lambda i: i == t - 1 if t else i < 8)
        srows = list(range(NV, 16))
        banks = dict(zip(srows, ("ZN", "PB", "D0", "D1", "TS", "PA")))

        def lines(i):
            return (R("M", 512 * i, 512 * i + 512), R("OFT", 32 * t, 32 * t + 32) if i == t - 1 else R(off, 32 * i, 32 * i + 32),
                    R("G", 512 * (i % 3), 512 * (i % 3) + 512))

        def by_vector(i):
            tt(lines(i)[0], ind(win, lines(i)[1]), own, ALU.max)
            sums(i, False)

        def by_scalar(i):
            act(lines(i)[2], ind(win, lines(i)[1]), ACT.Copy)
            mm(R(banks[i]), R("IDB"), lines(i)[2], False, True)

        def positive(i):
            act(lines(i)[0], R(banks[i]), ACT.Relu)
            sums(i, i == srows[-1])

        def less_own(i):
            mm(R(banks[i]), R("NEG"), own, True, False)

        def high(i):
            act(R("HI"), tpar, ACT.Identity, 129 - 0.484375, 1.0 / 32)

        def entry(r):
            mm(kcol(r, 128, 256), R(td, 512 * par + r, 512 * par + 512, 4), idf, False, False)

        def entry_high(r):
            mm(kcol(r, 0, 256), R("HI", r, 512, 4), R("HIR", 256 * x, 256 * x + 256), False, False)

        steps = [(by_scalar, i) for i in srows[:3]]
        for m, i in enumerate(srows[3:]):
            steps += [(positive, i - 3)] + [(high, 0)] * (m == HIAT) + [(by_scalar, i)]
        steps += [(positive, i) for i in srows[-3:]]
        spare = [(less_own, i) for i in srows[3:]] + [(entry, r) for r in range(4)] + [(entry_high, r) for r in range(4)]
        for i in srows[:3]:
            less_own(i)
        for r in range(4):
            mm(kcol(r, 0, 256), R("SD", par + 2 * r, 1024, 8), R("OWNR"), r % 2 == 0, False)
        ev, clock = [(GATHER * (k + 1), k, by_vector, i) for k, i in enumerate(vrows)], 0
        for k, (fn, i) in enumerate(steps):
            clock += GATHER if fn is by_scalar else PASS
            ev.append((clock, 20 + 2 * k, fn, i))
            if k < len(spare):
                ev.append((clock, 21 + 2 * k) + spare[k])
        for e in sorted(ev, key=lambda e: (e[0], e[1] < 20, e[1])):
            e[2](e[3])

        def spread_digits():
            for k in range(4):
                act(part3("EE", T.EE[:, :, 4 * k:4 * k + 4], k, k + 1), R("AB"), ACT.Copy, None, col(MC + k))

        if not last:
            tr(R("TX"), tnp)
            act(R("TG"), ind(R("TX"), L2), ACT.Copy)
        for k in range(8):
            a = 128 * (k // 4)
            scan(part3("KS", T.KS[:, a:a + 128, k % 4], k, k + 1), R("RM16"), kcol(k % 4, a, a + 128), ALU.add, ALU.max)
            if k == 6:
                ts(R("II", 0, 32), part3("KS", T.KS[:, 15:128:16, :], 0, 4), -129.0, ALU.add, 4095.0, ALU.max)

        def lists(*parts):
            for k in parts if not last else ():
                h, b0, s0 = k // 4, k // 2 % 2, k % 2
                mm(R("TS", 256 * h + b0, 256 * h + 256, 2), PM(b0, s0, x ^ (nxt == 0)),
                   R("TG", 256 * s0 + 128 * h, 256 * s0 + 128 * h + 128), s0 == 0, s0 == 1)

        lists(0, 1, 2)
        cnt = R("PA", 0, 128)
        one1 = R("ONES", 0, 128, p1=1)
        mm(cnt, one1, R("THR", 0, 128, p1=1), True, False)
        for r in range(4):
            for w in range(1 + x):
                a, c = 128 >> x, 128 * r + 64 * (w ^ x)
                act(R("ZP", c, c + a), kcol(r, 64 * w, 64 * w + a), ACT.Sign, 4095.5, -1.0)
        ts(R("DG", 0, 32), R("II", 0, 32), 1, sh, 112, an)
        cp(R("II", 32, 64), part3("KS", T.KS[:, 143:256:16, :], 4, 8))
        ts(R("DG", 32, 64), R("II", 0, 32), 31, an)
        tt(R("FB", 96, 224), ind(R("DG", 0, 32), FL), R("STAB"), ALU.is_equal)
        ts(R("DG", 96, 128), R("II", 32, 64), 1, an)
        ts(R("DG", 64, 96), R("II", 32, 64), 1, sh, 15, an)
        ts(R("AB", 64, 96), R("DG", 96, 128), 32.0, ALU.mult)
        tt(R("AB", 0, 32), R("DG", 0, 32), R("DG", 64, 96), ALU.add)
        cp(R("AB", 96, 128), R("DG", 0, 32))
        mm(cnt, R("L0"), R("FB", 96, 224), False, False)
        for k in range(1, 4):
            mm(cnt, R("LI"), R("FB", 96 - 32 * k, 224 - 32 * k), False, False)
            mm(cnt, R("LS"), R("FB", 96 + 32 * k, 224 + 32 * k), False, k == 3)
        tt(R("AB", 32, 64), R("DG", 32, 64), R("AB", 64, 96), ALU.add)

        def digit(k, c0):
            c = c0 + 16 * (k % 2) + 4 * (k // 2 % 4) + k // 8
            return R("AB", c, c + 1)

        def weight(k, c0=0):
            c = c0 + 8 * (k // 8) + 4 * (k % 2) + k // 2 % 4
            return R("TH", c, c + 1)

        def rows_of(ks):
            for k in ks:
                ts(R("AA", 128 * k, 128 * k + 128), R("IOT", 64 - 64 * (k % 2), 192 - 64 * (k % 2)), digit(k, 0), ALU.is_equal,
                   math.exp(-LG * (k // 8)), ALU.mult)

        def columns_of(ks):
            for k in ks:
                o = R("BB", 64 * k, 64 * k + 64)
                if k < 2 * NB:
                    act(o, R("BX", 64 * k, 64 * k + 64), ACT.Relu, weight(k), weight(k, 32))
                else:
                    ts(o, R("IOT", 64, 128), digit(k, 32), ALU.is_equal, weight(k), ALU.mult)

        def distances(ks):
            for k in ks:
                act(R("BX", 64 * k, 64 * k + 64), R("IOT", 64, 128), ACT.Abs, digit(k, 32), -1.0)

        distances(range(10))
        rows_of(range(0, 7))
        scan(R("OK"), R("RM4"), cnt, ALU.mult, ALU.min)
        rows_of(range(7, 12))
        for k in range(2):
            ts(R("TH", 32 * k, 32 * k + 32), R("OK", 3, 128, 4), -961.0, ALU.is_le, col(WP + k), ALU.mult)
        rows_of(range(12, 16))
        for r in range(4):
            mm(R("ZN", r, 512, 4), R("ZP", 128 * r, 128 * r + 128), R("IDB"), r == 0, False)

        def ofs(a, b):
            if not last:
                cp(R("OFS", a, b), R("TS", a, b))

        lists(3, 4, 5)
        mm(R("K0", 0, 256), R("NEF"), R(td, 512 * par, 512 * par + 256), True, False)

        rb = ["D0", "D1", "K1", "PA"]

        def products(r):
            for q in range(4):
                o, first = R(rb[r], 3 - q, 256, 4), True
                if (r, q) == (0, 3):
                    mm(o, one1, R("TINY", p1=1), True, False)
                    first = False
                for w in range(2):
                    k = 8 * r + 2 * q + w
                    mm(o, R("AA", 128 * k, 128 * k + 128), R("BB", 64 * k, 64 * k + 64), first and w == 0, w == 1)

        def larger(r):
            tt(R("HS"), R(rb[r], 0, 256), R("HS"), ALU.max)

        spread_digits()
        columns_of(range(2 * NB, 32))
        rows_of(range(24, 32))
        columns_of(range(0, 8))
        distances(range(10, 2 * NB))
        products(0)
        products(3)
        for c0, c1, w0, w1, y in ((0, 64, 0, 2, 0), (64, 96, 0, 1, 1), (64, 96, 1, 2, 1)) if x else ((0, 96, 0, 2, 0),):
            for k, dg in enumerate(DIGITS):
                a = 8 * dg + 4 * (w0 ^ y)
                mm(R("PB", c0, c1, 1, 64 * w0, 64 * w1), part3("EE", T.EE[:, a:a + 4 * (w1 - w0), :]),
                   R("RHS", 96 * k + c0, 96 * k + c1), k == 0, k == 4)
        columns_of(range(8, 16))
        products(1)
        columns_of(range(16, 2 * NB))
        cp(R("HS"), R(rb[0], 0, 256))
        rows_of(range(16, 21))
        larger(3)
        rows_of(range(21, 24))
        products(2)
        ts(R("CU", 0, 64), R("PB", 0, 64), 4095.0, ALU.min)
        larger(1)
        ts(R("PO", 0, 32), R("PB", 64, 96), col(Q1K), ALU.add)
        act(R("GC"), ind(win, R("CU", 0, 32)), ACT.Identity, -256.0)
        ofs(0, 128)
        mm(R("K0", 256, 512), R("NEF"), R(td, 512 * par + 256, 512 * par + 512), False, False)
        tt(R("HT"), R(rb[2], 0, 256), R("HS"), ALU.max)
        tt(R("ZQ"), R(rb[2], 0, 256), R("HS"), ALU.is_equal)
        ts(R("PO", 32, 64), R("PO", 0, 32), 4095, an)
        ofs(128, 256)
        lists(6, 7)
        mm(R("PA"), R("IDB"), R("GC"), True, False)
        scan(R("H2"), R("ZQ"), R("HT"), ALU.mult, ALU.add)
        scan(R("Q2"), R("ONES", 0, 256), R("ZQ"), ALU.add, ALU.mult)
        hs = R("H2", 3, 256, 4)
        ts(R("XY", 0, 64), hs, 1.0, ALU.min, 2.0 ** 62, ALU.mult)
        ts(R("XY", 64, 128), hs, 1.0, ALU.max, 2.0 ** -62, ALU.mult)
        ts(R("CB"), R("H2", 128 * par + 3, 128 * par + 128, 4), math.exp(LW0 - 511.5 * LG), ALU.is_gt, -1.0, ALU.mult)
        for k in range(2):
            act(R("LQ", 1 + k, 256, 4), R("XY", 64 * k, 64 * k + 64), ACT.Ln)
        ts(R("LQ", 3, 256, 4), R("Q2", 3, 256, 4), 1024.0, ALU.mult, EVEN, ALU.add)
        cp(R("CU", 64, 96), R("PO", 32, 64))
        act(R("DD"), ind(R(td), R("CU", 64, 96)), ACT.Copy)
        for l in range(16):
            c = 2064 * x + 128 * l + 15 - t
            mm(R("ZN", l, 512, 16), R("TOROW", c, c + 128), R("CB"), False, False)
        ts(R("Y1", 0, 64), hs, math.exp(LW0 - 511.5 * LG), ALU.is_gt, 8192.0, ALU.mult)
        ofs(256, 384)
        scan(R("T1"), R("RMQ"), R("LQ"), ALU.mult, ALU.add)
        tr(R("Y1", 64, 128), R("Y1", 0, 64))
        ofs(384, 512)
        ts(R("FU"), R("T1", 3, 256, 4), -EVEN, ALU.add, float(par), ALU.add)
        ts(R("FF"), R("T1", 3, 256, 4), -EVEN, ALU.add, float(par), ALU.add)
        tt(R("Y1", 128, 192), R("RY"), R("Y1", 64, 128), ALU.add)
        if not last:
            pass_on("ao%d" % t, R("OFS"), R(offn))

        def table():
            for s in range(4):
                mm(R("PB", 64 * s, 64 * s + 64), R("SELF", 128 * s, 128 * s + 128), R("T1", 3, 256, 4), True, True)
            act(R("G", 0, 256), ind(win, R("FU", 32 * par, 32 * par + 16)), ACT.Copy)
            act(R("WW", 0, 256), R("PB", 0, 256), ACT.Identity, col(Q1K + 1))
            act(R("G", 256, 512), ind(win, R("FU", 32 * par + 16, 32 * par + 32)), ACT.Copy)

        def from_caller(h, a, b):
            part = R("SD", h + 32 * a, 32 * b, 2)
            if h == par:
                tt(part, R("TS", 16 * a, 16 * b), part, ALU.max)
            else:
                tt(part, ind(win, R("FU", 32 * h + a, 32 * h + b)), part, ALU.max)

        def connected():
            tt(R("EQ"), ind(R("WW"), R("CU", 32, 64)), R("IDN"), ALU.is_equal)
            sums = ((R("PA"), R("BO2")), (R("ZN"), R("BO", 128 * x, 128 * x + 128)))
            for bank, ones in sums[::-1] if last else sums:
                mm(bank, ones, R("EQ"), False, True)

        def fixed_row():
            tt(R("RN"), R("Y1", 128, 192), R("FY"), ALU.min)
            for h in (npar, par):
                for a, b in row_pieces(td, t, "RN", h):
                    dma(a, b, "fx%s%d" % ("ab"[h], t))

        if not last:
            table()
            mm(R("K0", 0, 256), R("IDF", 0, 128), R("DD", 0, 256), False, False)
            mm(R("TS", 0, 256), R("IDB"), R("G", 0, 256), True, True)
            a, kb = 32 * npar, ["K1", "D0", "D1", "PB"]
            from_caller(npar, 0, 32)
            tr(R("FY"), R("FF"))
            for s in range(3):
                spread(kb[s], 0, s, sd[npar])
                if s == 0:
                    mm(R("TS", 256, 512), R("IDB"), R("G", 256, 512), True, True)
            for s in range(3):
                fill(swn, npar + 1024 * s, R(kb[s]), "s")
            connected()
            spread(kb[3], 0, 3, sd[npar])
            mm(R("K0", 256, 512), R("IDF", 0, 128), R("DD", 256, 512), False, True)
            fixed_row()
            from_caller(par, 0, 16)
            from_caller(par, 16, 32)
            pass_on("aa%d" % t, tnp, R(tdn, 512 * npar, 512 * npar + 512))
            act(R("MK"), R("ZN"), ACT.Relu, -1.0)
            db = [["D0", "D1"], ["TS", "PA"]]
            for h in range(2):
                part = R("SD", par + 512 * h, 512 * h + 512, 2)
                tt(part, R("PA", 256 * h, 256 * h + 256), part, ALU.max)
                for s in range(4):
                    spread(db[h][s // 2], 256 * (s % 2), s, part)
            tr(R("X1"), R("RN", a, a + 32))
            fill(swn, npar + 1024 * 3, R(kb[3]), "v")
            tt(R("TB", 0, 256), R("K0", 0, 256), R("MK", 0, 256), ALU.mult)
            for w0, w1 in ((0, 64), (64, 128)) if nxt == 0 else ((0, 128),):
                c = w0 ^ 64 * (nxt == 0)
                cp(R("OFT", 0, 32, 1, c, c + w1 - w0), R("X1", 0, 32, 1, w0, w1))
            for h in range(2):
                for s in range(4):
                    fill(swn, par + 1024 * s + 512 * h, R(db[h][s // 2], 256 * (s % 2), 256 * (s % 2) + 256), "sv"[s // 2])
            tt(R("TB", 256, 512), R("K0", 256, 512), R("MK", 256, 512), ALU.mult)
            pass_on("ab%d" % t, [R("TB"), tpar], R(tdn, 512 * par, 512 * par + 512))
            pass_on("an%d" % t, R("OFT", 0, 32), R("OFT", 32 * t + 32, 32 * t + 64))
            for h in (npar, par):
                old_row(tdn, t + 1, h)
                window(tdn, h, "tw%s%d" % ("ab"[h], t + 1))
            continue

        table()
        tr(R("FY"), R("FF"))
        from_caller(npar, 0, 12)
        fixed_row()
        from_caller(npar, 12, 32)
        mm(R("K0"), R("IDF", 0, 128), R("DD"), False, True)
        mm(R("TS"), R("IDB"), R("G", 0, 512), True, True)
        connected()
        from_caller(par, 0, 32)
        act(R("MK"), R("ZN"), ACT.Relu, -1.0)
        act(R("OT", npar, 1024, 2), tnp, ACT.Copy)
        parts = (("S", "SD", 0, 1024, T.ysec), ("T0", "OT", 0, 512, T.ytel), ("T1", "OT", 512, 512, T.ytel))
        for nm, src, c, width, y in parts:
            if nm == "S":
                tt(own, R("PA"), own, ALU.max)
                for h in (0, 256):
                    tt(R("D%d" % (h // 256), 0, 256), R("K0", h, h + 256), R("MK", h, h + 256), ALU.mult)
            else:
                h = c // 2
                tt(R("OT", c + par, c + 512, 2), R("D%d" % (h // 256), 0, 256), R(td, 512 * par + h, 512 * par + h + 256), ALU.add)
            for k, (k0, k1) in enumerate(spans):
                dma(DR("o" + nm, k0, k1), R(src, c, c + width, 1, 16 * k0, 16 * k1), "o" + nm, "y" if nm == "S" else "ys"[k % 2])
        for nm, src, c, width, y in parts:
            exchange("ao" + nm, "o" + nm, "lo" + nm, x * (nm != "S"))
        for mine in (True, False):
            for nm, src, c, width, y in parts:
                for k, gg in enumerate(gg for gg in range(8) if (gg % n == rank) == mine):
                    p0 = 64 * (gg // n ^ x * (nm != "S")) + 16 * rank
                    a = R(src, c, c + width, 1, p0, p0 + 16) if mine else DR("lo" + nm, gg, gg + 1)
                    dma(("raw", y[16 * gg:16 * gg + 16, c:c + width]), a, "out", "ys"[k % 2])

    emit(ops, Q, T, g)


def emit(ops, Q, T, g):
    hist = {}
    for k, o in enumerate(ops):
        deps = set()
        for kind in ("r", "w"):
            for a in o[kind]:
                psum = SCRATCH[a[0]][0] == "psum"
                for j, kj, b in hist.get(a[0], []):
                    pe = ops[j]["e"]
                    if psum and pe == "p" and o["e"] == "p":
                        continue
                    if (kind == "w" or kj == "w" or (psum and pe != o["e"])) and _touch(a, b):
                        deps.add(j)
        for kind in ("r", "w"):
            for a in o[kind]:
                hist.setdefault(a[0], []).append((k, kind, a))
        o["d"] = deps if o["e"] != "x" else set()
        best = {}
        for j in o["d"]:
            if ops[j]["grp"] is None:
                best[ops[j]["e"]] = max(best.get(ops[j]["e"], -1), j)
        o["cd"] = best
        for j in best.values():
            ops[j]["sig"] = True
    count, total = {}, {}
    for o in ops:
        if o["grp"] is not None:
            total[o["grp"]] = total.get(o["grp"], 0) + o["n"]
        elif o.get("sig"):
            count[o["e"]] = count.get(o["e"], 0) + 1
            o["tok"] = count[o["e"]]
    seen = {}
    for o in ops:
        if o["e"] == "x":
            continue
        need = {}
        for j in o["d"]:
            if ops[j]["grp"] is not None:
                need[ops[j]["grp"]] = total[ops[j]["grp"]]
        for e in o["cd"]:
            need[ENGSEM[e]] = ops[o["cd"][e]]["tok"]
        for s in sorted(need):
            if seen.get((o["e"], s), 0) < need[s]:
                Q[o["e"]].wait_ge(T.sem[s], need[s])
                seen[(o["e"], s)] = need[s]
        ins = o["f"]()
        if ins is not None:
            if o["grp"] is not None:
                ins.then_inc(T.sem[o["grp"]], 16)
            elif o.get("sig"):
                ins.then_inc(T.sem[ENGSEM[o["e"]]], 1)
    for e in count:
        g.wait_ge(T.sem[ENGSEM[e]], count[e])
    for s in total:
        g.wait_ge(T.sem[s], total[s])
